import numpy as np, ml_dtypes
CORES = [1,5,17,21,33,37,49,53]
N = 8
BF = ml_dtypes.bfloat16
R, D, CAP, MEETS = 4, 5, 64, (1, 6)
L = R * 4 ** D; P = (4 * L - R) // 3; I = P - L
OFF = [(R * 4 ** t - R) // 3 for t in range(D + 2)]
NODE = np.arange(P)
def rebuild(v):
    for t in range(D - 1, -1, -1):
        k = v[..., OFF[t + 1]:OFF[t + 2]]
        v[..., OFF[t]:OFF[t + 1]] = (k[..., 0::4] + 3 * k[..., 1::4] + 5 * k[..., 2::4] + 7 * k[..., 3::4]) & 255
    return v
def places(kids):
    c = kids.reshape(N, 8, 4, P); pl = np.zeros((N, 8, P), np.int64); pl[..., :R] = np.arange(R)
    for t in range(D):
        k = np.take_along_axis(c, pl[:, :, None, OFF[t]:OFF[t + 1]], 3)
        pl[..., OFF[t + 1]:OFF[t + 2]] = k.transpose(0, 1, 3, 2).reshape(N, 8, -1)
    return pl
def logical(dg, pl):
    return np.take_along_axis(dg.astype(np.float32).astype(np.int32).reshape(N, 8, 16, P), pl[:, :, None], 3)
def opened(v, m):
    o = np.any(v != v[np.arange(N) ^ m], axis=2)
    for t in range(D):
        o[..., OFF[t + 1]:OFF[t + 2]] &= np.repeat(o[..., OFF[t]:OFF[t + 1]], 4, axis=-1)
    return o
def meet(v, m):
    o = opened(v, m); u = v[np.arange(N) ^ m]; w = v.copy()
    up = o[..., I:] & (u[:, :, 15, I:] > v[:, :, 15, I:])
    w[..., I:] = np.where(up[:, :, None], u[..., I:], v[..., I:])
    return rebuild(w)
def put(rng, v):
    pl = np.concatenate([np.broadcast_to(np.arange(R), (N, 8, R)), R + np.argsort(rng.random((N, 8, P - R)), axis=-1)], axis=-1)
    k = np.zeros((N, 8, 4, P), np.int32); np.put_along_axis(k, pl[:, :, None, :I], pl[..., R:].reshape(N, 8, I, 4).transpose(0, 1, 3, 2).astype(np.int32), 3)
    e = np.zeros((N, 8, 16, P), np.float32); np.put_along_axis(e, pl[:, :, None], v.astype(np.float32), 3)
    return {"dg": e.reshape(N, 128, P).astype(BF), "kids": k.reshape(N, 32, P)}
def whole(rng, *shape):
    return rng.integers(0, 256, shape, dtype=np.int32)
def pool(rng):
    par = np.argsort(rng.random((8, L // 4)), axis=1)[:, :CAP // 8]; m = np.zeros((8, L // 4, 4), bool); np.put_along_axis(m, par[:, :, None], True, 1)
    m = m.reshape(8, L); np.put_along_axis(m, np.argsort(rng.random((8, L)), axis=1)[:, :CAP // 2 - 2], True, 1); m[:, 0] = True; m[:, -1] = True
    return m, par
def change(rng, base, m, x):
    mod = m & (rng.random((N, 8, L)) < 0.6); one = rng.random((N, 8, 1, L)) < 0.3
    c = mod[:, :, None] & (~one | (np.arange(16)[:, None] == rng.integers(0, 16, (N, 8, 1, L))))
    c[:, :, 15] &= rng.random((N, 8, L)) >= 0.25
    return np.ascontiguousarray(np.where(c, x, base))
def collide(rng, base, x, par):
    k = np.take_along_axis(base.reshape(8, 16, L // 4, 4), par[:, None, :, None], 2); k = np.repeat(k[None], N, axis=0)
    e = rng.integers(1, 256, k.shape[:-1], dtype=np.int32); k[..., 0] = (k[..., 0] - 3 * e) & 255; k[..., 1] = (k[..., 1] + e) & 255
    w = x.reshape(N, 8, 16, L // 4, 4).copy(); np.put_along_axis(w, par[None, :, None, :, None], k, 3); return w.reshape(N, 8, 16, L)
def grow(rng, base, x, m, hide, own):
    v = np.zeros((N, 8, 16, P), np.int32); v[..., I:] = x; rebuild(v); b = np.zeros((8, 16, P), np.int32); b[..., I:] = base; rebuild(b)
    cl = np.zeros((8, P), bool); cl[:, I:] = m
    for t in range(D - 1, -1, -1):
        cl[:, OFF[t]:OFF[t + 1]] = np.any(cl[:, OFF[t + 1]:OFF[t + 2]].reshape(8, -1, 4), axis=2)
    h = cl & (rng.random((8, P)) < hide) & (NODE < I); v = np.where(h[:, None], b, v)
    o = cl & (rng.random((N, 8, P)) < own) & (NODE < I); v = np.where(o[:, :, None], whole(rng, N, 8, 16, P), v)
    s = ~cl & (rng.random((8, P)) < 0.02) & (NODE < I)
    return np.where(s[:, None], whole(rng, 8, 16, P), v)
def balance(rng, v, m):
    a = np.arange(16)[:, None]; low = (np.arange(N) < (np.arange(N) ^ MEETS[0]))[:, None, None, None]
    for t in range(D):
        n = R * 4 ** t; k = np.any(m.reshape(8, n, -1), axis=2)
        e = rng.integers(1, 32, (N, 8, 1, n)) * rng.choice(np.array([-1, 1]), (N, 8, 1, n))
        if t % 2 == 0:
            s = rng.integers(0, 16, (N, 8, 1, n)); c = 1 * (a == s) - 1 * (a == ((s + rng.integers(1, 16, (N, 8, 1, n))) & 15))
        else:
            s = rng.integers(0, 14, (N, 8, 1, n)); c = 1 * (a == s) - 2 * (a == s + 1) + 1 * (a == s + 2)
        z = rng.integers(64, 192, (8, 16, n)) + low * e * c
        v[..., OFF[t]:OFF[t + 1]] = np.where(k[:, None], z, v[..., OFF[t]:OFF[t + 1]])
    return v
def setup_inputs(rng):
    base = whole(rng, 8, 16, L); m, par = pool(rng); x = change(rng, base, m, whole(rng, N, 8, 16, L)); x = collide(rng, base, x, par[:, :CAP // 32])
    return put(rng, grow(rng, base, x, m, 0.1 * (NODE >= OFF[D - 1]), 0.05))
def setup_inputs_full(rng):
    base = whole(rng, 8, 16, L); m = np.zeros((8, L), bool); t = [t for t in range(D + 1) if R * 4 ** t >= CAP][0]; w = 4 ** (D - t)
    for i, g in enumerate(rng.permutation(8)):
        if i % 4 == 1: l = (4 * rng.permutation(L // 4)[:CAP // 4, None] + np.arange(4)).reshape(-1)
        elif i % 4 == 3: l = np.arange(L - CAP, L)
        else: l = rng.permutation(R * 4 ** t)[:CAP] * w + rng.integers(0, w, CAP)
        m[g, l] = True
    z = whole(rng, N, 8, 16, L)
    for s in (0, 15): z[:, :, s] = (z[0, :, s].copy() + 31 * np.arange(N)[:, None, None]) & 255
    v = grow(rng, base, np.where(m[:, None], z, base), m, 0.0, 0.0)
    return put(rng, balance(rng, v, m & (rng.random((8, L)) < 0.5)))
def setup_inputs_ties(rng):
    base = whole(rng, 8, 16, L); base[:, 15] = rng.choice(np.array([0, 1, 254, 255]), (8, L)); m, par = pool(rng)
    x = change(rng, base, m, whole(rng, N, 8, 16, L)); c = np.any(x != base, axis=2)
    x[:, :, 15] = np.where(c, np.clip(base[:, 15] + rng.choice(np.array([-1, 0, 0, 1]), (N, 8, L)), 0, 255), base[:, 15])
    return put(rng, grow(rng, base, x, m, 0.0, 0.05))
def setup_inputs_hidden(rng):
    base = whole(rng, 8, 16, L); m, par = pool(rng); x = change(rng, base, m, whole(rng, N, 8, 16, L)); x = collide(rng, base, x, par)
    return put(rng, grow(rng, base, x, m, 0.15, 0.3))
def setup_inputs_calm(rng):
    base = whole(rng, 8, 16, L); m, par = pool(rng); p = rng.permutation(8); a = int(rng.integers(0, N)); m[p[:5]] = False; m[p[3], 0] = True; m[p[4], -1] = True
    x = change(rng, base, m, whole(rng, N, 8, 16, L))
    for g, l in ((p[3], 0), (p[4], L - 1)):
        x[:, g, :, l] = base[g, :, l]; x[a ^ MEETS[1], g, :, l] = (base[g, :, l] + rng.integers(1, 256, 16)) & 255
    v = grow(rng, base, x, m, 0.0, 0.0); v[a ^ MEETS[0]] = v[a]; return put(rng, v)
def setup_inputs_spread(rng):
    def uneven(*shape):
        u = rng.random(shape, dtype=np.float32); u = u * u * u; u = np.minimum(256 * u * u, 255).astype(np.int32)
        return np.where(rng.random(shape, dtype=np.float32) < 0.1, np.int32(255), u)
    base = uneven(8, 16, L) * (rng.random((8, 1, L)) > 0.0625).astype(np.int32); m, par = pool(rng)
    x = change(rng, base, m, uneven(N, 8, 16, L)); x = collide(rng, base, x, par[:, :CAP // 32])
    return put(rng, grow(rng, base, x, m, 0.1 * (NODE >= OFF[D - 1]), 0.05))
def check_inputs(d):
    bad = []; v = d["dg"].astype(np.float32); k = d["kids"].astype(np.int64)
    if not (np.isfinite(v).all() and (v == np.floor(v)).all() and v.min() >= 0 and v.max() <= 255): bad.append("symbols")
    if k.min() < 0 or k.max() >= P: return bad + ["children"]
    pl = places(k)
    if (np.sort(pl, axis=-1) != NODE).any(): bad.append("places")
    elif np.take_along_axis(k.reshape(N, 8, 4, P), pl[:, :, None, I:], 3).any(): bad.append("leaves")
    if bad: return bad
    v = logical(d["dg"], pl)
    for m in MEETS:
        o = opened(v, m)
        if max(int(np.count_nonzero(o[..., OFF[t]:OFF[t + 1]], axis=-1).max()) for t in range(D + 1)) > CAP: return ["open nodes"]
        v = meet(v, m)
    return []
def reference(dg, kids):
    pl = places(kids); v = logical(dg, pl)
    for m in MEETS:
        v = meet(v, m)
    y = np.zeros((N, 8, 16, P), np.float32); np.put_along_axis(y, pl[:, :, None], v.astype(np.float32), 3)
    return {"y": y.reshape(N, 128, P).astype(BF)}

@@ -1,0 +1,584 @@
+from concourse.mybir import AluOpType as ALU, ActivationFunctionType as ACT
+
+P = 5460
+DUM = 5464
+DW = 6496
+MEETS = (1, 6)
+BIG = 3221225472.0
+WK = (1, 3, 5, 7)
+PR = (1, 3, 5, 7, 9, 15, 21, 25, 35, 49)
+SC = PR + (-256,) + tuple(-w for w in PR)
+LA, LB = 3456, 3840
+SPLIT = 4096
+WV = (1792, 3712)
+WG = (4600, P)
+
+
+def _sb(n, t):
+    return ("sbuf", [128, n], t)
+
+
+_BF = dict(D=DW, Z=144, Z4=144, ZQ=144, B=128, U=128, UT=128, V=128, IDM=128 * len(SC), MO=1408, MI=1408, RT=16,
+           NE0=16, NE=1536, FB=80, OWN=64, NEP=64, LV=4352, L4=1088, L4S=1024, L4P=1088, T4=1024, T3=256, F5=352,
+           RS5=320, RS68=272, C127=512, CK=128, LE4=272, S16=272, LE=64, NEW0=256, NEW1=256, A0=256, A1=256, B0=256,
+           B1=256, GT=256, DF=256, MD0=256, MD1=256, PA0=64, PAP=64, UF=416)
+_F32 = dict(COL=16, ZR=144, Z1=144, M1=128, G=352, G4=1088, RSZ=128, ONE=72, KA=32, WP=192, THR=8, XF=64, C=72, CW=72,
+            S4=16, X0=64, X1=64, MM=192, MU=512, M4=64, ZS=128, SCN=128, XG=32)
+_I32 = dict(W=P, N0=256, N4=144, N16=128, CI32=8)
+_U16 = dict(OFF=96, LP=256, OC=16, CI=16, IDS0=16, IDS1=16, IDP=16, CP0=16, CP1=16, CL0=16, CL1=16, PL0=16)
+SCRATCH = {}
+for _d, _t in ((_BF, "bfloat16"), (_F32, "float32"), (_I32, "int32"), (_U16, "uint16")):
+    for _k in _d:
+        SCRATCH[_k] = _sb(_d[_k], _t)
+for _i in range(8):
+    SCRATCH["P%d" % _i] = ("psum", [128, 512], "float32")
+NPOOL = 100
+SEMAPHORES = (["s%d" % i for i in range(NPOOL)] + ["d%d" % i for i in range(10)]
+              + ["l%d" % i for i in range(12)] + ["r%d" % i for i in range(12)])
+
+
+def build(core, T, topo):
+    rank = T.rank_of(core)
+    peer = [T.cores[rank ^ m] for m in MEETS]
+    ops = []
+
+    def A(name, lo, hi, step=1):
+        ap = T[name][:, lo:hi] if step == 1 else T[name][:, lo:hi:step]
+        return (ap, [(name, lo, hi)], [])
+
+    def IND(win, off):
+        return (win[0].indirect(off[0]), win[1], off[1])
+
+    def only(a, tag):
+        return (a[0], [(a[1][0][0] + "_%d" % tag, 0, 1)], a[2])
+
+    def also(a, regions):
+        return (a[0], a[1], a[2] + regions)
+
+    def col(j):
+        return A("COL", j, j + 1)
+
+    def add(q, fn, outs, ins, kind="c", **kw):
+        w = [r for o in outs for r in o[1]]
+        rd = [r for o in ins for r in o[1]] + [r for o in list(outs) + list(ins) for r in o[2]]
+        ops.append(dict(q=q, fn=fn, w=w, r=rd, kind=kind, **kw))
+        return len(ops) - 1
+
+    def val(s):
+        return s[0] if isinstance(s, tuple) else s
+
+    def aps(*s):
+        return [x for x in s if isinstance(x, tuple)]
+
+    def copy(o, i):
+        return add("vector", lambda e: e.tensor_copy(o[0], i[0]), [o], [i])
+
+    def tt(o, a, b, op):
+        return add("vector", lambda e: e.tensor_tensor(o[0], a[0], b[0], op), [o], [a, b])
+
+    def ts(o, a, s1, s2, op0, op1=None):
+        if op1 is None:
+            fn = lambda e: e.tensor_scalar(o[0], a[0], val(s1), None, op0)
+        else:
+            fn = lambda e: e.tensor_scalar(o[0], a[0], val(s1), val(s2), op0, op1)
+        return add("vector", fn, [o], [a] + aps(s1, s2))
+
+    def scan(o, d0, d1, op0, op1):
+        return add("vector", lambda e: e.tensor_tensor_scan(o[0], d0[0], d1[0], 0.0, op0, op1), [o], [d0, d1])
+
+    def fill(o, c):
+        return add("vector", lambda e: e.memset(o[0], c), [o], [])
+
+    def act(o, i, scale=1.0, bias=0.0):
+        return add("scalar", lambda e: e.activation(o[0], i[0], ACT.Identity, bias=bias, scale=scale), [o], [i])
+
+    def afill(o, n, c):
+        return act(o, A("IDM", 0, n), scale=0.0, bias=c)
+
+    def iota(o, pat, base, cm, fl=False):
+        if fl:
+            fn = lambda e: e.iota(o[0], pat, base, cm, allow_small_or_imprecise_dtypes=True)
+        else:
+            fn = lambda e: e.iota(o[0], pat, base, cm)
+        return add("g", fn, [o], [])
+
+    def mm(o, terms, start=True, stop=True, after=None):
+        def fn(e):
+            last = None
+            for n, (l, r) in enumerate(terms):
+                last = e.matmul(o[0], l[0], r[0], start and n == 0, stop and n == len(terms) - 1)
+            return last
+        return add("tensor", fn, [o], [x for t in terms for x in t], after=after)
+
+    ndma = [0]
+
+    def dma(o, i, outs, ins, q="sync"):
+        ndma[0] += 1
+        return add(q, lambda e: e.dma_start(o, i), outs, ins, kind="dma", sem="d%d" % (ndma[0] - 1), n=16)
+
+    nmsg = [0]
+
+    def send(m, dst, src):
+        k = nmsg[0]
+        nmsg[0] += 1
+        rid, pid = topo.addr(peer[m])[:2]
+        mask = topo.mask(core, peer[m])
+        n = len(topo.engines(core, peer[m]))
+        add("g", lambda e: e.remote_dma(dst[0], src[0], T.sem["r%d" % k], T.sem["l%d" % k], pid, rid, mask),
+            [], [src], kind="send", sem="l%d" % k, n=n)
+        add(None, None, [dst], [], kind="arr", sem="r%d" % k, n=len(topo.engines(peer[m], core)))
+
+    def ident(w):
+        j = SC.index(w)
+        return A("IDM", 128 * j, 128 * j + 128)
+
+    def R(q):
+        return A("ZR", 12 - 4 * q, 140 - 4 * q)
+
+    def E(p, name="Z"):
+        return A(name, 15 - p, 143 - p)
+
+    def rnd(o, i):
+        ts(o, i, BIG, BIG, ALU.add, ALU.subtract)
+
+    DWIN = A("D", 0, DW)
+    WWIN = A("W", 0, P)
+    LWIN = A("LV", 0, 4352)
+    PA = (A("PA0", 0, 64), A("UF", 352, 416))
+    PL = (A("PL0", 0, 4), A("OFF", 90, 94))
+
+    def kids(lo, hi):
+        dma(T["W"][0:128:4, lo:hi], T["kids"][:, lo:hi], [A("W", lo, hi)], [])
+
+    dma(T["D"][:, 0:512], T["dg"][:, 0:512], [A("D", 0, 512)], [])
+    dma(T["D"][:, 512:SPLIT], T["dg"][:, 512:SPLIT], [A("D", 512, SPLIT)], [])
+    iota(A("N0", 0, 256), [[1, 256]], 0, 0)
+    iota(A("CI32", 0, 1), [[0, 1]], 0, 1)
+    iota(A("W", WV[1], WG[0]), [[1, WG[0] - WV[1]]], WV[1], 0)
+    iota(A("W", WG[0], P), [[1, P - WG[0]]], WG[0], 0)
+    fill(A("D", 5456, DW), 0.0)
+    for c in range(0, WV[1], 256):
+        n = min(256, WV[1] - c)
+        ts(A("W", c, c + n), A("N0", 0, n), float(c), None, ALU.add)
+        if c + n == WV[0]:
+            kids(0, WV[0])
+            kids(WV[1], WG[0])
+    kids(WV[0], WV[1])
+    kids(WG[0], P)
+    dma(T["D"][:, SPLIT:P], T["dg"][:, SPLIT:P], [A("D", SPLIT, 5464)], [])
+    send(0, A("RT", 0, 4), A("D", 0, 4))
+    ts(A("CI32", 1, 2), A("CI32", 0, 1), 15, None, ALU.bitwise_and)
+    ts(A("CI32", 2, 3), A("CI32", 0, 1), 12, None, ALU.bitwise_and)
+    copy(A("COL", 1, 2), A("CI32", 0, 1))
+    ts(A("N4", 0, 144), A("N0", 0, 144), 508, None, ALU.bitwise_and)
+    copy(A("COL", 0, 1), A("CI32", 1, 2))
+    ts(A("COL", 7, 8), A("CI32", 2, 3), 3.0, None, ALU.add)
+    ts(ident(1), A("N0", 0, 128), col(1), None, ALU.is_equal)
+    tt(A("COL", 2, 3), col(1), col(0), ALU.subtract)
+    ts(A("N16", 0, 128), A("N0", 0, 128), 496, None, ALU.bitwise_and)
+    ts(A("COL", 3, 4), col(0), 0.25, col(2), ALU.mult, ALU.add)
+    ts(A("M1", 0, 128), A("N4", 0, 128), col(1), None, ALU.is_equal)
+    ts(A("ZR", 0, 144), A("N0", 0, 144), -12.0, col(3), ALU.add, ALU.is_equal)
+    ts(A("Z", 0, 144), A("N0", 0, 144), -15.0, col(2), ALU.add, ALU.is_equal)
+    ts(A("Z4", 0, 144), A("N4", 0, 144), -12.0, col(2), ALU.add, ALU.is_equal)
+    ts(A("B", 0, 128), A("N16", 0, 128), col(2), None, ALU.is_equal)
+    copy(A("G", 0, 4), A("W", 0, 4))
+    mm(A("P0", 0, 1), [(R(q), A("G", q, q + 1)) for q in range(4)])
+    mm(A("P0", 4, 8), [(A("M1", 0, 128), A("G", 0, 4))])
+    for w in SC[1:11]:
+        act(ident(w), ident(1), scale=float(w))
+    afill(A("CK", 0, 64), 64, 0.5)
+    afill(A("CK", 64, 128), 64, -127.5)
+    afill(A("C127", 0, 512), 512, 127.5)
+    afill(A("KA", 0, 16), 16, 120.5)
+    afill(A("KA", 16, 32), 16, 0.5)
+    afill(A("LV", 4096, 4352), 256, 0.0)
+    afill(A("RSZ", 0, 128), 128, 1.0)
+    ts(A("UT", 0, 128), A("N0", 0, 128), col(1), None, ALU.is_lt)
+    ts(A("COL", 4, 5), col(0), 1.0, None, ALU.is_equal)
+    ts(A("COL", 5, 6), col(0), 15.0, None, ALU.is_equal)
+    ts(A("COL", 6, 7), col(0), float(DUM), None, ALU.add)
+    ts(A("COL", 8, 9), col(0), 3.0, 16.0, ALU.min, ALU.mult)
+    ts(A("COL", 9, 10), col(0), 15.0, float(DUM + 2), ALU.mult, ALU.add)
+    copy(A("OC", 10, 14), A("N0", 0, 4))
+    fill(A("F5", 320, 340), 1.0)
+    fill(A("RS5", 0, 320), 0.0)
+    fill(A("RS68", 0, 272), 1.0)
+    copy(A("OFF", 88, 89), A("P0", 0, 1))
+    copy(A("OFF", 64, 68), A("P0", 4, 8))
+    iota(A("WP", 0, 64), [[0, 16], [2, 4]], 1, 0, True)
+    iota(A("WP", 128, 192), [[0, 4], [2, 4], [0, 4]], 1, 0, True)
+
+    def late(part):
+        if part == 0:
+            tt(A("U", 0, 128), A("UT", 0, 128), A("B", 0, 128), ALU.mult)
+            ts(A("V", 0, 128), A("B", 0, 128), col(5), None, ALU.mult)
+            ts(A("G4", 1024, 1088), A("N0", 0, 64), 16.0, col(6), ALU.mult, ALU.add)
+            ts(A("THR", 0, 4), A("N0", 0, 4), 16.0, col(0), ALU.mult, ALU.add)
+            copy(A("XF", 0, 64), A("N0", 0, 64))
+            fill(A("RS5", 0, 320, 5), 1.0)
+            fill(A("RS68", 0, 272, 68), 0.0)
+        elif part == 1:
+            fill(A("ONE", 0, 68), 1.0)
+            ts(A("Z1", 0, 144), A("Z", 0, 144), col(4), None, ALU.mult)
+            ts(A("OC", 0, 4), A("N0", 0, 4), 16.0, 79.0, ALU.mult, ALU.add)
+            ts(A("OC", 4, 8), A("N0", 0, 4), 16.0, col(7), ALU.mult, ALU.add)
+            ts(A("OC", 8, 9), col(0), 4.0, 3.0, ALU.mult, ALU.add)
+            ts(A("COL", 10, 11), col(0), 4.0, col(9), ALU.is_ge, ALU.mult)
+            ts(A("ZQ", 0, 144), A("Z", 0, 144), 4.0, None, ALU.mult)
+            fill(A("FB", 64, 68), 1.0)
+        else:
+            fill(A("NE", 1024, 1088), 0.0)
+            fill(A("L4", 1024, 1088), 0.0)
+            fill(A("L4P", 1024, 1088), 0.0)
+            ts(A("OC", 9, 10), col(8), 79.0, None, ALU.add)
+            ts(A("OFF", 89, 90), col(10), col(0), None, ALU.add)
+            fill(A("RSZ", 0, 64, 4), 0.0)
+            fill(A("RSZ", 64, 128, 16), 0.0)
+            tt(A("WP", 64, 128), A("WP", 0, 64), A("WP", 128, 192), ALU.mult)
+
+    for part, (go, n, src, dst) in enumerate(((16, 16, 88, 84), (32, 64, 84, 68), (96, 256, 68, 0))):
+        copy(A("G", go, go + n), IND(WWIN, A("OFF", src, src + n // 16)))
+        mm(A("P0", 0, n // 4), [(R(q), A("G", go + q, go + n, 4)) for q in range(4)])
+        if n == 256:
+            act(A("MO", 1024, 1408), IND(DWIN, A("OFF", 64, 88)))
+            send(0, A("MI", 1024, 1408), A("MO", 1024, 1408))
+        late(part)
+        copy(A("OFF", dst, dst + n // 4), A("P0", 0, n // 4))
+    for h in range(2):
+        act(A("MO", 512 * h, 512 * h + 256), IND(DWIN, A("OFF", 32 * h, 32 * h + 16)))
+        copy(A("MO", 512 * h + 256, 512 * h + 512), IND(DWIN, A("OFF", 32 * h + 16, 32 * h + 32)))
+        send(0, A("MI", 512 * h, 512 * h + 512), A("MO", 512 * h, 512 * h + 512))
+    QB = ("P0", "P5", "P6", "P7")
+
+    def quarter(h):
+        copy(A("G4", 256 * h, 256 * h + 256), IND(WWIN, A("OFF", 16 * h, 16 * h + 16)))
+        mm(A(QB[h], 0, 64), [(R(q), A("G4", 256 * h + q, 256 * h + 256, 4)) for q in range(4)])
+
+    def quarter_out(h):
+        copy(A("LP", 64 * h, 64 * h + 64), A(QB[h], 0, 64))
+        if h < 3:
+            act(A("LV", 1024 * h, 1024 * h + 1024), IND(DWIN, A("LP", 64 * h, 64 * h + 64)))
+
+    quarter(0)
+    quarter(1)
+    tt(A("NE0", 0, 4), A("D", 0, 4), A("RT", 0, 4), ALU.not_equal)
+    quarter_out(0)
+    quarter(2)
+    quarter_out(1)
+    quarter(3)
+    copy(A("NE", 1472, 1536), IND(A("NE0", 0, 4), A("OC", 10, 14)))
+    tt(A("NE", 1088, 1472), A("MO", 1024, 1408), A("MI", 1024, 1408), ALU.not_equal)
+    quarter_out(2)
+    quarter_out(3)
+
+    def leaves(lo, hi):
+        copy(A("LV", lo, hi), IND(DWIN, A("LP", lo // 16, hi // 16)))
+
+    SHUT = (A("P1", 0, 256), A("P1", 256, 512), A("P2", 0, 256), A("P7", 0, 256))
+    OPEN = (A("P6", 0, 256), A("P0", 0, 256), A("P5", 0, 256), A("P1", 0, 256))
+    bs = [None] * 4
+
+    def bulk_sum(h, shut=True, opened=True):
+        terms = [(ident(WK[k]), A("LV", 1024 * h + k, 1024 * h + 1024, 4)) for k in range(4)]
+        if shut:
+            mm(SHUT[h], terms)
+        if opened:
+            bs[h] = mm(OPEN[h], terms, stop=False)
+
+    def bulk_q(h, src):
+        act(A("T4", 256 * h, 256 * h + src[1][0][2]), src, scale=1.0 / 256, bias=128.501953125)
+
+    def bulk_fix(h):
+        mm(OPEN[h], [(ident(-256), A("T4", 256 * h, 256 * h + 256))], start=False, after=bs[h])
+        act(A("L4S", 256 * h, 256 * h + 256), OPEN[h], bias=129.0 * 256 - 127.5)
+
+    def count4():
+        mm(A("P3", 0, 320, 5), [(E(p), A("NE", p, 1024, 16)) for p in range(16)])
+
+    def count4_half(h):
+        mm(A("P3", 384 + 32 * h, 416 + 32 * h), [(E(p), A("NE", 512 * h + p, 512 * h + 512, 16)) for p in range(16)])
+
+    def count3(l3):
+        mm(A("P3", 1, 320, 5), [(A("Z4", 12 - 4 * k, 140 - 4 * k), A("NE", l3 + k, l3 + 256, 4)) for k in range(4)])
+
+    def count_up(t, lo):
+        mm(A("P3", t, 320, 5), [(A("B", 0, 128), A("NE", lo, lo + 64))])
+
+    def candidates(m, f, hook):
+        a, b = "A%d" % m, "B%d" % m
+        mm(A("P4", 0, 68), [(A("B", 0, 128), f)])
+        mm(A("P4", 68, 136), [(A("U", 0, 128), f)])
+        hook(0)
+        scan(A("C", 0, 68), A("ONE", 0, 68), A("P4", 0, 68), ALU.mult, ALU.add)
+        for q in range(4):
+            ts(A("LE4", 68 * q, 68 * q + 68), A("C", 0, 68), A("THR", q, q + 1), 16.0, ALU.is_le, ALU.mult)
+        tt(A("CW", 0, 68), A("C", 0, 68), A("P4", 68, 136), ALU.subtract)
+        scan(A("S16", 0, 272), A("RS68", 0, 272), A("LE4", 0, 272), ALU.mult, ALU.add)
+        ts(A("CI", 0, 4), A("S16", 67, 272, 68), 1.0 / 16, None, ALU.mult)
+        tt(A("LE", 0, 64), IND(A("CW", 0, 68), A("CI", 0, 4)), A("XF", 0, 64), ALU.is_le)
+        mm(A("P4", 256, 260), [(E(p, "ZQ"), A("LE", p, 64, 16)) for p in range(16)])
+        for k in range(4):
+            ts(A("S4", 4 * k, 4 * k + 4), A("S16", 67, 272, 68), 4.0, float(k), ALU.mult, ALU.add)
+        hook(1)
+        cl = "CL%d" % m
+        for q in range(4):
+            ts(only(A(cl, q, 16, 4), q), A("S4", q, 16, 4), A("P4", 256 + q, 257 + q), None, ALU.add)
+        allcl = [(cl + "_%d" % q, 0, 1) for q in range(4)]
+        if m == 0:
+            copy(A(a, 0, 256), also(IND(LWIN, A(cl, 0, 16)), allcl))
+        else:
+            act(A(a, 0, 128), also(IND(LWIN, A(cl, 0, 8)), allcl))
+            copy(A(a, 128, 256), also(IND(LWIN, A(cl, 8, 16)), allcl))
+        send(m, A(b, 0, 256), A(a, 0, 256))
+        ts(A("IDS%d" % m, 0, 4), also(A(cl, 0, 4), allcl), 0.25, None, ALU.mult)
+
+    def places(m):
+        copy(A("X%d" % m, 0, 64), IND(A("G4", 0, 1088), A("IDS%d" % m, 0, 4)))
+
+    def places_kids(m):
+        mm(A("P2", 0, 16), [(R(q), A("X%d" % m, q, 64, 4)) for q in range(4)])
+
+    def places_own(m, lo, hi, after=None):
+        return mm(A("P1", 0, 4), [(E(p, "Z1"), A("X%d" % m, p, 64, 16)) for p in range(lo, hi)], lo == 0, hi == 16, after)
+
+    def places_out(m, which):
+        if which == 0:
+            copy(A("CP%d" % m, 0, 16), A("P2", 0, 16))
+        else:
+            copy(PL[m], A("P1", 0, 4))
+
+    def open4(m):
+        a = "A%d" % m
+        return mm(A("P6", 0, 64), [(ident(1), A("CK", 64, 128))]
+                  + [(ident(WK[k]), A(a, 64 * k, 64 * k + 64)) for k in range(4)], stop=False)
+
+    def settle(m, g4):
+        a, b, pa, md = A("A%d" % m, 0, 256), A("B%d" % m, 0, 256), PA[m], "MD%d" % m
+        tt(A("GT", 0, 256), b, a, ALU.is_gt)
+        mm(A("P5", 0, 256), [(A("V", 0, 128), A("GT", 0, 256))])
+        tt(A("DF", 0, 256), b, a, ALU.subtract)
+        tt(A(md, 0, 256), A("P5", 0, 256), A("DF", 0, 256), ALU.mult)
+        mm(A("P6", 0, 64), [(ident(WK[k]), A(md, 64 * k, 64 * k + 64)) for k in range(4)], start=False, after=g4)
+        for k in range(4):
+            tt(only(A("NEW%d" % m, k, 256, 4), k), A("A%d" % m, 64 * k, 64 * k + 64), A(md, 64 * k, 64 * k + 64), ALU.add)
+        rnd(A("M4", 0, 64), A("P6", 0, 64))
+        tt(pa, A("P6", 0, 64), A("M4", 0, 64), ALU.subtract)
+
+    l2, l3 = A("P0", 0, 64), A("P7", 0, 256)
+
+    def sum2(src, sign, start, stop, after=None):
+        return mm(l2, [(ident(sign * WK[j // 4] * WK[j % 4]), A(src, j, 1024, 16)) for j in range(16)], start, stop, after)
+
+    def sum3(src, sign, start, stop, after=None):
+        return mm(l3, [(ident(sign * WK[k]), A(src, k, 1024, 4)) for k in range(4)], start, stop, after)
+
+    def low_sums():
+        tt(A("ZS", 0, 64), l2, A("WP", 0, 64), ALU.mult)
+        tt(A("ZS", 64, 128), l2, A("WP", 64, 128), ALU.mult)
+        rnd(A("MM", 0, 64), l2)
+        scan(A("SCN", 0, 128), A("RSZ", 0, 128), A("ZS", 0, 128), ALU.mult, ALU.add)
+
+    def mod3():
+        o = A("P2", 0, 256)
+        act(A("T3", 0, 256), l3, scale=1.0 / 256, bias=2040 / 256.0 + 128.501953125)
+        first = mm(o, [(ident(WK[k]), A("L4", k, 1024, 4)) for k in range(4)], stop=False)
+        mm(o, [(ident(-256), A("T3", 0, 256))], start=False, after=first)
+        act(A("UF", 0, 256), o, bias=2040 + 129.0 * 256 - 127.5)
+
+    def own4(m):
+        copy(IND(A("L4", 0, 1088), A("IDS%d" % m, 0, 4)), PA[m])
+
+    def put_leaves(m):
+        copy(IND(DWIN, A("CP%d" % m, 0, 16)), also(A("NEW%d" % m, 0, 256), [("NEW%d_%d" % (m, k), 0, 1) for k in range(4)]))
+
+    def put_l4(lo, hi, src="L4"):
+        tt(IND(DWIN, A("OFF", lo // 16, hi // 16)), A(src, lo, hi), A("C127", 0, hi - lo), ALU.add)
+
+    count3(1152)
+    count_up(2, 1408)
+    count_up(3, 1088)
+    count_up(4, 1472)
+    count_up(0, 1472)
+    bulk_sum(0)
+    tt(A("NE", 0, 512), A("MO", 0, 512), A("MI", 0, 512), ALU.not_equal)
+    scan(A("F5", 0, 320), A("RS5", 0, 320), A("P3", 0, 320), ALU.max, ALU.min)
+    count4_half(0)
+    tt(A("NE", 512, 1024), A("MO", 512, 1024), A("MI", 512, 1024), ALU.not_equal)
+    count4_half(1)
+    leaves(3072, LA)
+    tt(A("FB", 0, 64), A("P3", 384, 448), A("F5", 4, 320, 5), ALU.min)
+
+    def hook0(i):
+        if i == 0:
+            bulk_sum(1)
+            act(A("LV", LB, 4096), IND(DWIN, A("LP", LB // 16, 256)))
+            bulk_q(0, A("P1", 0, 512))
+        else:
+            leaves(LA, LB)
+            bulk_sum(2, True, False)
+            bulk_fix(0)
+            bulk_fix(1)
+            bulk_q(2, SHUT[2])
+            bulk_sum(3, True, False)
+            bulk_q(3, SHUT[3])
+            bulk_sum(2, False, True)
+            bulk_fix(2)
+            bulk_sum(3, False, True)
+            bulk_fix(3)
+
+    candidates(0, A("FB", 0, 68), hook0)
+    act(A("L4", 0, 1024), A("L4S", 0, 1024))
+    send(1, A("L4P", 0, 512), A("L4S", 0, 512))
+    send(1, A("IDP", 0, 4), A("IDS0", 0, 4))
+    send(1, A("L4P", 512, 1024), A("L4S", 512, 1024))
+    for w in SC[11:]:
+        act(ident(w), ident(1), scale=float(w))
+    g4 = open4(0)
+    places(0)
+    put_l4(0, 512, "L4S")
+    settle(0, g4)
+    send(1, A("PAP", 0, 64), PA[0])
+    own4(0)
+    g2 = sum2("L4", 1, True, False)
+    g3 = sum3("L4", 1, True, False)
+    places_kids(0)
+    tt(IND(LWIN, A("CL0", 0, 16)), A("A0", 0, 256), A("MD0", 0, 256), ALU.add)
+    copy(A("OWN", 0, 64), IND(A("L4", 0, 1088), A("IDP", 0, 4)))
+    tt(A("NE", 0, 512), A("L4", 0, 512), A("L4P", 0, 512), ALU.not_equal)
+    tt(A("NE", 512, 1024), A("L4", 512, 1024), A("L4P", 512, 1024), ALU.not_equal)
+    copy(IND(A("L4P", 0, 1088), A("IDP", 0, 4)), A("PAP", 0, 64))
+    sum2("L4P", -1, False, True, g2)
+    sum3("L4P", -1, False, True, g3)
+    tt(A("NEP", 0, 64), A("OWN", 0, 64), A("PAP", 0, 64), ALU.not_equal)
+    copy(IND(A("NE", 0, 1088), A("IDP", 0, 4)), A("NEP", 0, 64))
+    count4()
+    act(A("MU", 0, 256), l3, bias=BIG)
+    act(A("MU", 256, 512), A("MU", 0, 256), bias=-BIG)
+    low_sums()
+    low = IND(A("SCN", 0, 128), A("OC", 0, 8))
+    tt(A("NE", 1472, 1536), l2, A("MM", 0, 64), ALU.not_equal)
+    count_up(2, 1472)
+    rnd(A("MM", 64, 192), low)
+    tt(A("NE", 1088, 1216), low, A("MM", 64, 192), ALU.not_equal)
+    count_up(3, 1152)
+    count_up(4, 1088)
+    places_out(0, 0)
+    tt(A("NE", 1216, 1472), l3, A("MU", 256, 512), ALU.not_equal)
+    count3(1216)
+    put_l4(512, 576)
+    scan(A("F5", 0, 320), A("RS5", 0, 320), A("P3", 0, 320), ALU.max, ALU.min)
+    po = [None]
+
+    def hook1(i):
+        if i == 0:
+            po[0] = places_own(0, 0, 8)
+        else:
+            put_l4(576, 704)
+            places_own(0, 8, 16, po[0])
+
+    candidates(1, A("F5", 4, 340, 5), hook1)
+    g4 = open4(1)
+    g2 = mm(l2, [(ident(1), A("CK", 0, 64))], stop=False)
+    places(1)
+    put_leaves(0)
+    places_out(0, 1)
+    places_kids(1)
+    places_own(1, 0, 16)
+    tt(IND(DWIN, PL[0]), PA[0], A("C127", 0, 64), ALU.add)
+    put_l4(704, 1024)
+    places_out(1, 0)
+    settle(1, g4)
+    own4(1)
+    sum3("L4", 1, True, True)
+    sum2("L4", 1, False, True, g2)
+    mod3()
+    put_leaves(1)
+    places_out(1, 1)
+    low_sums()
+    tt(A("UF", 256, 320), l2, A("MM", 0, 64), ALU.subtract)
+    tt(A("XG", 0, 32), IND(A("SCN", 0, 128), A("OC", 8, 10)), A("KA", 0, 32), ALU.add)
+    rnd(A("MM", 64, 96), A("XG", 0, 32))
+    tt(A("UF", 320, 352), A("XG", 0, 32), A("MM", 64, 96), ALU.subtract)
+    tt(IND(DWIN, A("OFF", 68, 94)), A("UF", 0, 416), A("C127", 0, 416), ALU.add)
+    dma(T["y"][:, 0:P], T["D"][:, 0:P], [], [A("D", 0, P)])
+    return ops
+
+
+def _meet(a, b):
+    return a[0] == b[0] and a[1] < b[2] and b[1] < a[2]
+
+
+def _depends(x, y):
+    for a in x["w"] + x["r"]:
+        if a[0][0] == "P" and a[0][1:].isdigit():
+            if x["q"] != y["q"] and any(b[0] == a[0] for b in y["w"] + y["r"]):
+                return True
+    if x["q"] == "tensor" and y["q"] == "tensor":
+        return False
+    return (any(_meet(a, b) for a in x["r"] + x["w"] for b in y["w"])
+            or any(_meet(a, b) for a in x["w"] for b in y["r"]))
+
+
+def rank_program(g, core, T, topo):
+    if T.rank_of(core) is None:
+        return
+    ops = build(core, T, topo)
+    eng = {"g": g, "vector": g.vector, "scalar": g.scalar, "tensor": g.tensor, "sync": g.sync}
+    known = {q: set() for q in eng}
+    before = []
+    waits = []
+    for i, x in enumerate(ops):
+        if x["kind"] == "arr":
+            before.append(set())
+            waits.append([])
+            continue
+        k = known[x["q"]]
+        need = [j for j in range(i) if j not in k and _depends(x, ops[j])]
+        implied = set()
+        for j in need:
+            implied |= before[j]
+            if ops[j].get("after") is not None:
+                implied.add(ops[j]["after"])
+        need = [j for j in need if j not in implied]
+        k |= implied | set(need)
+        waits.append(need)
+        before.append(set(k))
+    waited = set(j for w in waits for j in w)
+    tail = [i for i, x in enumerate(ops) if x["kind"] != "c" and i not in waited]
+    waiters = {}
+    for i, w in enumerate(waits):
+        for j in w:
+            waiters.setdefault(j, []).append(i)
+    groups = []
+    for j in sorted(waiters):
+        if ops[j]["kind"] != "c":
+            continue
+        for grp in groups:
+            if (waiters[grp[0]][0] == waiters[j][0] and all(j in before[y] for i in grp for y in waiters[i])
+                    and all(i in before[y] for i in grp for y in waiters[j])):
+                grp.append(j)
+                break
+        else:
+            groups.append([j])
+    pool = [[[], 0] for _ in range(NPOOL)]
+    for grp in groups:
+        s = [n for n in range(NPOOL) if all(j in before[i] for j in pool[n][0] for i in grp)][0]
+        pool[s] = [grp, pool[s][1] + len(grp)]
+        for i in grp:
+            ops[i]["sem"], ops[i]["n"] = "s%d" % s, pool[s][1]
+    done = {q: set() for q in eng}
+    for i, x in enumerate(ops):
+        if x["kind"] == "arr":
+            continue
+        e = eng[x["q"]]
+        for s, n in sorted(set((ops[j]["sem"], ops[j]["n"]) for j in waits[i]) - done[x["q"]]):
+            e.wait_ge(T.sem[s], n)
+            done[x["q"]].add((s, n))
+        r = x["fn"](e)
+        if x["kind"] == "dma":
+            r.then_inc(T.sem[x["sem"]], 16)
+        elif x["kind"] == "c" and i in waited:
+            r.then_inc(T.sem[x["sem"]], 1)
+    for i in tail:
+        eng[ops[i]["q"] or "g"].wait_ge(T.sem[ops[i]["sem"]], ops[i]["n"])

@@ -5,63 +5,74 @@ DUM = 5464
 DW = 6496
 MEETS = (1, 6)
 BIG = 3221225472.0
+MID = 49152.0
 WK = (1, 3, 5, 7)
 PR = (1, 3, 5, 7, 9, 15, 21, 25, 35, 49)
-SC = PR + (-256,) + tuple(-w for w in PR)
-LA, LB = 3456, 3840
-SPLIT = 4096
-WV = (1792, 3712)
-WG = (4600, P)
+SC = PR + tuple(-w for w in PR)
+SPLIT = 2816
+WR = 1664
+WV = (3104, 4256)
+WG = (4864, P)
+LEAVES = ((3072, 3328, "V"), (3328, 3584, "V"), (0, 1024, "S"), (0, 1024, "send"), (1024, 2048, "S"),
+          (1024, 2048, "send"), (2048, 3072, "S"), (2048, 3072, "send"), (3584, 3840, ""), (3840, 4096, ""),
+          (3072, 4096, "send"))
+EARLY = 1
+PUT = 128
+ALL1 = False
 
 
 def _sb(n, t):
     return ("sbuf", [128, n], t)
 
 
-_BF = dict(D=DW, Z=144, Z4=144, ZQ=144, B=128, U=128, UT=128, V=128, IDM=128 * len(SC), MO=1408, MI=1408, RT=16,
-           NE0=16, NE=1536, FB=80, OWN=64, NEP=64, LV=4352, L4=1088, L4S=1024, L4P=1088, T4=1024, T3=256, F5=352,
-           RS5=320, RS68=272, C127=512, CK=128, LE4=272, S16=272, LE=64, NEW0=256, NEW1=256, A0=256, A1=256, B0=256,
-           B1=256, GT=256, DF=256, MD0=256, MD1=256, PA0=64, PAP=64, UF=416)
-_F32 = dict(COL=16, ZR=144, Z1=144, M1=128, G=352, G4=1088, RSZ=128, ONE=72, KA=32, WP=192, THR=8, XF=64, C=72, CW=72,
-            S4=16, X0=64, X1=64, MM=192, MU=512, M4=64, ZS=128, SCN=128, XG=32)
-_I32 = dict(W=P, N0=256, N4=144, N16=128, CI32=8)
-_U16 = dict(OFF=96, LP=256, OC=16, CI=16, IDS0=16, IDS1=16, IDP=16, CP0=16, CP1=16, CL0=16, CL1=16, PL0=16)
+_BF = dict(D=DW, Z=144, Z4=144, ZQ=144, Z1=144, B=128, U=128, V=128, NV=128, N4=144, N16=128, CB=16,
+           IDM=128 * len(SC), MO=1472, MI=1472, ONE=256, IOT=80, CF=64, NE=1536, FB=80, OWN=64, OTH=64, NEO=64,
+           NEP=64, LV=4352, LVP=4352, L4=1088, L4S=1024, L4P=1088, T4=1024, T3=256, F5=352, RS5=320, RS68=272, CADD=160,
+           CK=128, C15=256, LE4=272, S16=272, LE=64, A0=256, A1=256, B0=256, B1=256, GT=256, MD0=256, MD1=256, PA0=64,
+           PAP=64, UF=416, XH=64, XL=64, M3=256, N32=32, M4=64)
+_F32 = dict(COL=24, NF=256, ZR=144, G=352, G4=1088, RSZ=128, KA=32, WP=192, THR=8, XF=64, C=72, CW=72,
+            X0=64, X1=64, XO=64, MM=192, ZS=128, SCN=128, XG=32, SK=512, OP4=1088)
+_I32 = dict(W=P, K0=8)
+_U16 = dict(OFF=96, LP=256, OC=16, CI=16, IDS0=16, IDS1=16, IDP=16, CP0=16, CP1=16, CL0=16, CL1=16)
 SCRATCH = {}
 for _d, _t in ((_BF, "bfloat16"), (_F32, "float32"), (_I32, "int32"), (_U16, "uint16")):
     for _k in _d:
         SCRATCH[_k] = _sb(_d[_k], _t)
 for _i in range(8):
     SCRATCH["P%d" % _i] = ("psum", [128, 512], "float32")
-NPOOL = 100
-SEMAPHORES = (["s%d" % i for i in range(NPOOL)] + ["d%d" % i for i in range(10)]
-              + ["l%d" % i for i in range(12)] + ["r%d" % i for i in range(12)])
+NPOOL = 90
+NMSG = 24
+SEMAPHORES = (["s%d" % i for i in range(NPOOL)] + ["d%d" % i for i in range(12)]
+              + ["l%d" % i for i in range(NMSG)] + ["r%d" % i for i in range(NMSG)])
+CYC, TCYC = 0.83e-3, 0.4e-3
+WAKE, TURN = 0.16, 0.14
+GATHER, SCATTER = 1.4, 2.75
+SMALL, SSMALL = 0.035, 0.16
+LOCAL, NEAR, FAR = 540e3, 270e3, 190e3
+LAG, RLAG = 1.3, 1.45
+MARGIN = 0.0
+SPARE = 0.2
 
 
-def build(core, T, topo):
+def build(core, T, topo, puts=()):
     rank = T.rank_of(core)
     peer = [T.cores[rank ^ m] for m in MEETS]
     ops = []
 
     def A(name, lo, hi, step=1):
         ap = T[name][:, lo:hi] if step == 1 else T[name][:, lo:hi:step]
-        return (ap, [(name, lo, hi)], [])
+        return (ap, [(name, lo, hi)], [], len(range(lo, hi, step)), "")
 
     def IND(win, off):
-        return (win[0].indirect(off[0]), win[1], off[1])
-
-    def only(a, tag):
-        return (a[0], [(a[1][0][0] + "_%d" % tag, 0, 1)], a[2])
-
-    def also(a, regions):
-        return (a[0], a[1], a[2] + regions)
+        return (win[0].indirect(off[0]), win[1], off[1], 16 * off[3], "ind")
 
     def col(j):
         return A("COL", j, j + 1)
 
-    def add(q, fn, outs, ins, kind="c", **kw):
+    def add(ways, outs, ins, kind="c", **kw):
         w = [r for o in outs for r in o[1]]
         rd = [r for o in ins for r in o[1]] + [r for o in list(outs) + list(ins) for r in o[2]]
-        ops.append(dict(q=q, fn=fn, w=w, r=rd, kind=kind, **kw))
+        ops.append(dict(ways=ways, q=list(ways)[0], w=w, r=rd, kind=kind, **kw))
         return len(ops) - 1
 
     def val(s):
@@ -70,37 +81,66 @@ def build(core, T, topo):
     def aps(*s):
         return [x for x in s if isinstance(x, tuple)]
 
+    def vtime(o, ins, both=1.0):
+        if o[4]:
+            return 0.07 + o[3] * SCATTER * CYC
+        if any(i[4] for i in ins):
+            return 0.07 + o[3] * GATHER * CYC
+        narrow = all(SCRATCH[x[1][0][0]][2] in ("bfloat16", "uint16") for x in [o] + ins)
+        return SMALL + max(64, o[3] * both * (0.5 if narrow else 1)) * CYC
+
+    def stime(o, i):
+        return 0.09 + o[3] * GATHER * CYC if i[4] else SSMALL + max(64, o[3]) * CYC
+
     def copy(o, i):
-        return add("vector", lambda e: e.tensor_copy(o[0], i[0]), [o], [i])
+        return add({"vector": (lambda e: e.tensor_copy(o[0], i[0]), vtime(o, [i]))}, [o], [i])
 
     def tt(o, a, b, op):
-        return add("vector", lambda e: e.tensor_tensor(o[0], a[0], b[0], op), [o], [a, b])
+        both = 1.0 if a[1][0][0][0] == "P" and a[1][0][0][1:].isdigit() else 2.0
+        return add({"vector": (lambda e: e.tensor_tensor(o[0], a[0], b[0], op), vtime(o, [a, b], both))}, [o], [a, b])
 
     def ts(o, a, s1, s2, op0, op1=None):
         if op1 is None:
             fn = lambda e: e.tensor_scalar(o[0], a[0], val(s1), None, op0)
         else:
             fn = lambda e: e.tensor_scalar(o[0], a[0], val(s1), val(s2), op0, op1)
-        return add("vector", fn, [o], [a] + aps(s1, s2))
+        return add({"vector": (fn, vtime(o, [a]))}, [o], [a] + aps(s1, s2))
 
-    def scan(o, d0, d1, op0, op1):
-        return add("vector", lambda e: e.tensor_tensor_scan(o[0], d0[0], d1[0], 0.0, op0, op1), [o], [d0, d1])
+    def scan(o, d0, d1, op0, op1, first=0.0):
+        return add({"vector": (lambda e: e.tensor_tensor_scan(o[0], d0[0], d1[0], first, op0, op1),
+                               vtime(o, [d0, d1]))}, [o], [d0, d1])
 
-    def fill(o, c):
-        return add("vector", lambda e: e.memset(o[0], c), [o], [])
+    def act(o, i, scale=1.0, bias=0.0, func=ACT.Identity):
+        return add({"scalar": (lambda e: e.activation(o[0], i[0], func, bias=val(bias), scale=val(scale)),
+                               stime(o, i))}, [o], [i] + aps(scale, bias))
 
-    def act(o, i, scale=1.0, bias=0.0):
-        return add("scalar", lambda e: e.activation(o[0], i[0], ACT.Identity, bias=bias, scale=scale), [o], [i])
+    def aff(o, i, scale=1.0, bias=0.0):
+        return add({"vector": (lambda e: e.tensor_scalar(o[0], i[0], val(scale), val(bias), ALU.mult, ALU.add),
+                               vtime(o, [i])),
+                    "scalar": (lambda e: e.activation(o[0], i[0], ACT.Identity, bias=val(bias), scale=val(scale)),
+                               stime(o, i))}, [o], [i] + aps(scale, bias))
 
-    def afill(o, n, c):
-        return act(o, A("IDM", 0, n), scale=0.0, bias=c)
+    def move(o, i):
+        return add({"vector": (lambda e: e.tensor_copy(o[0], i[0]), vtime(o, [i])),
+                    "scalar": (lambda e: e.activation(o[0], i[0], ACT.Identity), stime(o, i))}, [o], [i])
+
+    def memset(o, c):
+        return add({"vector": (lambda e: e.memset(o[0], c), vtime(o, []))}, [o], [])
+
+    def fill(name, lo, hi, c, step=1):
+        for a in range(lo, hi, 256 * step):
+            o = A(name, a, min(hi, a + 256 * step), step)
+            i = A("ONE", 0, o[3])
+            add({"vector": (lambda e, o=o: e.memset(o[0], c), vtime(o, [])),
+                 "scalar": (lambda e, o=o, i=i: e.activation(o[0], i[0], ACT.Identity, bias=c, scale=0.0),
+                            stime(o, i))}, [o], [i])
 
     def iota(o, pat, base, cm, fl=False):
         if fl:
             fn = lambda e: e.iota(o[0], pat, base, cm, allow_small_or_imprecise_dtypes=True)
         else:
             fn = lambda e: e.iota(o[0], pat, base, cm)
-        return add("g", fn, [o], [])
+        return add({"g": (fn, 0.13 + 2 * o[3] * CYC)}, [o], [])
 
     def mm(o, terms, start=True, stop=True, after=None):
         def fn(e):
@@ -108,13 +148,17 @@ def build(core, T, topo):
             for n, (l, r) in enumerate(terms):
                 last = e.matmul(o[0], l[0], r[0], start and n == 0, stop and n == len(terms) - 1)
             return last
-        return add("tensor", fn, [o], [x for t in terms for x in t], after=after)
+        wide = 4 if SCRATCH[terms[0][0][1][0][0]][2] == "float32" else 1
+        return add({"tensor": (fn, 0.02 + len(terms) * max(64, o[3]) * wide * TCYC)}, [o],
+                   [x for t in terms for x in t], after=after)
 
     ndma = [0]
 
-    def dma(o, i, outs, ins, q="sync"):
+    def dma(pairs, outs, ins, size, q="sync"):
         ndma[0] += 1
-        return add(q, lambda e: e.dma_start(o, i), outs, ins, kind="dma", sem="d%d" % (ndma[0] - 1), n=16)
+        return add({q: (lambda e: [e.dma_start(o, i) for o, i in pairs], 0.05 * len(pairs))}, outs, ins, kind="dma",
+                   sem="d%d" % (ndma[0] - 1), n=16 * len(pairs), lane="local" if size > 5000 else "small",
+                   size=size / LOCAL, lag=LAG)
 
     nmsg = [0]
 
@@ -124,254 +168,143 @@ def build(core, T, topo):
         rid, pid = topo.addr(peer[m])[:2]
         mask = topo.mask(core, peer[m])
         n = len(topo.engines(core, peer[m]))
-        add("g", lambda e: e.remote_dma(dst[0], src[0], T.sem["r%d" % k], T.sem["l%d" % k], pid, rid, mask),
-            [], [src], kind="send", sem="l%d" % k, n=n)
-        add(None, None, [dst], [], kind="arr", sem="r%d" % k, n=len(topo.engines(peer[m], core)))
+        far = topo.chip(core) != topo.chip(peer[m])
+        s = add({"g": (lambda e: e.remote_dma(dst[0], src[0], T.sem["r%d" % k], T.sem["l%d" % k], pid, rid, mask), 0.4)},
+                [], [src], kind="send", sem="l%d" % k, n=n, lane="far" if far else "near", lag=RLAG,
+                size=(0.1 if far else 0.05) + 256 * src[3] / (FAR if far else NEAR))
+        add({None: (None, 0.0)}, [dst], [], kind="arr", sem="r%d" % k, n=len(topo.engines(peer[m], core)), of=s)
 
     def ident(w):
         j = SC.index(w)
         return A("IDM", 128 * j, 128 * j + 128)
 
+    def idents(w0, w1):
+        return A("IDM", 128 * SC.index(w0), 128 * SC.index(w1) + 128)
+
+    def slid(name, lo):
+        return A(name, lo, lo + 128)
+
     def R(q):
-        return A("ZR", 12 - 4 * q, 140 - 4 * q)
+        return slid("ZR", 12 - 4 * q)
 
     def E(p, name="Z"):
-        return A(name, 15 - p, 143 - p)
+        return slid(name, 15 - p)
 
     def rnd(o, i):
         ts(o, i, BIG, BIG, ALU.add, ALU.subtract)
+
+    def apart(m, i):
+        ops[i]["apart"] = m
+
+    def in_parts(o, terms, n):
+        last = None
+        for a in range(0, len(terms), n):
+            last = mm(o, terms[a:a + n], a == 0, a + n >= len(terms), last)
 
     DWIN = A("D", 0, DW)
     WWIN = A("W", 0, P)
     LWIN = A("LV", 0, 4352)
     PA = (A("PA0", 0, 64), A("UF", 352, 416))
-    PL = (A("PL0", 0, 4), A("OFF", 90, 94))
+    BM = A("B", 0, 128)
+    ONE = A("ONE", 0, 256)
+    G16, G4 = A("CB", 0, 1), A("CB", 8, 9)
+    S, K4, LAST = col(5), col(6), col(9)
+    l2, l3 = A("P0", 0, 64), A("P7", 0, 256)
+    mid = (ident(1), A("C15", 0, 256))
 
-    def kids(lo, hi):
-        dma(T["W"][0:128:4, lo:hi], T["kids"][:, lo:hi], [A("W", lo, hi)], [])
+    def NF(n):
+        return A("NF", 0, n)
 
-    dma(T["D"][:, 0:512], T["dg"][:, 0:512], [A("D", 0, 512)], [])
-    dma(T["D"][:, 512:SPLIT], T["dg"][:, 512:SPLIT], [A("D", 512, SPLIT)], [])
-    iota(A("N0", 0, 256), [[1, 256]], 0, 0)
-    iota(A("CI32", 0, 1), [[0, 1]], 0, 1)
-    iota(A("W", WV[1], WG[0]), [[1, WG[0] - WV[1]]], WV[1], 0)
-    iota(A("W", WG[0], P), [[1, P - WG[0]]], WG[0], 0)
-    fill(A("D", 5456, DW), 0.0)
-    for c in range(0, WV[1], 256):
-        n = min(256, WV[1] - c)
-        ts(A("W", c, c + n), A("N0", 0, n), float(c), None, ALU.add)
-        if c + n == WV[0]:
-            kids(0, WV[0])
-            kids(WV[1], WG[0])
-    kids(WV[0], WV[1])
-    kids(WG[0], P)
-    dma(T["D"][:, SPLIT:P], T["dg"][:, SPLIT:P], [A("D", SPLIT, 5464)], [])
-    send(0, A("RT", 0, 4), A("D", 0, 4))
-    ts(A("CI32", 1, 2), A("CI32", 0, 1), 15, None, ALU.bitwise_and)
-    ts(A("CI32", 2, 3), A("CI32", 0, 1), 12, None, ALU.bitwise_and)
-    copy(A("COL", 1, 2), A("CI32", 0, 1))
-    ts(A("N4", 0, 144), A("N0", 0, 144), 508, None, ALU.bitwise_and)
-    copy(A("COL", 0, 1), A("CI32", 1, 2))
-    ts(A("COL", 7, 8), A("CI32", 2, 3), 3.0, None, ALU.add)
-    ts(ident(1), A("N0", 0, 128), col(1), None, ALU.is_equal)
-    tt(A("COL", 2, 3), col(1), col(0), ALU.subtract)
-    ts(A("N16", 0, 128), A("N0", 0, 128), 496, None, ALU.bitwise_and)
-    ts(A("COL", 3, 4), col(0), 0.25, col(2), ALU.mult, ALU.add)
-    ts(A("M1", 0, 128), A("N4", 0, 128), col(1), None, ALU.is_equal)
-    ts(A("ZR", 0, 144), A("N0", 0, 144), -12.0, col(3), ALU.add, ALU.is_equal)
-    ts(A("Z", 0, 144), A("N0", 0, 144), -15.0, col(2), ALU.add, ALU.is_equal)
-    ts(A("Z4", 0, 144), A("N4", 0, 144), -12.0, col(2), ALU.add, ALU.is_equal)
-    ts(A("B", 0, 128), A("N16", 0, 128), col(2), None, ALU.is_equal)
-    copy(A("G", 0, 4), A("W", 0, 4))
-    mm(A("P0", 0, 1), [(R(q), A("G", q, q + 1)) for q in range(4)])
-    mm(A("P0", 4, 8), [(A("M1", 0, 128), A("G", 0, 4))])
-    for w in SC[1:11]:
-        act(ident(w), ident(1), scale=float(w))
-    afill(A("CK", 0, 64), 64, 0.5)
-    afill(A("CK", 64, 128), 64, -127.5)
-    afill(A("C127", 0, 512), 512, 127.5)
-    afill(A("KA", 0, 16), 16, 120.5)
-    afill(A("KA", 16, 32), 16, 0.5)
-    afill(A("LV", 4096, 4352), 256, 0.0)
-    afill(A("RSZ", 0, 128), 128, 1.0)
-    ts(A("UT", 0, 128), A("N0", 0, 128), col(1), None, ALU.is_lt)
-    ts(A("COL", 4, 5), col(0), 1.0, None, ALU.is_equal)
-    ts(A("COL", 5, 6), col(0), 15.0, None, ALU.is_equal)
-    ts(A("COL", 6, 7), col(0), float(DUM), None, ALU.add)
-    ts(A("COL", 8, 9), col(0), 3.0, 16.0, ALU.min, ALU.mult)
-    ts(A("COL", 9, 10), col(0), 15.0, float(DUM + 2), ALU.mult, ALU.add)
-    copy(A("OC", 10, 14), A("N0", 0, 4))
-    fill(A("F5", 320, 340), 1.0)
-    fill(A("RS5", 0, 320), 0.0)
-    fill(A("RS68", 0, 272), 1.0)
-    copy(A("OFF", 88, 89), A("P0", 0, 1))
-    copy(A("OFF", 64, 68), A("P0", 4, 8))
-    iota(A("WP", 0, 64), [[0, 16], [2, 4]], 1, 0, True)
-    iota(A("WP", 128, 192), [[0, 4], [2, 4], [0, 4]], 1, 0, True)
+    def digests(lo, hi, end):
+        dma([(T["D"][:, lo:hi], T["dg"][:, lo:hi])], [A("D", lo, end)], [], 256 * (hi - lo))
 
-    def late(part):
-        if part == 0:
-            tt(A("U", 0, 128), A("UT", 0, 128), A("B", 0, 128), ALU.mult)
-            ts(A("V", 0, 128), A("B", 0, 128), col(5), None, ALU.mult)
-            ts(A("G4", 1024, 1088), A("N0", 0, 64), 16.0, col(6), ALU.mult, ALU.add)
-            ts(A("THR", 0, 4), A("N0", 0, 4), 16.0, col(0), ALU.mult, ALU.add)
-            copy(A("XF", 0, 64), A("N0", 0, 64))
-            fill(A("RS5", 0, 320, 5), 1.0)
-            fill(A("RS68", 0, 272, 68), 0.0)
-        elif part == 1:
-            fill(A("ONE", 0, 68), 1.0)
-            ts(A("Z1", 0, 144), A("Z", 0, 144), col(4), None, ALU.mult)
-            ts(A("OC", 0, 4), A("N0", 0, 4), 16.0, 79.0, ALU.mult, ALU.add)
-            ts(A("OC", 4, 8), A("N0", 0, 4), 16.0, col(7), ALU.mult, ALU.add)
-            ts(A("OC", 8, 9), col(0), 4.0, 3.0, ALU.mult, ALU.add)
-            ts(A("COL", 10, 11), col(0), 4.0, col(9), ALU.is_ge, ALU.mult)
-            ts(A("ZQ", 0, 144), A("Z", 0, 144), 4.0, None, ALU.mult)
-            fill(A("FB", 64, 68), 1.0)
-        else:
-            fill(A("NE", 1024, 1088), 0.0)
-            fill(A("L4", 1024, 1088), 0.0)
-            fill(A("L4P", 1024, 1088), 0.0)
-            ts(A("OC", 9, 10), col(8), 79.0, None, ALU.add)
-            ts(A("OFF", 89, 90), col(10), col(0), None, ALU.add)
-            fill(A("RSZ", 0, 64, 4), 0.0)
-            fill(A("RSZ", 64, 128, 16), 0.0)
-            tt(A("WP", 64, 128), A("WP", 0, 64), A("WP", 128, 192), ALU.mult)
-
-    for part, (go, n, src, dst) in enumerate(((16, 16, 88, 84), (32, 64, 84, 68), (96, 256, 68, 0))):
+    def level(go, n, src, dst):
         copy(A("G", go, go + n), IND(WWIN, A("OFF", src, src + n // 16)))
         mm(A("P0", 0, n // 4), [(R(q), A("G", go + q, go + n, 4)) for q in range(4)])
-        if n == 256:
-            act(A("MO", 1024, 1408), IND(DWIN, A("OFF", 64, 88)))
-            send(0, A("MI", 1024, 1408), A("MO", 1024, 1408))
-        late(part)
         copy(A("OFF", dst, dst + n // 4), A("P0", 0, n // 4))
-    for h in range(2):
-        act(A("MO", 512 * h, 512 * h + 256), IND(DWIN, A("OFF", 32 * h, 32 * h + 16)))
-        copy(A("MO", 512 * h + 256, 512 * h + 512), IND(DWIN, A("OFF", 32 * h + 16, 32 * h + 32)))
-        send(0, A("MI", 512 * h, 512 * h + 512), A("MO", 512 * h, 512 * h + 512))
-    QB = ("P0", "P5", "P6", "P7")
 
     def quarter(h):
+        bank = A(("P0", "P5", "P6", "P7")[h], 0, 64)
         copy(A("G4", 256 * h, 256 * h + 256), IND(WWIN, A("OFF", 16 * h, 16 * h + 16)))
-        mm(A(QB[h], 0, 64), [(R(q), A("G4", 256 * h + q, 256 * h + 256, 4)) for q in range(4)])
+        mm(bank, [(R(q), A("G4", 256 * h + q, 256 * h + 256, 4)) for q in range(4)])
+        copy(A("LP", 64 * h, 64 * h + 64), bank)
 
-    def quarter_out(h):
-        copy(A("LP", 64 * h, 64 * h + 64), A(QB[h], 0, 64))
-        if h < 3:
-            act(A("LV", 1024 * h, 1024 * h + 1024), IND(DWIN, A("LP", 64 * h, 64 * h + 64)))
+    def stored4(h):
+        for lo in (512 * h, 512 * h + 256):
+            (copy if lo == 256 else act)(A("MO", lo, lo + 256), IND(DWIN, A("OFF", lo // 16, lo // 16 + 16)))
+        send(0, A("MI", 512 * h, 512 * h + 512), A("MO", 512 * h, 512 * h + 512))
 
-    quarter(0)
-    quarter(1)
-    tt(A("NE0", 0, 4), A("D", 0, 4), A("RT", 0, 4), ALU.not_equal)
-    quarter_out(0)
-    quarter(2)
-    quarter_out(1)
-    quarter(3)
-    copy(A("NE", 1472, 1536), IND(A("NE0", 0, 4), A("OC", 10, 14)))
-    tt(A("NE", 1088, 1472), A("MO", 1024, 1408), A("MI", 1024, 1408), ALU.not_equal)
-    quarter_out(2)
-    quarter_out(3)
+    def leaves(pieces):
+        for lo, hi, eng in pieces:
+            if eng == "send":
+                if ALL1:
+                    send(0, A("LVP", lo, hi), A("LV", lo, hi))
+            else:
+                {"V": copy, "S": act, "": move}[eng](A("LV", lo, hi), IND(DWIN, A("LP", lo // 16, hi // 16)))
 
-    def leaves(lo, hi):
-        copy(A("LV", lo, hi), IND(DWIN, A("LP", lo // 16, hi // 16)))
-
-    SHUT = (A("P1", 0, 256), A("P1", 256, 512), A("P2", 0, 256), A("P7", 0, 256))
-    OPEN = (A("P6", 0, 256), A("P0", 0, 256), A("P5", 0, 256), A("P1", 0, 256))
-    bs = [None] * 4
-
-    def bulk_sum(h, shut=True, opened=True):
-        terms = [(ident(WK[k]), A("LV", 1024 * h + k, 1024 * h + 1024, 4)) for k in range(4)]
-        if shut:
-            mm(SHUT[h], terms)
-        if opened:
-            bs[h] = mm(OPEN[h], terms, stop=False)
-
-    def bulk_q(h, src):
-        act(A("T4", 256 * h, 256 * h + src[1][0][2]), src, scale=1.0 / 256, bias=128.501953125)
-
-    def bulk_fix(h):
-        mm(OPEN[h], [(ident(-256), A("T4", 256 * h, 256 * h + 256))], start=False, after=bs[h])
-        act(A("L4S", 256 * h, 256 * h + 256), OPEN[h], bias=129.0 * 256 - 127.5)
-
-    def count4():
-        mm(A("P3", 0, 320, 5), [(E(p), A("NE", p, 1024, 16)) for p in range(16)])
-
-    def count4_half(h):
-        mm(A("P3", 384 + 32 * h, 416 + 32 * h), [(E(p), A("NE", 512 * h + p, 512 * h + 512, 16)) for p in range(16)])
+    def level4(h):
+        s4, t4 = A(("P0", "P7", "P2", "P1")[h], 0, 256), A("T4", 256 * h, 256 * h + 256)
+        mm(s4, [mid] + [(ident(WK[k]), A("LV", 1024 * h + k, 1024 * h + 1024, 4)) for k in range(4)])
+        aff(t4, s4, 1.0, -127.5)
+        tt(A("L4S", 256 * h, 256 * h + 256), s4, t4, ALU.subtract)
+        if h % 2:
+            send(1, A("L4P", 256 * h - 256, 256 * h + 256), A("L4S", 256 * h - 256, 256 * h + 256))
 
     def count3(l3):
-        mm(A("P3", 1, 320, 5), [(A("Z4", 12 - 4 * k, 140 - 4 * k), A("NE", l3 + k, l3 + 256, 4)) for k in range(4)])
+        mm(A("P3", 1, 320, 5), [(slid("Z4", 12 - 4 * k), A("NE", l3 + k, l3 + 256, 4)) for k in range(4)])
 
     def count_up(t, lo):
-        mm(A("P3", t, 320, 5), [(A("B", 0, 128), A("NE", lo, lo + 64))])
+        mm(A("P3", t, 320, 5), [(BM, A("NE", lo, lo + 64))])
 
-    def candidates(m, f, hook):
-        a, b = "A%d" % m, "B%d" % m
-        mm(A("P4", 0, 68), [(A("B", 0, 128), f)])
+    def candidates(m, f):
+        mm(A("P4", 0, 68), [(BM, f)])
         mm(A("P4", 68, 136), [(A("U", 0, 128), f)])
-        hook(0)
         scan(A("C", 0, 68), A("ONE", 0, 68), A("P4", 0, 68), ALU.mult, ALU.add)
         for q in range(4):
             ts(A("LE4", 68 * q, 68 * q + 68), A("C", 0, 68), A("THR", q, q + 1), 16.0, ALU.is_le, ALU.mult)
-        tt(A("CW", 0, 68), A("C", 0, 68), A("P4", 68, 136), ALU.subtract)
         scan(A("S16", 0, 272), A("RS68", 0, 272), A("LE4", 0, 272), ALU.mult, ALU.add)
+        tt(A("CW", 0, 68), A("C", 0, 68), A("P4", 68, 136), ALU.subtract)
         ts(A("CI", 0, 4), A("S16", 67, 272, 68), 1.0 / 16, None, ALU.mult)
         tt(A("LE", 0, 64), IND(A("CW", 0, 68), A("CI", 0, 4)), A("XF", 0, 64), ALU.is_le)
-        mm(A("P4", 256, 260), [(E(p, "ZQ"), A("LE", p, 64, 16)) for p in range(16)])
-        for k in range(4):
-            ts(A("S4", 4 * k, 4 * k + 4), A("S16", 67, 272, 68), 4.0, float(k), ALU.mult, ALU.add)
-        hook(1)
-        cl = "CL%d" % m
-        for q in range(4):
-            ts(only(A(cl, q, 16, 4), q), A("S4", q, 16, 4), A("P4", 256 + q, 257 + q), None, ALU.add)
-        allcl = [(cl + "_%d" % q, 0, 1) for q in range(4)]
-        if m == 0:
-            copy(A(a, 0, 256), also(IND(LWIN, A(cl, 0, 16)), allcl))
-        else:
-            act(A(a, 0, 128), also(IND(LWIN, A(cl, 0, 8)), allcl))
-            copy(A(a, 128, 256), also(IND(LWIN, A(cl, 8, 16)), allcl))
-        send(m, A(b, 0, 256), A(a, 0, 256))
-        ts(A("IDS%d" % m, 0, 4), also(A(cl, 0, 4), allcl), 0.25, None, ALU.mult)
+        move(A("CF", 0, 64), IND(A("IOT", 0, 80), A("CI", 0, 4)))
+        mm(A("P4", 256, 272), [(slid("ZQ", 12 - 4 * k), A(x, k, 64, 4)) for x in ("LE", "CF") for k in range(4)])
+        ts(A("CL%d" % m, 0, 16), A("P4", 256, 272), K4, None, ALU.add)
+
+    def ids(m):
+        in_parts(A("P4", 320, 324),
+                 [(ident(1), A("S16", 67, 272, 68))] + [(E(p), A("LE", p, 64, 16)) for p in range(16)], 9)
+        copy(A("IDS%d" % m, 0, 4), A("P4", 320, 324))
+
+    def exchange(m):
+        a, cl = "A%d" % m, "CL%d" % m
+        for lo in (0, 128):
+            move(A(a, lo, lo + 128), IND(LWIN, A(cl, lo // 16, lo // 16 + 8)))
+        send(m, A("B%d" % m, 0, 256), A(a, 0, 256))
 
     def places(m):
-        copy(A("X%d" % m, 0, 64), IND(A("G4", 0, 1088), A("IDS%d" % m, 0, 4)))
-
-    def places_kids(m):
+        move(A("X%d" % m, 0, 64), IND(A("G4", 0, 1088), A("IDS%d" % m, 0, 4)))
         mm(A("P2", 0, 16), [(R(q), A("X%d" % m, q, 64, 4)) for q in range(4)])
+        copy(A("CP%d" % m, 0, 16), A("P2", 0, 16))
 
-    def places_own(m, lo, hi, after=None):
-        return mm(A("P1", 0, 4), [(E(p, "Z1"), A("X%d" % m, p, 64, 16)) for p in range(lo, hi)], lo == 0, hi == 16, after)
-
-    def places_out(m, which):
-        if which == 0:
-            copy(A("CP%d" % m, 0, 16), A("P2", 0, 16))
-        else:
-            copy(PL[m], A("P1", 0, 4))
-
-    def open4(m):
-        a = "A%d" % m
-        return mm(A("P6", 0, 64), [(ident(1), A("CK", 64, 128))]
-                  + [(ident(WK[k]), A(a, 64 * k, 64 * k + 64)) for k in range(4)], stop=False)
-
-    def settle(m, g4):
-        a, b, pa, md = A("A%d" % m, 0, 256), A("B%d" % m, 0, 256), PA[m], "MD%d" % m
-        tt(A("GT", 0, 256), b, a, ALU.is_gt)
-        mm(A("P5", 0, 256), [(A("V", 0, 128), A("GT", 0, 256))])
-        tt(A("DF", 0, 256), b, a, ALU.subtract)
-        tt(A(md, 0, 256), A("P5", 0, 256), A("DF", 0, 256), ALU.mult)
-        mm(A("P6", 0, 64), [(ident(WK[k]), A(md, 64 * k, 64 * k + 64)) for k in range(4)], start=False, after=g4)
-        for k in range(4):
-            tt(only(A("NEW%d" % m, k, 256, 4), k), A("A%d" % m, 64 * k, 64 * k + 64), A(md, 64 * k, 64 * k + 64), ALU.add)
-        rnd(A("M4", 0, 64), A("P6", 0, 64))
+    def settle(m):
+        a, b, pa, md = "A%d" % m, A("B%d" % m, 0, 256), PA[m], "MD%d" % m
+        own = (mm(A("P5", 0, 256), [(A("NV", 0, 128), A(a, 0, 256))], stop=False),
+               mm(A("P3", 0, 256), [(ident(-1), A(a, 0, 256))], stop=False),
+               mm(A("P6", 0, 64), [(ident(1), A("C15", 0, 64))]
+                  + [(ident(WK[k]), A(a, k, 256, 4)) for k in range(4)], stop=False))
+        mm(A("P5", 0, 256), [(A("V", 0, 128), b)], start=False, after=own[0])
+        mm(A("P3", 0, 256), [(ident(1), b)], start=False, after=own[1])
+        ts(A("GT", 0, 256), A("P5", 0, 256), 0.0, None, ALU.is_gt)
+        tt(A(md, 0, 256), A("P3", 0, 256), A("GT", 0, 256), ALU.mult)
+        mm(A("P6", 0, 64), [(ident(WK[k]), A(md, k, 256, 4)) for k in range(4)], start=False, after=own[2])
+        ts(A("M4", 0, 64), A("P6", 0, 64), -127.5, None, ALU.add)
         tt(pa, A("P6", 0, 64), A("M4", 0, 64), ALU.subtract)
-
-    l2, l3 = A("P0", 0, 64), A("P7", 0, 256)
 
     def sum2(src, sign, start, stop, after=None):
         return mm(l2, [(ident(sign * WK[j // 4] * WK[j % 4]), A(src, j, 1024, 16)) for j in range(16)], start, stop, after)
 
-    def sum3(src, sign, start, stop, after=None):
-        return mm(l3, [(ident(sign * WK[k]), A(src, k, 1024, 4)) for k in range(4)], start, stop, after)
+    def terms3(src, sign):
+        return [(ident(sign * WK[k]), A(src, k, 1024, 4)) for k in range(4)]
 
     def low_sums():
         tt(A("ZS", 0, 64), l2, A("WP", 0, 64), ALU.mult)
@@ -379,129 +312,216 @@ def build(core, T, topo):
         rnd(A("MM", 0, 64), l2)
         scan(A("SCN", 0, 128), A("RSZ", 0, 128), A("ZS", 0, 128), ALU.mult, ALU.add)
 
-    def mod3():
-        o = A("P2", 0, 256)
-        act(A("T3", 0, 256), l3, scale=1.0 / 256, bias=2040 / 256.0 + 128.501953125)
-        first = mm(o, [(ident(WK[k]), A("L4", k, 1024, 4)) for k in range(4)], stop=False)
-        mm(o, [(ident(-256), A("T3", 0, 256))], start=False, after=first)
-        act(A("UF", 0, 256), o, bias=2040 + 129.0 * 256 - 127.5)
-
     def own4(m):
         copy(IND(A("L4", 0, 1088), A("IDS%d" % m, 0, 4)), PA[m])
 
-    def put_leaves(m):
-        copy(IND(DWIN, A("CP%d" % m, 0, 16)), also(A("NEW%d" % m, 0, 256), [("NEW%d_%d" % (m, k), 0, 1) for k in range(4)]))
+    def put_leaves(m, n):
+        for lo in range(0, 256, n):
+            apart(m, tt(IND(DWIN, A("CP%d" % m, lo // 16, (lo + n) // 16)), A("A%d" % m, lo, lo + n),
+                        A("MD%d" % m, lo, lo + n), ALU.add))
 
-    def put_l4(lo, hi, src="L4"):
-        tt(IND(DWIN, A("OFF", lo // 16, hi // 16)), A(src, lo, hi), A("C127", 0, hi - lo), ALU.add)
-
+    dma([(T["K0"][q:128:4, 0:4], T["kids"][:, 0:4]) for q in range(4)], [A("K0", 0, 4)], [], 2048, "scalar")
+    dma([(T["D"][:, 0:16], T["dg"][:, 0:16])], [A("D", 0, 16)], [], 4096, "scalar")
+    dma([(T["W"][q:128:4, 0:WR], T["kids"][:, 0:WR]) for q in range(4)], [A("W", 0, WR)], [], 512 * WR)
+    iota(A("COL", 0, 5), [[768, 5]], 0, 1, True)
+    memset(ONE, 1.0)
+    memset(A("W", WR, WV[0]), 0)
+    scan(NF(256), ONE, ONE, ALU.mult, ALU.add, -1.0)
+    memset(A("W", WV[0], WV[1]), 0)
+    for lo, hi in zip(WV[-1:] + WG, WG):
+        iota(A("W", lo, hi), [[0, hi - lo]], 0, 0)
+    for lo, hi in ((WV[-1], WG[0]), (WR, WV[0]), (WG[0], WG[1]), (WV[0], WV[1])):
+        dma([(T["W"][0:128:4, lo:hi], T["kids"][:, lo:hi])], [A("W", lo, hi)], [], 128 * (hi - lo))
+    digests(16, SPLIT, SPLIT)
+    fill("D", 5456, DW, 0.0)
+    digests(SPLIT, P, 5464)
+    aff(G16, col(4), 1.0, -7.5)
+    aff(col(8), col(0), 0.25, 12.0 - 2304.0)
+    aff(col(7), G16, 0.75, col(8))
+    ts(A("ZR", 0, 144), NF(144), col(7), None, ALU.is_equal)
+    copy(A("G", 0, 4), A("K0", 0, 4))
+    mm(A("P0", 0, 1), [(R(q), A("G", q, q + 1)) for q in range(4)])
+    copy(A("OFF", 88, 89), A("P0", 0, 1))
+    copy(A("OFF", 64, 68), A("K0", 0, 4))
+    copy(A("OC", 10, 14), NF(4))
+    level(16, 16, 88, 84)
+    level(32, 64, 84, 68)
+    level(96, 256, 68, 0)
+    move(A("MO", 1408, 1472), IND(A("D", 0, 16), A("OC", 10, 14)))
+    send(0, A("MI", 1408, 1472), A("MO", 1408, 1472))
+    act(A("MO", 1024, 1408), IND(DWIN, A("OFF", 64, 88)))
+    send(0, A("MI", 1024, 1408), A("MO", 1024, 1408))
+    quarter(0)
+    stored4(0)
+    stored4(1)
+    quarter(1)
+    aff(G4, col(1), 1.0, -1.5)
+    aff(A("N4", 0, 144), NF(144), 1.0, 766.5)
+    aff(A("N16", 0, 128), NF(128), 1.0, 3064.5)
+    aff(S, G16, -1.0, col(4))
+    aff(K4, G4, -1.0, col(1))
+    ts(A("Z", 0, 144), NF(144), 3057.0, G16, ALU.add, ALU.is_equal)
+    ts(A("Z4", 0, 144), A("N4", 0, 144), 2292.0, G16, ALU.add, ALU.is_equal)
+    ts(BM, A("N16", 0, 128), G16, None, ALU.is_equal)
+    ts(ident(1), NF(128), col(0), None, ALU.is_equal)
+    add({"g": (lambda e: e.affine_select(T["U"][:, 0:128], BM[0], [[-1, 128]], ALU.is_gt, 0.0, 0, 1), 0.38)},
+        [A("U", 0, 128)], [BM])
+    fill("RS5", 0, 320, 0.0)
+    fill("RS5", 0, 320, 1.0, 5)
+    fill("RS68", 0, 272, 1.0)
+    fill("RS68", 0, 272, 0.0, 68)
+    fill("FB", 64, 68, 1.0)
+    fill("LV", 4096, 4352, 0.0)
+    if ALL1:
+        fill("LVP", 4096, 4352, 0.0)
+    aff(A("THR", 0, 4), NF(4), 16.0, S)
+    move(A("XF", 0, 64), NF(64))
+    move(A("IOT", 0, 80), NF(80))
+    aff(A("ZQ", 0, 144), A("Z4", 0, 144), 4.0)
+    fill("C15", 0, 256, MID)
+    for w in WK[1:] + (-1,):
+        aff(ident(w), ident(1), float(w))
+    act(LAST, S, 1.0, -14.0, ACT.Relu)
+    aff(A("V", 0, 128), BM, LAST)
+    aff(A("NV", 0, 128), A("V", 0, 128), -1.0)
+    for name in ("L4P", "L4", "NE"):
+        fill(name, 1024, 1088, 0.0)
+    aff(col(10), S, 1.0, float(DUM))
+    aff(A("G4", 1024, 1088), NF(64), 16.0, col(10))
+    aff(idents(9, 21), idents(3, 7), 3.0)
+    aff(idents(25, 35), idents(5, 7), 5.0)
+    aff(ident(49), ident(7), 7.0)
+    quarter(2)
+    tt(A("NE", 1088, 1536), A("MO", 1024, 1472), A("MI", 1024, 1472), ALU.not_equal)
     count3(1152)
     count_up(2, 1408)
     count_up(3, 1088)
     count_up(4, 1472)
     count_up(0, 1472)
-    bulk_sum(0)
-    tt(A("NE", 0, 512), A("MO", 0, 512), A("MI", 0, 512), ALU.not_equal)
+    for h in range(2):
+        tt(A("NE", 512 * h, 512 * h + 512), A("MO", 512 * h, 512 * h + 512), A("MI", 512 * h, 512 * h + 512), ALU.not_equal)
+        mm(A("P4", 384 + 32 * h, 416 + 32 * h), [(E(p), A("NE", 512 * h + p, 512 * h + 512, 16)) for p in range(16)])
+    quarter(3)
     scan(A("F5", 0, 320), A("RS5", 0, 320), A("P3", 0, 320), ALU.max, ALU.min)
-    count4_half(0)
-    tt(A("NE", 512, 1024), A("MO", 512, 1024), A("MI", 512, 1024), ALU.not_equal)
-    count4_half(1)
-    leaves(3072, LA)
-    tt(A("FB", 0, 64), A("P3", 384, 448), A("F5", 4, 320, 5), ALU.min)
-
-    def hook0(i):
-        if i == 0:
-            bulk_sum(1)
-            act(A("LV", LB, 4096), IND(DWIN, A("LP", LB // 16, 256)))
-            bulk_q(0, A("P1", 0, 512))
-        else:
-            leaves(LA, LB)
-            bulk_sum(2, True, False)
-            bulk_fix(0)
-            bulk_fix(1)
-            bulk_q(2, SHUT[2])
-            bulk_sum(3, True, False)
-            bulk_q(3, SHUT[3])
-            bulk_sum(2, False, True)
-            bulk_fix(2)
-            bulk_sum(3, False, True)
-            bulk_fix(3)
-
-    candidates(0, A("FB", 0, 68), hook0)
-    act(A("L4", 0, 1024), A("L4S", 0, 1024))
-    send(1, A("L4P", 0, 512), A("L4S", 0, 512))
-    send(1, A("IDP", 0, 4), A("IDS0", 0, 4))
-    send(1, A("L4P", 512, 1024), A("L4S", 512, 1024))
-    for w in SC[11:]:
-        act(ident(w), ident(1), scale=float(w))
-    g4 = open4(0)
-    places(0)
-    put_l4(0, 512, "L4S")
-    settle(0, g4)
+    leaves(LEAVES[:EARLY])
+    tt(A("FB", 0, 64), A("P4", 384, 448), A("F5", 4, 320, 5), ALU.min)
+    candidates(0, A("FB", 0, 68))
+    leaves(LEAVES[EARLY:])
+    if ALL1:
+        move(A("A0", 0, 256), IND(LWIN, A("CL0", 0, 16)))
+        move(A("B0", 0, 256), IND(A("LVP", 0, 4352), A("CL0", 0, 16)))
+        settle(0)
+        for h in range(4):
+            level4(h)
+    else:
+        exchange(0)
+        for h in range(4):
+            level4(h)
+        settle(0)
     send(1, A("PAP", 0, 64), PA[0])
+    ids(0)
+    send(1, A("IDP", 0, 4), A("IDS0", 0, 4))
+    for lo in (0, 512):
+        move(A("L4", lo, lo + 512), A("L4S", lo, lo + 512))
     own4(0)
+    aff(idents(-3, -9), idents(3, 9), -1.0)
+    aff(idents(-15, -25), idents(15, 25), -1.0)
+    aff(idents(-35, -49), idents(35, 49), -1.0)
+    for h, bank in enumerate(("P2", "P1")):
+        mm(A(bank, 0, 512), [(ident(1), A("L4S", 512 * h, 512 * h + 512)), (ident(-1), A("L4P", 512 * h, 512 * h + 512))])
+        act(A("NE", 512 * h, 512 * h + 512), A(bank, 0, 512), func=ACT.Abs)
     g2 = sum2("L4", 1, True, False)
-    g3 = sum3("L4", 1, True, False)
-    places_kids(0)
-    tt(IND(LWIN, A("CL0", 0, 16)), A("A0", 0, 256), A("MD0", 0, 256), ALU.add)
-    copy(A("OWN", 0, 64), IND(A("L4", 0, 1088), A("IDP", 0, 4)))
-    tt(A("NE", 0, 512), A("L4", 0, 512), A("L4P", 0, 512), ALU.not_equal)
-    tt(A("NE", 512, 1024), A("L4", 512, 1024), A("L4P", 512, 1024), ALU.not_equal)
+    g3 = mm(l3, [mid] + terms3("L4", 1), stop=False)
+    move(A("OTH", 0, 64), IND(A("L4P", 0, 1088), A("IDS0", 0, 4)))
+    move(A("OWN", 0, 64), IND(A("L4", 0, 1088), A("IDP", 0, 4)))
     copy(IND(A("L4P", 0, 1088), A("IDP", 0, 4)), A("PAP", 0, 64))
     sum2("L4P", -1, False, True, g2)
-    sum3("L4P", -1, False, True, g3)
+    mm(l3, terms3("L4P", -1), False, True, g3)
+    tt(A("NEO", 0, 64), A("OTH", 0, 64), PA[0], ALU.not_equal)
+    copy(IND(A("NE", 0, 1088), A("IDS0", 0, 4)), A("NEO", 0, 64))
     tt(A("NEP", 0, 64), A("OWN", 0, 64), A("PAP", 0, 64), ALU.not_equal)
     copy(IND(A("NE", 0, 1088), A("IDP", 0, 4)), A("NEP", 0, 64))
-    count4()
-    act(A("MU", 0, 256), l3, bias=BIG)
-    act(A("MU", 256, 512), A("MU", 0, 256), bias=-BIG)
+    mm(A("P3", 0, 320, 5), [(E(p), A("NE", p, 1024, 16)) for p in range(16)])
+    fill("RSZ", 0, 128, 1.0)
+    fill("RSZ", 0, 64, 0.0, 4)
+    fill("RSZ", 64, 128, 0.0, 16)
+    fill("F5", 320, 340, 1.0)
+    iota(A("WP", 0, 64), [[0, 16], [2, 4]], 1, 0, True)
+    iota(A("WP", 128, 192), [[0, 4], [2, 4], [0, 4]], 1, 0, True)
+    tt(A("WP", 64, 128), A("WP", 0, 64), A("WP", 128, 192), ALU.mult)
+    ts(A("OC", 0, 4), NF(4), 4.0, 19.0, ALU.mult, ALU.add)
+    ts(col(11), S, K4, 0.25, ALU.subtract, ALU.mult)
+    ts(A("OC", 4, 8), NF(4), 4.0, col(11), ALU.mult, ALU.add)
+    act(A("M3", 0, 256), l3)
     low_sums()
-    low = IND(A("SCN", 0, 128), A("OC", 0, 8))
+    rnd(A("MM", 64, 96), A("SCN", 3, 128, 4))
+    tt(A("N32", 0, 32), A("SCN", 3, 128, 4), A("MM", 64, 96), ALU.not_equal)
+    move(A("NE", 1088, 1216), IND(A("N32", 0, 32), A("OC", 0, 8)))
     tt(A("NE", 1472, 1536), l2, A("MM", 0, 64), ALU.not_equal)
+    tt(A("NE", 1216, 1472), l3, A("M3", 0, 256), ALU.not_equal)
     count_up(2, 1472)
-    rnd(A("MM", 64, 192), low)
-    tt(A("NE", 1088, 1216), low, A("MM", 64, 192), ALU.not_equal)
+    count3(1216)
     count_up(3, 1152)
     count_up(4, 1088)
-    places_out(0, 0)
-    tt(A("NE", 1216, 1472), l3, A("MU", 256, 512), ALU.not_equal)
-    count3(1216)
-    put_l4(512, 576)
     scan(A("F5", 0, 320), A("RS5", 0, 320), A("P3", 0, 320), ALU.max, ALU.min)
-    po = [None]
-
-    def hook1(i):
-        if i == 0:
-            po[0] = places_own(0, 0, 8)
-        else:
-            put_l4(576, 704)
-            places_own(0, 8, 16, po[0])
-
-    candidates(1, A("F5", 4, 340, 5), hook1)
-    g4 = open4(1)
-    g2 = mm(l2, [(ident(1), A("CK", 0, 64))], stop=False)
+    candidates(1, A("F5", 4, 340, 5))
+    for lo in (0, 128):
+        tt(IND(LWIN, A("CL0", lo // 16, lo // 16 + 8)), A("A0", lo, lo + 128), A("MD0", lo, lo + 128), ALU.add)
+    exchange(1)
+    ts(A("COL", 16, 20), NF(4), 4.0, S, ALU.mult, ALU.is_equal)
+    for q in range(4):
+        aff(A("SK", 128 * q, 128 * q + 128), BM, col(16 + q))
+    places(0)
+    for h, bank in enumerate(("P5", "P6")):
+        for k in range(4):
+            mm(A(bank, k, 512, 4), [(A("SK", 128 * k, 128 * k + 128), A("G", 96 + 128 * h, 224 + 128 * h))])
+        act(A("OP4", 512 * h, 512 * h + 512), A(bank, 0, 512))
+    settle(1)
+    ids(1)
+    put_leaves(0, 128)
+    for lo, hi in zip(puts, puts[1:]):
+        i = copy(IND(DWIN, A("OFF", lo // 16, hi // 16)), A("L4", lo, hi))
+        apart(0, i)
+        ops[i]["piece"] = lo
+    fill("CK", 0, 64, 0.5)
+    fill("CK", 64, 128, -32640.0)
+    g2 = mm(l2, [(ident(1), A("CK", 0, 64)), (ident(1), A("CK", 64, 128))], stop=False)
+    g3 = mm(l3, [mid], stop=False)
     places(1)
-    put_leaves(0)
-    places_out(0, 1)
-    places_kids(1)
-    places_own(1, 0, 16)
-    tt(IND(DWIN, PL[0]), PA[0], A("C127", 0, 64), ALU.add)
-    put_l4(704, 1024)
-    places_out(1, 0)
-    settle(1, g4)
+    g4 = mm(A("P2", 0, 256), [mid], stop=False)
     own4(1)
-    sum3("L4", 1, True, True)
     sum2("L4", 1, False, True, g2)
-    mod3()
-    put_leaves(1)
-    places_out(1, 1)
+    mm(l3, terms3("L4", 1), False, True, g3)
+    act(A("T3", 0, 256), l3, bias=-127.5)
+    g4 = mm(A("P2", 0, 256), terms3("L4", 1), False, False, g4)
+    mm(A("P2", 0, 256), [(ident(-1), A("T3", 0, 256))], start=False, after=g4)
+    act(A("UF", 0, 256), A("P2", 0, 256))
+    fill("KA", 0, 16, 120.5)
+    fill("KA", 16, 32, 0.5)
+    fill("CADD", 0, 96, 127.5)
+    fill("CADD", 96, 160, 0.0)
+    ts(A("OC", 8, 9), S, 4.0, 3.0, ALU.mult, ALU.add)
+    ts(col(12), S, 3.0, 16.0, ALU.min, ALU.mult)
+    ts(A("OC", 9, 10), col(12), 79.0, None, ALU.add)
+    aff(col(13), S, 15.0, float(DUM + 2))
+    ts(col(14), S, 4.0, col(13), ALU.is_ge, ALU.mult)
+    ts(A("OFF", 89, 90), col(14), S, None, ALU.add)
+    put_leaves(1, 256)
     low_sums()
-    tt(A("UF", 256, 320), l2, A("MM", 0, 64), ALU.subtract)
     tt(A("XG", 0, 32), IND(A("SCN", 0, 128), A("OC", 8, 10)), A("KA", 0, 32), ALU.add)
+    tt(A("UF", 256, 320), l2, A("MM", 0, 64), ALU.subtract)
     rnd(A("MM", 64, 96), A("XG", 0, 32))
     tt(A("UF", 320, 352), A("XG", 0, 32), A("MM", 64, 96), ALU.subtract)
-    tt(IND(DWIN, A("OFF", 68, 94)), A("UF", 0, 416), A("C127", 0, 416), ALU.add)
-    dma(T["y"][:, 0:P], T["D"][:, 0:P], [], [A("D", 0, P)])
+    aff(A("OP4", 1024, 1088), NF(64), 16.0, float(DUM))
+    aff(A("Z1", 0, 144), A("Z", 0, 144), LAST)
+    move(A("XO", 0, 64), IND(A("OP4", 0, 1088), A("IDS1", 0, 4)))
+    move(A("XH", 0, 64), A("XO", 0, 64))
+    tt(A("XL", 0, 64), A("XO", 0, 64), A("XH", 0, 64), ALU.subtract)
+    in_parts(A("P1", 0, 4), [(E(p, "Z1"), A(x, p, 64, 16)) for x in ("XH", "XL") for p in range(16)], 8)
+    copy(A("OFF", 90, 94), A("P1", 0, 4))
+    apart(1, tt(IND(DWIN, A("OFF", 84, 94)), A("UF", 256, 416), A("CADD", 0, 160), ALU.add))
+    apart(1, copy(IND(DWIN, A("OFF", 68, 84)), A("UF", 0, 256)))
+    dma([(T["y"][:, 0:P], T["D"][:, 0:P])], [], [A("D", 0, P)], 256 * P)
     return ops
 
 
@@ -509,41 +529,104 @@ def _meet(a, b):
     return a[0] == b[0] and a[1] < b[2] and b[1] < a[2]
 
 
+def _banks(x):
+    return set(a[0] for a in x["w"] + x["r"] if a[0][0] == "P" and a[0][1:].isdigit())
+
+
+def _clash(x, y, free=True):
+    apart = free and x.get("apart") is not None and x.get("apart") == y.get("apart")
+    return (any(_meet(a, b) for a in x["r"] + ([] if apart else x["w"]) for b in y["w"])
+            or any(_meet(a, b) for a in x["w"] for b in y["r"]))
+
+
+def _line(x, y):
+    return x["kind"] == y["kind"] == "dma" and list(x["ways"]) == list(y["ways"])
+
+
 def _depends(x, y):
-    for a in x["w"] + x["r"]:
-        if a[0][0] == "P" and a[0][1:].isdigit():
-            if x["q"] != y["q"] and any(b[0] == a[0] for b in y["w"] + y["r"]):
-                return True
+    if x["q"] != y["q"] and _banks(x) & _banks(y):
+        return True
     if x["q"] == "tensor" and y["q"] == "tensor":
         return False
-    return (any(_meet(a, b) for a in x["r"] + x["w"] for b in y["w"])
-            or any(_meet(a, b) for a in x["w"] for b in y["r"]))
+    return _clash(x, y, False)
+
+
+def _after(x, y, qx, qy, took):
+    if _line(x, y):
+        return 0.05
+    if x["kind"] == "arr":
+        return took
+    if qx != qy or y["kind"] != "c":
+        return took + WAKE
+    return took + (TURN if qx != "tensor" and _clash(x, y) else 0.0)
+
+
+def _arrange(ops):
+    n = len(ops)
+    busy, start, end, queue, lanes = {}, [0.0] * n, [0.0] * n, [None] * n, {}
+    for i, x in enumerate(ops):
+        pre = [j for j in range(i) if _clash(x, ops[j]) or _banks(x) & _banks(ops[j]) or x.get("of") == j
+               or _line(x, ops[j])]
+        best = None
+        for q, (_, t) in x["ways"].items():
+            at = max([0.0] + [start[j] + _after(x, ops[j], q, queue[j], end[j] - start[j]) for j in pre])
+            for a, b in busy.get(q, []):
+                if at + t + MARGIN <= a:
+                    break
+                at = max(at, b)
+            if best is None or at + t - SPARE < best[0] + best[1]:
+                best = (at, t, q)
+        start[i], t, queue[i] = best
+        end[i] = start[i] + t
+        if queue[i] is not None:
+            busy[queue[i]] = sorted(busy.get(queue[i], []) + [(start[i], end[i])])
+        if "lane" in x:
+            end[i] = max(start[i] + x["lag"], lanes.get(x["lane"], 0.0)) + x["size"]
+            lanes[x["lane"]] = end[i]
+    return sorted(range(n), key=lambda i: (start[i], i)), queue
+
+
+_PLAN = {}
 
 
 def rank_program(g, core, T, topo):
     if T.rank_of(core) is None:
         return
-    ops = build(core, T, topo)
+    if not _PLAN:
+        ops = build(core, T, topo, range(0, 1025, PUT))
+        order, queue = _arrange(ops)
+        line = [ops[i].get("piece") for i in order if queue[i] == "vector"]
+        _PLAN["puts"] = [b for a, b in zip([None] + line, line) if b is not None and a != b - PUT] + [1024]
+        _PLAN["puts"].sort()
+        _PLAN["order"], _PLAN["queue"] = _arrange(build(core, T, topo, _PLAN["puts"]))
+    ops = build(core, T, topo, _PLAN["puts"])
+    for x, q in zip(ops, _PLAN["queue"]):
+        x["q"], x["fn"] = q, x["ways"][q][0]
+    where = {j: i for i, j in enumerate(_PLAN["order"])}
+    ops = [ops[j] for j in _PLAN["order"]]
     eng = {"g": g, "vector": g.vector, "scalar": g.scalar, "tensor": g.tensor, "sync": g.sync}
-    known = {q: set() for q in eng}
-    before = []
-    waits = []
-    for i, x in enumerate(ops):
-        if x["kind"] == "arr":
-            before.append(set())
-            waits.append([])
-            continue
-        k = known[x["q"]]
-        need = [j for j in range(i) if j not in k and _depends(x, ops[j])]
-        implied = set()
-        for j in need:
-            implied |= before[j]
-            if ops[j].get("after") is not None:
-                implied.add(ops[j]["after"])
-        need = [j for j in need if j not in implied]
-        k |= implied | set(need)
-        waits.append(need)
-        before.append(set(k))
+    if "waits" not in _PLAN:
+        known = {q: set() for q in eng}
+        before = []
+        waits = []
+        for i, x in enumerate(ops):
+            if x["kind"] == "arr":
+                before.append(set())
+                waits.append([])
+                continue
+            k = known[x["q"]]
+            need = [j for j in range(i) if j not in k and _depends(x, ops[j])]
+            implied = set()
+            for j in need:
+                implied |= before[j]
+                if ops[j].get("after") is not None:
+                    implied.add(where[ops[j]["after"]])
+            need = [j for j in need if j not in implied]
+            k |= implied | set(need)
+            waits.append(need)
+            before.append(set(k))
+        _PLAN["waits"], _PLAN["before"] = waits, before
+    waits, before = _PLAN["waits"], _PLAN["before"]
     waited = set(j for w in waits for j in w)
     tail = [i for i, x in enumerate(ops) if x["kind"] != "c" and i not in waited]
     waiters = {}
@@ -577,7 +660,8 @@ def rank_program(g, core, T, topo):
             done[x["q"]].add((s, n))
         r = x["fn"](e)
         if x["kind"] == "dma":
-            r.then_inc(T.sem[x["sem"]], 16)
+            for one in r:
+                one.then_inc(T.sem[x["sem"]], 16)
         elif x["kind"] == "c" and i in waited:
             r.then_inc(T.sem[x["sem"]], 1)
     for i in tail:

@@ -1,39 +1,49 @@
 from concourse.mybir import AluOpType as ALU, ActivationFunctionType as ACT
 
 P = 5460
-DUM = 5464
-DW = 6496
+DUM = 5504
+DW = 6656
 MEETS = (1, 6)
 BIG = 3221225472.0
 MID = 49152.0
 WK = (1, 3, 5, 7)
-PR = (1, 3, 5, 7, 9, 15, 21, 25, 35, 49)
-SC = PR + tuple(-w for w in PR)
-SPLIT = 2816
-WR = 1664
-WV = (3104, 4256)
-WG = (4864, P)
-LEAVES = ((3072, 3328, "V"), (3328, 3584, "V"), (0, 1024, "S"), (0, 1024, "send"), (1024, 2048, "S"),
-          (1024, 2048, "send"), (2048, 3072, "S"), (2048, 3072, "send"), (3584, 3840, ""), (3840, 4096, ""),
-          (3072, 4096, "send"))
-EARLY = 1
+SC = (1, 3, 5, 7, 9, 15, 21, 25, 35, 49, -1, 16)
+WR = 2048
+WV = (3456, 4416)
+WG = (P,)
+STEPS = (("mo", 0, 512, "s"), ("mi", 0, 512), ("g4", 0), ("o4",), ("mo", 512, 1024, "s"), ("mi", 512, 1024),
+         ("g4", 1), ("g4", 2), ("lp", 0), ("g4", 3), ("lp", 1),
+         ("lv", 0, 512, "s"), ("out", 0, 512), ("lv", 1024, 1280, "v"), ("lp", 2), ("lv", 512, 1024, "s"),
+         ("lv", 1280, 1536, "v"), ("out", 512, 1536), ("lp", 3), ("lv", 1536, 1792, "v"), ("lv", 1792, 2560, "s"),
+         ("out", 1536, 2560), ("up",), ("ne", 0, 512), ("ne", 512, 1024), ("f5",), ("lv", 2560, 3328, "s"),
+         ("out", 2560, 3328), ("lv", 3328, 3840, "s"), ("lv", 3840, 4096, "v"), ("out", 3328, 4096), ("ls",),
+         ("l4", 0, "s"), ("l4", 1, "s"), ("far", 0, 512), ("l4", 2, "s"), ("l4", 3, "s"), ("far", 512, 1024),
+         ("ab",), ("id",))
+ALL1 = True
+if not ALL1:
+    STEPS = STEPS[:11] + (
+        ("lv", 0, 1024, "s"), ("lv", 1024, 1280, "v"), ("lp", 2), ("up",), ("lp", 3), ("lv", 1536, 2560, "s"),
+        ("lv", 1280, 1536, "v"), ("ne", 0, 512), ("ne", 512, 1024), ("f5",), ("lv", 2560, 3712, "s"),
+        ("lv", 3840, 4096, "v"), ("ls",), ("lv", 3712, 3840, "v"), ("ab",), ("l4", 0, "s"), ("l4", 1, "s"),
+        ("far", 0, 512), ("l4", 2, "s"), ("l4", 3, "s"), ("far", 512, 1024), ("id",))
+DFV = 512
+OVER, LEAST, REST = 0.05, 64, 0.4
 PUT = 128
-ALL1 = False
 
 
 def _sb(n, t):
     return ("sbuf", [128, n], t)
 
 
-_BF = dict(D=DW, Z=144, Z4=144, ZQ=144, Z1=144, B=128, U=128, V=128, NV=128, N4=144, N16=128, CB=16,
-           IDM=128 * len(SC), MO=1472, MI=1472, ONE=256, IOT=80, CF=64, NE=1536, FB=80, OWN=64, OTH=64, NEO=64,
-           NEP=64, LV=4352, LVP=4352, L4=1088, L4S=1024, L4P=1088, T4=1024, T3=256, F5=352, RS5=320, RS68=272, CADD=160,
-           CK=128, C15=256, LE4=272, S16=272, LE=64, A0=256, A1=256, B0=256, B1=256, GT=256, MD0=256, MD1=256, PA0=64,
-           PAP=64, UF=416, XH=64, XL=64, M3=256, N32=32, M4=64)
-_F32 = dict(COL=24, NF=256, ZR=144, G=352, G4=1088, RSZ=128, KA=32, WP=192, THR=8, XF=64, C=72, CW=72,
-            X0=64, X1=64, XO=64, MM=192, ZS=128, SCN=128, XG=32, SK=512, OP4=1088)
-_I32 = dict(W=P, K0=8)
-_U16 = dict(OFF=96, LP=256, OC=16, CI=16, IDS0=16, IDS1=16, IDP=16, CP0=16, CP1=16, CL0=16, CL1=16)
+_BF = dict(D=DW, Z=144, Z4=576, BM=128, ZQ=144, ZI=144, B=128, U=256, V=128, NV=128, N4=144, N16=128, CB=16,
+           IDM=128 * len(SC), MO=1472, MI=1472, ONE=320, IOT=80, CF=64, NE=1536, FB=80, OWN=64,
+           LV=4352, LVP=4352, L4=1088, L4P=1024, DF=1088, T4=1024, T3=256, F5=352, RS5=320, RS69=276, STEP=276,
+           NB=128, C15=256, LE4=276, S16=276, LE=64, A0=256, A1=256, B0=256, B1=256, GT=256, MD0=256, MD1=256, PA0=64,
+           PAP=64, UF=416, YH=64, YL=64, PL=160, M3=256, N32=32, M4=64)
+_F32 = dict(COL=24, NF=144, ZR=144, G=352, G4=1088, RSZ=128, FLOOR=276, WP=192, THR=8, XF=64, CW=72,
+            X0=64, X1=64, MM=192, ZS=128, SCN=128, XG=32, SF=16)
+_I32 = dict(W=P, K0=8, IU=160, IV=160)
+_U16 = dict(OFF=104, LP=256, OC=4, CI0=4, CI1=4, IDS0=4, IDS1=4, IDP=4, CP0=16, CP1=16, CL0=16, CL1=16)
 SCRATCH = {}
 for _d, _t in ((_BF, "bfloat16"), (_F32, "float32"), (_I32, "int32"), (_U16, "uint16")):
     for _k in _d:
@@ -44,20 +54,23 @@ NPOOL = 90
 NMSG = 24
 SEMAPHORES = (["s%d" % i for i in range(NPOOL)] + ["d%d" % i for i in range(12)]
               + ["l%d" % i for i in range(NMSG)] + ["r%d" % i for i in range(NMSG)])
-CYC, TCYC = 0.83e-3, 0.4e-3
+CYC, TCYC = 0.87e-3, 0.42e-3
 WAKE, TURN = 0.16, 0.14
-GATHER, SCATTER = 1.4, 2.75
+GATHER, SCATTER = 1.45, 3.0
 SMALL, SSMALL = 0.035, 0.16
-LOCAL, NEAR, FAR = 540e3, 270e3, 190e3
+LOCAL, NEAR, FAR = 540e3, 240e3, 190e3
 LAG, RLAG = 1.3, 1.45
 MARGIN = 0.0
 SPARE = 0.2
+LATE = 2.0
 
 
 def build(core, T, topo, puts=()):
     rank = T.rank_of(core)
     peer = [T.cores[rank ^ m] for m in MEETS]
     ops = []
+    gate = [None]
+    mark = {}
 
     def A(name, lo, hi, step=1):
         ap = T[name][:, lo:hi] if step == 1 else T[name][:, lo:hi:step]
@@ -69,10 +82,11 @@ def build(core, T, topo, puts=()):
     def col(j):
         return A("COL", j, j + 1)
 
-    def add(ways, outs, ins, kind="c", **kw):
+    def add(ways, outs, ins, kind="c", on="", **kw):
+        ways = {q: w for q, w in ways.items() if not on or q[0] in on}
         w = [r for o in outs for r in o[1]]
         rd = [r for o in ins for r in o[1]] + [r for o in list(outs) + list(ins) for r in o[2]]
-        ops.append(dict(ways=ways, q=list(ways)[0], w=w, r=rd, kind=kind, **kw))
+        ops.append(dict(ways=ways, q=list(ways)[0], w=w, r=rd, kind=kind, since=gate[0], **kw))
         return len(ops) - 1
 
     def val(s):
@@ -80,6 +94,9 @@ def build(core, T, topo, puts=()):
 
     def aps(*s):
         return [x for x in s if isinstance(x, tuple)]
+
+    def psum(x):
+        return SCRATCH[x[1][0][0]][0] == "psum"
 
     def vtime(o, ins, both=1.0):
         if o[4]:
@@ -96,7 +113,7 @@ def build(core, T, topo, puts=()):
         return add({"vector": (lambda e: e.tensor_copy(o[0], i[0]), vtime(o, [i]))}, [o], [i])
 
     def tt(o, a, b, op):
-        both = 1.0 if a[1][0][0][0] == "P" and a[1][0][0][1:].isdigit() else 2.0
+        both = 1.0 if psum(a) or psum(b) else 2.0
         return add({"vector": (lambda e: e.tensor_tensor(o[0], a[0], b[0], op), vtime(o, [a, b], both))}, [o], [a, b])
 
     def ts(o, a, s1, s2, op0, op1=None):
@@ -114,33 +131,44 @@ def build(core, T, topo, puts=()):
         return add({"scalar": (lambda e: e.activation(o[0], i[0], func, bias=val(bias), scale=val(scale)),
                                stime(o, i))}, [o], [i] + aps(scale, bias))
 
-    def aff(o, i, scale=1.0, bias=0.0):
+    def aff(o, i, scale=1.0, bias=0.0, on="", spare=None):
         return add({"vector": (lambda e: e.tensor_scalar(o[0], i[0], val(scale), val(bias), ALU.mult, ALU.add),
                                vtime(o, [i])),
                     "scalar": (lambda e: e.activation(o[0], i[0], ACT.Identity, bias=val(bias), scale=val(scale)),
-                               stime(o, i))}, [o], [i] + aps(scale, bias))
+                               stime(o, i))}, [o], [i] + aps(scale, bias), on=on, spare=spare)
 
-    def move(o, i):
+    def const(o, i, scale=1.0, bias=0.0, on=""):
+        return aff(o, i, scale, bias, on, LATE)
+
+    def move(o, i, on=""):
         return add({"vector": (lambda e: e.tensor_copy(o[0], i[0]), vtime(o, [i])),
-                    "scalar": (lambda e: e.activation(o[0], i[0], ACT.Identity), stime(o, i))}, [o], [i])
+                    "scalar": (lambda e: e.activation(o[0], i[0], ACT.Identity), stime(o, i))}, [o], [i], on=on)
+
+    def nonzero(o, i, on=""):
+        return add({"vector": (lambda e: e.tensor_scalar(o[0], i[0], 0.0, None, ALU.not_equal), vtime(o, [i])),
+                    "scalar": (lambda e: e.activation(o[0], i[0], ACT.Abs), stime(o, i))}, [o], [i], on=on)
 
     def memset(o, c):
         return add({"vector": (lambda e: e.memset(o[0], c), vtime(o, []))}, [o], [])
 
-    def fill(name, lo, hi, c, step=1):
-        for a in range(lo, hi, 256 * step):
-            o = A(name, a, min(hi, a + 256 * step), step)
-            i = A("ONE", 0, o[3])
-            add({"vector": (lambda e, o=o: e.memset(o[0], c), vtime(o, [])),
-                 "scalar": (lambda e, o=o, i=i: e.activation(o[0], i[0], ACT.Identity, bias=c, scale=0.0),
-                            stime(o, i))}, [o], [i])
+    def fill(name, lo, hi, c, on=""):
+        o, i = A(name, lo, hi), A("ONE", 0, hi - lo)
+        ways = {"vector": (lambda e: e.memset(o[0], c), vtime(o, [])),
+                "scalar": (lambda e: e.activation(o[0], i[0], ACT.Identity, bias=c, scale=0.0), stime(o, i))}
+        if c == int(c):
+            ways["g"] = (lambda e: e.iota(o[0], [[0, o[3]]], int(c), 0, allow_small_or_imprecise_dtypes=True),
+                         0.13 + 2 * o[3] * CYC)
+        add(ways, [o], [i], on=on, spare=LATE)
 
-    def iota(o, pat, base, cm, fl=False):
+    def iota(o, pat, base, cm, fl=True):
         if fl:
             fn = lambda e: e.iota(o[0], pat, base, cm, allow_small_or_imprecise_dtypes=True)
         else:
             fn = lambda e: e.iota(o[0], pat, base, cm)
         return add({"g": (fn, 0.13 + 2 * o[3] * CYC)}, [o], [])
+
+    def pick(o, i, pat, op, other, cm=0):
+        return add({"g": (lambda e: e.affine_select(o[0], i[0], pat, op, other, 0, cm), 0.17 + 2 * o[3] * CYC)}, [o], [i])
 
     def mm(o, terms, start=True, stop=True, after=None):
         def fn(e):
@@ -201,12 +229,13 @@ def build(core, T, topo, puts=()):
         for a in range(0, len(terms), n):
             last = mm(o, terms[a:a + n], a == 0, a + n >= len(terms), last)
 
+    DG = A("D", 0, P)
     DWIN = A("D", 0, DW)
     WWIN = A("W", 0, P)
     LWIN = A("LV", 0, 4352)
-    PA = (A("PA0", 0, 64), A("UF", 352, 416))
+    L4W = A("L4", 0, 1088)
+    PA = (A("PA0", 0, 64), A("IV", 96, 160))
     BM = A("B", 0, 128)
-    ONE = A("ONE", 0, 256)
     G16, G4 = A("CB", 0, 1), A("CB", 8, 9)
     S, K4, LAST = col(5), col(6), col(9)
     l2, l3 = A("P0", 0, 64), A("P7", 0, 256)
@@ -215,40 +244,37 @@ def build(core, T, topo, puts=()):
     def NF(n):
         return A("NF", 0, n)
 
-    def digests(lo, hi, end):
-        dma([(T["D"][:, lo:hi], T["dg"][:, lo:hi])], [A("D", lo, end)], [], 256 * (hi - lo))
+    def ONE(n):
+        return A("ONE", 0, n)
+
+    def children(o, src, lo, n):
+        return mm(o, [(R(q), A(src, lo + q, lo + n, 4)) for q in range(4)])
 
     def level(go, n, src, dst):
         copy(A("G", go, go + n), IND(WWIN, A("OFF", src, src + n // 16)))
-        mm(A("P0", 0, n // 4), [(R(q), A("G", go + q, go + n, 4)) for q in range(4)])
+        children(A("P0", 0, n // 4), "G", go, n)
         copy(A("OFF", dst, dst + n // 4), A("P0", 0, n // 4))
 
     def quarter(h):
         bank = A(("P0", "P5", "P6", "P7")[h], 0, 64)
         copy(A("G4", 256 * h, 256 * h + 256), IND(WWIN, A("OFF", 16 * h, 16 * h + 16)))
-        mm(bank, [(R(q), A("G4", 256 * h + q, 256 * h + 256, 4)) for q in range(4)])
-        copy(A("LP", 64 * h, 64 * h + 64), bank)
+        children(bank, "G4", 256 * h, 256)
 
-    def stored4(h):
-        for lo in (512 * h, 512 * h + 256):
-            (copy if lo == 256 else act)(A("MO", lo, lo + 256), IND(DWIN, A("OFF", lo // 16, lo // 16 + 16)))
-        send(0, A("MI", 512 * h, 512 * h + 512), A("MO", 512 * h, 512 * h + 512))
+    def stored4(lo, hi, on):
+        move(A("MO", lo, hi), IND(DG, A("OFF", lo // 16, hi // 16)), on)
 
-    def leaves(pieces):
-        for lo, hi, eng in pieces:
-            if eng == "send":
-                if ALL1:
-                    send(0, A("LVP", lo, hi), A("LV", lo, hi))
-            else:
-                {"V": copy, "S": act, "": move}[eng](A("LV", lo, hi), IND(DWIN, A("LP", lo // 16, hi // 16)))
+    def leaves(lo, hi, on=""):
+        move(A("LV", lo, hi), IND(DG, A("LP", lo // 16, hi // 16)), on)
 
-    def level4(h):
+    def across(m, dst, src, lo, hi):
+        send(m, A(dst, lo, hi), A(src, lo, hi))
+
+    def level4(h, on=""):
         s4, t4 = A(("P0", "P7", "P2", "P1")[h], 0, 256), A("T4", 256 * h, 256 * h + 256)
-        mm(s4, [mid] + [(ident(WK[k]), A("LV", 1024 * h + k, 1024 * h + 1024, 4)) for k in range(4)])
-        aff(t4, s4, 1.0, -127.5)
-        tt(A("L4S", 256 * h, 256 * h + 256), s4, t4, ALU.subtract)
-        if h % 2:
-            send(1, A("L4P", 256 * h - 256, 256 * h + 256), A("L4S", 256 * h - 256, 256 * h + 256))
+        grp = mm(s4, [mid], stop=False)
+        mm(s4, [(ident(WK[k]), A("LV", 1024 * h + k, 1024 * h + 1024, 4)) for k in range(4)], False, True, grp)
+        aff(t4, s4, 1.0, -127.5, on)
+        tt(A("L4", 256 * h, 256 * h + 256), s4, t4, ALU.subtract)
 
     def count3(l3):
         mm(A("P3", 1, 320, 5), [(slid("Z4", 12 - 4 * k), A("NE", l3 + k, l3 + 256, 4)) for k in range(4)])
@@ -257,271 +283,281 @@ def build(core, T, topo, puts=()):
         mm(A("P3", t, 320, 5), [(BM, A("NE", lo, lo + 64))])
 
     def candidates(m, f):
-        mm(A("P4", 0, 68), [(BM, f)])
-        mm(A("P4", 68, 136), [(A("U", 0, 128), f)])
-        scan(A("C", 0, 68), A("ONE", 0, 68), A("P4", 0, 68), ALU.mult, ALU.add)
+        ci = A("CI%d" % m, 0, 4)
+        grp = mm(A("P5", 0, 276), [(ident(1), A("STEP", 0, 276))], stop=False)
         for q in range(4):
-            ts(A("LE4", 68 * q, 68 * q + 68), A("C", 0, 68), A("THR", q, q + 1), 16.0, ALU.is_le, ALU.mult)
-        scan(A("S16", 0, 272), A("RS68", 0, 272), A("LE4", 0, 272), ALU.mult, ALU.add)
-        tt(A("CW", 0, 68), A("C", 0, 68), A("P4", 68, 136), ALU.subtract)
-        ts(A("CI", 0, 4), A("S16", 67, 272, 68), 1.0 / 16, None, ALU.mult)
-        tt(A("LE", 0, 64), IND(A("CW", 0, 68), A("CI", 0, 4)), A("XF", 0, 64), ALU.is_le)
-        move(A("CF", 0, 64), IND(A("IOT", 0, 80), A("CI", 0, 4)))
-        mm(A("P4", 256, 272), [(slid("ZQ", 12 - 4 * k), A(x, k, 64, 4)) for x in ("LE", "CF") for k in range(4)])
+            grp = mm(A("P5", 69 * q + 1, 69 * q + 69), [(A("NB", 0, 128), f(0, 68))], False, q == 3, grp)
+        grp = mm(A("P4", 0, 68), [(A("U", 0, 128), f(0, 68))], stop=False)
+        mm(A("P4", 1, 68), [(A("U", 128, 256), f(0, 67))], False, True, grp)
+        scan(A("LE4", 0, 276), A("P5", 0, 276), A("FLOOR", 0, 276), ALU.add, ALU.max)
+        scan(A("CW", 0, 68), ONE(68), A("P4", 0, 68), ALU.mult, ALU.add)
+        scan(A("S16", 0, 276), A("RS69", 0, 276), A("LE4", 0, 276), ALU.max, ALU.min)
+        copy(ci, A("S16", 68, 276, 69))
+        tt(A("LE", 0, 64), IND(A("CW", 0, 68), ci), A("XF", 0, 64), ALU.is_equal)
+        move(A("CF", 0, 64), IND(A("IOT", 0, 80), ci), "s")
+        mm(A("P4", 256, 272), [(slid(z, 12 - 4 * k), A(x, k, 64, 4)) for z, x in (("Z4", "CF"), ("ZQ", "LE")) for k in range(4)])
         ts(A("CL%d" % m, 0, 16), A("P4", 256, 272), K4, None, ALU.add)
 
     def ids(m):
         in_parts(A("P4", 320, 324),
-                 [(ident(1), A("S16", 67, 272, 68))] + [(E(p), A("LE", p, 64, 16)) for p in range(16)], 9)
+                 [(ident(16), A("S16", 68, 276, 69))] + [(E(p, "ZI"), A("LE", p, 64, 16)) for p in range(16)], 9)
         copy(A("IDS%d" % m, 0, 4), A("P4", 320, 324))
 
-    def exchange(m):
-        a, cl = "A%d" % m, "CL%d" % m
-        for lo in (0, 128):
-            move(A(a, lo, lo + 128), IND(LWIN, A(cl, lo // 16, lo // 16 + 8)))
-        send(m, A("B%d" % m, 0, 256), A(a, 0, 256))
-
     def places(m):
-        move(A("X%d" % m, 0, 64), IND(A("G4", 0, 1088), A("IDS%d" % m, 0, 4)))
-        mm(A("P2", 0, 16), [(R(q), A("X%d" % m, q, 64, 4)) for q in range(4)])
-        copy(A("CP%d" % m, 0, 16), A("P2", 0, 16))
+        move(A("X%d" % m, 0, 64), IND(A("G4", 0, 1088), A("IDS%d" % m, 0, 4)), "s")
+        children(A("P2", 0, 16), "X%d" % m, 0, 64)
+        mark["cp%d" % m] = copy(A("CP%d" % m, 0, 16), A("P2", 0, 16))
 
     def settle(m):
         a, b, pa, md = "A%d" % m, A("B%d" % m, 0, 256), PA[m], "MD%d" % m
         own = (mm(A("P5", 0, 256), [(A("NV", 0, 128), A(a, 0, 256))], stop=False),
-               mm(A("P3", 0, 256), [(ident(-1), A(a, 0, 256))], stop=False),
-               mm(A("P6", 0, 64), [(ident(1), A("C15", 0, 64))]
-                  + [(ident(WK[k]), A(a, k, 256, 4)) for k in range(4)], stop=False))
+               mm(A("P3", 0, 256), [(ident(-1), A(a, 0, 256))], stop=False))
+        sums = [(ident(1), A("C15", 0, 64))] + [(ident(WK[k]), A(a, k, 256, 4)) for k in range(4)]
+        if m or not ALL1:
+            g6 = mm(A("P6", 0, 64), sums, stop=False)
         mm(A("P5", 0, 256), [(A("V", 0, 128), b)], start=False, after=own[0])
         mm(A("P3", 0, 256), [(ident(1), b)], start=False, after=own[1])
-        ts(A("GT", 0, 256), A("P5", 0, 256), 0.0, None, ALU.is_gt)
-        tt(A(md, 0, 256), A("P3", 0, 256), A("GT", 0, 256), ALU.mult)
-        mm(A("P6", 0, 64), [(ident(WK[k]), A(md, k, 256, 4)) for k in range(4)], start=False, after=own[2])
-        ts(A("M4", 0, 64), A("P6", 0, 64), -127.5, None, ALU.add)
-        tt(pa, A("P6", 0, 64), A("M4", 0, 64), ALU.subtract)
+        if not m and ALL1:
+            g6 = mm(A("P6", 0, 64), sums, stop=False)
+        mark["gt%d" % m] = len(ops)
+        for lo in (0, 128):
+            ts(A("GT", lo, lo + 128), A("P5", lo, lo + 128), 0.0, None, ALU.is_gt)
+        for lo in (0, 128):
+            mark["md%d" % m] = tt(A(md, lo, lo + 128), A("P3", lo, lo + 128), A("GT", lo, lo + 128), ALU.mult)
+        mm(A("P6", 0, 64), [(ident(WK[k]), A(md, k, 256, 4)) for k in range(4)], start=False, after=g6)
+        if m:
+            copy(A("IU", 96, 160), A("P6", 0, 64))
+            ts(pa, A("IU", 96, 160), 255, None, ALU.bitwise_and)
+        else:
+            ts(A("M4", 0, 64), A("P6", 0, 64), -127.5, None, ALU.add)
+            tt(pa, A("P6", 0, 64), A("M4", 0, 64), ALU.subtract)
 
-    def sum2(src, sign, start, stop, after=None):
-        return mm(l2, [(ident(sign * WK[j // 4] * WK[j % 4]), A(src, j, 1024, 16)) for j in range(16)], start, stop, after)
+    def sum2(src, start=True, after=None):
+        return mm(l2, [(ident(WK[j // 4] * WK[j % 4]), A(src, j, 1024, 16)) for j in range(16)], start, True, after)
 
-    def terms3(src, sign):
-        return [(ident(sign * WK[k]), A(src, k, 1024, 4)) for k in range(4)]
+    def terms3(src):
+        return [(ident(WK[k]), A(src, k, 1024, 4)) for k in range(4)]
 
-    def low_sums():
+    def low_sums(between):
         tt(A("ZS", 0, 64), l2, A("WP", 0, 64), ALU.mult)
         tt(A("ZS", 64, 128), l2, A("WP", 64, 128), ALU.mult)
-        rnd(A("MM", 0, 64), l2)
+        between()
         scan(A("SCN", 0, 128), A("RSZ", 0, 128), A("ZS", 0, 128), ALU.mult, ALU.add)
 
     def own4(m):
-        copy(IND(A("L4", 0, 1088), A("IDS%d" % m, 0, 4)), PA[m])
-
-    def put_leaves(m, n):
-        for lo in range(0, 256, n):
-            apart(m, tt(IND(DWIN, A("CP%d" % m, lo // 16, (lo + n) // 16)), A("A%d" % m, lo, lo + n),
-                        A("MD%d" % m, lo, lo + n), ALU.add))
+        return copy(IND(L4W, A("IDS%d" % m, 0, 4)), PA[m])
 
     dma([(T["K0"][q:128:4, 0:4], T["kids"][:, 0:4]) for q in range(4)], [A("K0", 0, 4)], [], 2048, "scalar")
     dma([(T["D"][:, 0:16], T["dg"][:, 0:16])], [A("D", 0, 16)], [], 4096, "scalar")
     dma([(T["W"][q:128:4, 0:WR], T["kids"][:, 0:WR]) for q in range(4)], [A("W", 0, WR)], [], 512 * WR)
-    iota(A("COL", 0, 5), [[768, 5]], 0, 1, True)
-    memset(ONE, 1.0)
-    memset(A("W", WR, WV[0]), 0)
-    scan(NF(256), ONE, ONE, ALU.mult, ALU.add, -1.0)
-    memset(A("W", WV[0], WV[1]), 0)
+    iota(A("COL", 0, 5), [[768, 5]], 0, 1)
+    for lo, hi in zip((WR,) + WV, WV):
+        memset(A("W", lo, hi), 0)
     for lo, hi in zip(WV[-1:] + WG, WG):
-        iota(A("W", lo, hi), [[0, hi - lo]], 0, 0)
-    for lo, hi in ((WV[-1], WG[0]), (WR, WV[0]), (WG[0], WG[1]), (WV[0], WV[1])):
+        iota(A("W", lo, hi), [[0, hi - lo]], 0, 0, False)
+    iota(NF(144), [[1, 144]], 0, 0)
+    ends = (WR,) + WV + WG
+    for lo, hi in zip(ends, ends[1:]):
         dma([(T["W"][0:128:4, lo:hi], T["kids"][:, lo:hi])], [A("W", lo, hi)], [], 128 * (hi - lo))
-    digests(16, SPLIT, SPLIT)
-    fill("D", 5456, DW, 0.0)
-    digests(SPLIT, P, 5464)
-    aff(G16, col(4), 1.0, -7.5)
-    aff(col(8), col(0), 0.25, 12.0 - 2304.0)
-    aff(col(7), G16, 0.75, col(8))
+    dma([(T["D"][:, 16:P], T["dg"][:, 16:P])], [A("D", 16, P)], [], 256 * (P - 16))
+    const(G16, col(4), 1.0, -7.5, "s")
+    const(col(8), col(0), 0.25, 12.0 - 2304.0, "s")
+    const(col(7), G16, 0.75, col(8), "s")
     ts(A("ZR", 0, 144), NF(144), col(7), None, ALU.is_equal)
     copy(A("G", 0, 4), A("K0", 0, 4))
-    mm(A("P0", 0, 1), [(R(q), A("G", q, q + 1)) for q in range(4)])
+    children(A("P0", 0, 1), "G", 0, 4)
     copy(A("OFF", 88, 89), A("P0", 0, 1))
     copy(A("OFF", 64, 68), A("K0", 0, 4))
-    copy(A("OC", 10, 14), NF(4))
+    copy(A("OC", 0, 4), NF(4))
+    first = len(ops)
     level(16, 16, 88, 84)
     level(32, 64, 84, 68)
-    level(96, 256, 68, 0)
-    move(A("MO", 1408, 1472), IND(A("D", 0, 16), A("OC", 10, 14)))
-    send(0, A("MI", 1408, 1472), A("MO", 1408, 1472))
-    act(A("MO", 1024, 1408), IND(DWIN, A("OFF", 64, 88)))
-    send(0, A("MI", 1024, 1408), A("MO", 1024, 1408))
-    quarter(0)
-    stored4(0)
-    stored4(1)
-    quarter(1)
-    aff(G4, col(1), 1.0, -1.5)
-    aff(A("N4", 0, 144), NF(144), 1.0, 766.5)
-    aff(A("N16", 0, 128), NF(128), 1.0, 3064.5)
-    aff(S, G16, -1.0, col(4))
-    aff(K4, G4, -1.0, col(1))
+    for h in range(2):
+        copy(A("G", 96 + 128 * h, 224 + 128 * h), IND(WWIN, A("OFF", 68 + 8 * h, 76 + 8 * h)))
+    for h, bank in enumerate(("P0", "P1")):
+        children(A(bank, 0, 32), "G", 96 + 128 * h, 128)
+    copy(A("OFF", 0, 32), A("P0", 0, 32))
+    move(A("MO", 1408, 1472), IND(A("D", 0, 16), A("OC", 0, 4)), "s")
+    move(A("MO", 1024, 1408), IND(DG, A("OFF", 64, 88)), "s")
+    memset(ONE(256), 1.0)
+    const(A("N16", 0, 128), NF(128), 1.0, 3064.5, "s")
+    ts(BM, A("N16", 0, 128), G16, None, ALU.is_equal)
+    iota(A("WP", 0, 64), [[0, 16], [2, 4]], 1, 0)
+    iota(A("WP", 128, 192), [[0, 4], [2, 4], [0, 4]], 1, 0)
+    iota(A("FLOOR", 0, 276), [[0, 4], [1, 69]], -1, 0)
+    pick(A("U", 128, 256), BM, [[-1, 128]], ALU.is_gt, 0.0, 1)
+    gate[0] = pick(A("U", 128, 256), A("U", 128, 256), [[-1, 128]], ALU.not_equal, -128.0, 1)
+    across(0, "MI", "MO", 1408, 1472)
+    gate[0] = None
+    across(0, "MI", "MO", 1024, 1408)
+    const(G4, col(1), 1.0, -1.5, "s")
+    const(S, G16, -1.0, col(4), "s")
+    const(K4, G4, -1.0, col(1), "s")
+    const(A("N4", 0, 144), NF(144), 1.0, 766.5, "s")
+    ts(ident(1), NF(128), col(0), None, ALU.is_equal)
     ts(A("Z", 0, 144), NF(144), 3057.0, G16, ALU.add, ALU.is_equal)
     ts(A("Z4", 0, 144), A("N4", 0, 144), 2292.0, G16, ALU.add, ALU.is_equal)
-    ts(BM, A("N16", 0, 128), G16, None, ALU.is_equal)
-    ts(ident(1), NF(128), col(0), None, ALU.is_equal)
-    add({"g": (lambda e: e.affine_select(T["U"][:, 0:128], BM[0], [[-1, 128]], ALU.is_gt, 0.0, 0, 1), 0.38)},
-        [A("U", 0, 128)], [BM])
-    fill("RS5", 0, 320, 0.0)
-    fill("RS5", 0, 320, 1.0, 5)
-    fill("RS68", 0, 272, 1.0)
-    fill("RS68", 0, 272, 0.0, 68)
-    fill("FB", 64, 68, 1.0)
-    fill("LV", 4096, 4352, 0.0)
-    if ALL1:
-        fill("LVP", 4096, 4352, 0.0)
-    aff(A("THR", 0, 4), NF(4), 16.0, S)
-    move(A("XF", 0, 64), NF(64))
-    move(A("IOT", 0, 80), NF(80))
-    aff(A("ZQ", 0, 144), A("Z4", 0, 144), 4.0)
-    fill("C15", 0, 256, MID)
-    for w in WK[1:] + (-1,):
-        aff(ident(w), ident(1), float(w))
+    const(A("XF", 0, 64), NF(64), 1.0, 129.0, "s")
+    const(A("IOT", 0, 80), NF(80), 4.0, 0.0, "s")
+    const(A("THR", 0, 4), NF(4), 16.0, S, "s")
+    const(col(10), S, 4.0, 0.0, "s")
     act(LAST, S, 1.0, -14.0, ACT.Relu)
-    aff(A("V", 0, 128), BM, LAST)
-    aff(A("NV", 0, 128), A("V", 0, 128), -1.0)
-    for name in ("L4P", "L4", "NE"):
-        fill(name, 1024, 1088, 0.0)
-    aff(col(10), S, 1.0, float(DUM))
-    aff(A("G4", 1024, 1088), NF(64), 16.0, col(10))
-    aff(idents(9, 21), idents(3, 7), 3.0)
-    aff(idents(25, 35), idents(5, 7), 5.0)
-    aff(ident(49), ident(7), 7.0)
-    quarter(2)
-    tt(A("NE", 1088, 1536), A("MO", 1024, 1472), A("MI", 1024, 1472), ALU.not_equal)
-    count3(1152)
-    count_up(2, 1408)
-    count_up(3, 1088)
-    count_up(4, 1472)
-    count_up(0, 1472)
-    for h in range(2):
-        tt(A("NE", 512 * h, 512 * h + 512), A("MO", 512 * h, 512 * h + 512), A("MI", 512 * h, 512 * h + 512), ALU.not_equal)
-        mm(A("P4", 384 + 32 * h, 416 + 32 * h), [(E(p), A("NE", 512 * h + p, 512 * h + 512, 16)) for p in range(16)])
-    quarter(3)
-    scan(A("F5", 0, 320), A("RS5", 0, 320), A("P3", 0, 320), ALU.max, ALU.min)
-    leaves(LEAVES[:EARLY])
-    tt(A("FB", 0, 64), A("P4", 384, 448), A("F5", 4, 320, 5), ALU.min)
-    candidates(0, A("FB", 0, 68))
-    leaves(LEAVES[EARLY:])
+    fill("FB", 64, 68, 1.0, "s")
+    fill("C15", 0, 256, MID, "s")
+    fill("LV", 4096, 4352, 0.0, "s")
     if ALL1:
-        move(A("A0", 0, 256), IND(LWIN, A("CL0", 0, 16)))
-        move(A("B0", 0, 256), IND(A("LVP", 0, 4352), A("CL0", 0, 16)))
-        settle(0)
-        for h in range(4):
-            level4(h)
-    else:
-        exchange(0)
-        for h in range(4):
-            level4(h)
-        settle(0)
-    send(1, A("PAP", 0, 64), PA[0])
-    ids(0)
-    send(1, A("IDP", 0, 4), A("IDS0", 0, 4))
-    for lo in (0, 512):
-        move(A("L4", lo, lo + 512), A("L4S", lo, lo + 512))
-    own4(0)
-    aff(idents(-3, -9), idents(3, 9), -1.0)
-    aff(idents(-15, -25), idents(15, 25), -1.0)
-    aff(idents(-35, -49), idents(35, 49), -1.0)
-    for h, bank in enumerate(("P2", "P1")):
-        mm(A(bank, 0, 512), [(ident(1), A("L4S", 512 * h, 512 * h + 512)), (ident(-1), A("L4P", 512 * h, 512 * h + 512))])
-        act(A("NE", 512 * h, 512 * h + 512), A(bank, 0, 512), func=ACT.Abs)
-    g2 = sum2("L4", 1, True, False)
-    g3 = mm(l3, [mid] + terms3("L4", 1), stop=False)
-    move(A("OTH", 0, 64), IND(A("L4P", 0, 1088), A("IDS0", 0, 4)))
-    move(A("OWN", 0, 64), IND(A("L4", 0, 1088), A("IDP", 0, 4)))
-    copy(IND(A("L4P", 0, 1088), A("IDP", 0, 4)), A("PAP", 0, 64))
-    sum2("L4P", -1, False, True, g2)
-    mm(l3, terms3("L4P", -1), False, True, g3)
-    tt(A("NEO", 0, 64), A("OTH", 0, 64), PA[0], ALU.not_equal)
-    copy(IND(A("NE", 0, 1088), A("IDS0", 0, 4)), A("NEO", 0, 64))
-    tt(A("NEP", 0, 64), A("OWN", 0, 64), A("PAP", 0, 64), ALU.not_equal)
-    copy(IND(A("NE", 0, 1088), A("IDP", 0, 4)), A("NEP", 0, 64))
-    mm(A("P3", 0, 320, 5), [(E(p), A("NE", p, 1024, 16)) for p in range(16)])
-    fill("RSZ", 0, 128, 1.0)
-    fill("RSZ", 0, 64, 0.0, 4)
-    fill("RSZ", 64, 128, 0.0, 16)
-    fill("F5", 320, 340, 1.0)
-    iota(A("WP", 0, 64), [[0, 16], [2, 4]], 1, 0, True)
-    iota(A("WP", 128, 192), [[0, 4], [2, 4], [0, 4]], 1, 0, True)
-    tt(A("WP", 64, 128), A("WP", 0, 64), A("WP", 128, 192), ALU.mult)
-    ts(A("OC", 0, 4), NF(4), 4.0, 19.0, ALU.mult, ALU.add)
-    ts(col(11), S, K4, 0.25, ALU.subtract, ALU.mult)
-    ts(A("OC", 4, 8), NF(4), 4.0, col(11), ALU.mult, ALU.add)
-    act(A("M3", 0, 256), l3)
-    low_sums()
-    rnd(A("MM", 64, 96), A("SCN", 3, 128, 4))
-    tt(A("N32", 0, 32), A("SCN", 3, 128, 4), A("MM", 64, 96), ALU.not_equal)
-    move(A("NE", 1088, 1216), IND(A("N32", 0, 32), A("OC", 0, 8)))
-    tt(A("NE", 1472, 1536), l2, A("MM", 0, 64), ALU.not_equal)
-    tt(A("NE", 1216, 1472), l3, A("M3", 0, 256), ALU.not_equal)
-    count_up(2, 1472)
-    count3(1216)
-    count_up(3, 1152)
-    count_up(4, 1088)
-    scan(A("F5", 0, 320), A("RS5", 0, 320), A("P3", 0, 320), ALU.max, ALU.min)
-    candidates(1, A("F5", 4, 340, 5))
-    for lo in (0, 128):
-        tt(IND(LWIN, A("CL0", lo // 16, lo // 16 + 8)), A("A0", lo, lo + 128), A("MD0", lo, lo + 128), ALU.add)
-    exchange(1)
-    ts(A("COL", 16, 20), NF(4), 4.0, S, ALU.mult, ALU.is_equal)
-    for q in range(4):
-        aff(A("SK", 128 * q, 128 * q + 128), BM, col(16 + q))
-    places(0)
-    for h, bank in enumerate(("P5", "P6")):
-        for k in range(4):
-            mm(A(bank, k, 512, 4), [(A("SK", 128 * k, 128 * k + 128), A("G", 96 + 128 * h, 224 + 128 * h))])
-        act(A("OP4", 512 * h, 512 * h + 512), A(bank, 0, 512))
-    settle(1)
-    ids(1)
-    put_leaves(0, 128)
-    for lo, hi in zip(puts, puts[1:]):
-        i = copy(IND(DWIN, A("OFF", lo // 16, hi // 16)), A("L4", lo, hi))
-        apart(0, i)
-        ops[i]["piece"] = lo
-    fill("CK", 0, 64, 0.5)
-    fill("CK", 64, 128, -32640.0)
-    g2 = mm(l2, [(ident(1), A("CK", 0, 64)), (ident(1), A("CK", 64, 128))], stop=False)
+        fill("LVP", 4096, 4352, 0.0, "s")
+    fill("L4", 1024, 1088, 0.0, "s")
+    gate[0] = first
+    for w in WK[1:] + (-1,):
+        const(ident(w), ident(1), float(w), 0.0, "v")
+    for name, n, step, c, at in (("RS5", 320, 5, 0.0, 1.0), ("RS69", 276, 69, 0.0, 16384.0), ("STEP", 276, 69, 1.0, -16384.0)):
+        memset(A(name, 0, n), c)
+        memset(A(name, 0, n, step), at)
+    const(A("FLOOR", 0, 276, 69), A("THR", 0, 4), 128.0, 127.0, "s")
+    tt(A("U", 0, 128), BM, A("U", 128, 256), ALU.subtract)
+    const(A("NB", 0, 128), BM, -128.0, 0.0, "s")
+    const(ident(16), ident(1), 16.0, 0.0, "s")
+    const(A("ZQ", 0, 144), A("Z4", 0, 144), col(10), 0.0, "v")
+    const(A("ZI", 0, 144), A("Z", 0, 144), S, 0.0, "v")
+    const(A("V", 0, 128), BM, LAST, 0.0, "v")
+    const(A("NV", 0, 128), A("V", 0, 128), -1.0, 0.0, "v")
+
+    def upper():
+        tt(A("NE", 1088, 1536), A("MO", 1024, 1472), A("MI", 1024, 1472), ALU.not_equal)
+        count3(1152)
+        count_up(2, 1408)
+        count_up(3, 1088)
+        count_up(4, 1472)
+        count_up(0, 1472)
+
+    def differ(lo, hi):
+        tt(A("NE", lo, hi), A("MO", lo, hi), A("MI", lo, hi), ALU.not_equal)
+        if hi == 1024:
+            mm(A("P4", 384, 448), [(E(p), A("NE", p, 1024, 16)) for p in range(16)])
+
+    def listed():
+        tt(A("FB", 0, 64), A("P4", 384, 448), A("F5", 4, 320, 5), ALU.min)
+        candidates(0, lambda lo, hi: A("FB", lo, hi))
+
+    def pair():
+        if ALL1:
+            move(A("A0", 0, 256), IND(LWIN, A("CL0", 0, 16)), "v")
+            move(A("B0", 0, 256), IND(A("LVP", 0, 4352), A("CL0", 0, 16)), "s")
+        else:
+            for lo, on in ((0, "s"), (128, "v")):
+                move(A("A0", lo, lo + 128), IND(LWIN, A("CL0", lo // 16, lo // 16 + 8)), on)
+            across(0, "B0", "A0", 0, 256)
+
+    step = dict(mo=stored4, mi=lambda lo, hi: across(0, "MI", "MO", lo, hi), g4=quarter,
+                lp=lambda h: copy(A("LP", 64 * h, 64 * h + 64), A(("P0", "P5", "P6", "P7")[h], 0, 64)),
+                lv=leaves, out=lambda lo, hi: across(0, "LVP", "LV", lo, hi), up=upper, ne=differ,
+                f5=lambda: scan(A("F5", 0, 320), A("RS5", 0, 320), A("P3", 0, 320), ALU.max, ALU.min),
+                o4=lambda: copy(A("OFF", 32, 64), A("P1", 0, 32)),
+                id=lambda: (ids(0), across(1, "IDP", "IDS0", 0, 4)), ls=listed, ab=pair, l4=level4, far=lambda lo, hi: across(1, "L4P", "L4", lo, hi))
+    for x in STEPS:
+        step[x[0]](*x[1:])
+        if x[0] == "ls":
+            found = len(ops) - 1
+    gate[0] = found
+    settle(0)
+    across(1, "PAP", "PA0", 0, 64)
+    mark["own0"] = own4(0)
+    for lo, hi, bank in ((0, 512, "P2"), (512, DFV, "P1")):
+        if lo < hi:
+            mm(A(bank, 0, hi - lo), [(ident(1), A("L4P", lo, hi)), (ident(-1), A("L4", lo, hi))])
+            act(A("DF", lo, hi), A(bank, 0, hi - lo))
+    if DFV < 1024:
+        tt(A("DF", DFV, 1024), A("L4P", DFV, 1024), A("L4", DFV, 1024), ALU.subtract)
+    act(A("OWN", 0, 64), IND(L4W, A("IDP", 0, 4)), -1.0)
+    const(idents(9, 21), idents(3, 7), 3.0)
+    const(idents(25, 35), idents(5, 7), 5.0)
+    const(ident(49), ident(7), 7.0)
     g3 = mm(l3, [mid], stop=False)
+    mark["patch"] = tt(IND(A("DF", 0, 1088), A("IDP", 0, 4)), A("PAP", 0, 64), A("OWN", 0, 64), ALU.add)
+    sum2("DF")
+    mm(l3, terms3("DF"), False, True, g3)
+    nonzero(A("NE", 0, 1024), A("DF", 0, 1024), "s")
+    tt(A("WP", 64, 128), A("WP", 0, 64), A("WP", 128, 192), ALU.mult)
+    fill("RSZ", 0, 128, 1.0, "vs")
+    memset(A("RSZ", 0, 64, 4), 0.0)
+    memset(A("RSZ", 64, 128, 16), 0.0)
+    ts(col(11), S, K4, 0.25, ALU.subtract, ALU.mult)
+    const(col(15), S, 1.0, float(DUM))
+    const(A("G4", 1024, 1088), NF(64), 16.0, col(15))
+    fill("F5", 320, 340, 1.0, "vs")
+    act(col(12), K4, 1.0, -2.0, ACT.Relu)
+    const(col(13), S, 1.0, float(DUM + 64))
+    ts(col(14), col(11), col(13), None, ALU.subtract)
+    const(A("SF", 1, 9), NF(8), 16.0, 15.0)
+    const(col(16), col(11), 4.0, 3.0)
+    const(A("SF", 9, 13), NF(4), 16.0, col(16))
+    const(A("SF", 0, 1), col(12), col(14), col(13))
+    copy(A("OFF", 89, 102), A("SF", 0, 13))
+    low_sums(lambda: rnd(A("MM", 0, 64), l2))
+    wide = IND(A("SCN", 0, 128), A("OFF", 94, 102))
+    rnd(A("MM", 64, 192), wide)
+    tt(A("NE", 1088, 1216), wide, A("MM", 64, 192), ALU.not_equal)
+    act(A("M3", 0, 256), l3, -1.0, 127.5)
+    tt(A("NE", 1472, 1536), l2, A("MM", 0, 64), ALU.not_equal)
+    for k in range(1, 4):
+        const(A("Z4", 144 * k, 144 * k + 144), A("Z4", 0, 144), float(WK[k]))
+    const(A("BM", 0, 128), BM, MID)
+    g3 = mm(A("P3", 0, 320), [(A("BM", 0, 128), A("RS5", 0, 320))], stop=False)
+    for t, terms in ((0, [(slid("Z4", 144 * (j % 4) + 12 - j // 4 * 4), A("DF", j, 1024, 16)) for j in range(16)]),
+                     (1, [(E(p), A("NE", p, 1024, 16)) for p in range(16)]),
+                     (0, [(slid("Z4", 12 - 4 * k), A("M3", k, 256, 4)) for k in range(4)]),
+                     (2, [(BM, A("NE", 1472, 1536))]), (3, [(BM, A("NE", 1152, 1216))]), (4, [(BM, A("NE", 1088, 1152))])):
+        g3 = mm(A("P3", t, 320, 5), terms, False, t == 4, g3)
+    scan(A("F5", 0, 320), A("RS5", 0, 320), A("P3", 0, 320), ALU.max, ALU.min)
+    candidates(1, lambda lo, hi: A("F5", 5 * lo + 4, 5 * hi, 5))
+    found = len(ops) - 1
+    for lo, on in ((0, "s"), (128, "v")):
+        move(A("A1", lo, lo + 128), IND(LWIN, A("CL1", lo // 16, lo // 16 + 8)), on)
+    across(1, "B1", "A1", 0, 256)
+    ids(1)
+    places(0)
     places(1)
+    settle(1)
+    children(A("P1", 0, 64), "G", 96, 256)
+    act(A("PL", 0, 64), A("P1", 0, 64))
+    tt(A("PL", 80, 144), A("P1", 0, 64), A("PL", 0, 64), ALU.subtract)
+    fill("PL", 64, 68, float(DUM), "vs")
+    const(A("PL", 144, 148), A("THR", 0, 4))
+    for y, lo in (("YH", 0), ("YL", 80)):
+        tt(A(y, 0, 64), IND(A("PL", lo, lo + 68), A("CI1", 0, 4)), A("LE", 0, 64), ALU.mult)
+    g3 = mm(l3, [mid], stop=False)
     g4 = mm(A("P2", 0, 256), [mid], stop=False)
     own4(1)
-    sum2("L4", 1, False, True, g2)
-    mm(l3, terms3("L4", 1), False, True, g3)
+    sum2("L4")
+    mm(l3, terms3("L4"), False, True, g3)
     act(A("T3", 0, 256), l3, bias=-127.5)
-    g4 = mm(A("P2", 0, 256), terms3("L4", 1), False, False, g4)
+    g4 = mm(A("P2", 0, 256), terms3("L4"), False, False, g4)
     mm(A("P2", 0, 256), [(ident(-1), A("T3", 0, 256))], start=False, after=g4)
     act(A("UF", 0, 256), A("P2", 0, 256))
-    fill("KA", 0, 16, 120.5)
-    fill("KA", 16, 32, 0.5)
-    fill("CADD", 0, 96, 127.5)
-    fill("CADD", 96, 160, 0.0)
-    ts(A("OC", 8, 9), S, 4.0, 3.0, ALU.mult, ALU.add)
-    ts(col(12), S, 3.0, 16.0, ALU.min, ALU.mult)
-    ts(A("OC", 9, 10), col(12), 79.0, None, ALU.add)
-    aff(col(13), S, 15.0, float(DUM + 2))
-    ts(col(14), S, 4.0, col(13), ALU.is_ge, ALU.mult)
-    ts(A("OFF", 89, 90), col(14), S, None, ALU.add)
-    put_leaves(1, 256)
-    low_sums()
-    tt(A("XG", 0, 32), IND(A("SCN", 0, 128), A("OC", 8, 10)), A("KA", 0, 32), ALU.add)
-    tt(A("UF", 256, 320), l2, A("MM", 0, 64), ALU.subtract)
-    rnd(A("MM", 64, 96), A("XG", 0, 32))
-    tt(A("UF", 320, 352), A("XG", 0, 32), A("MM", 64, 96), ALU.subtract)
-    aff(A("OP4", 1024, 1088), NF(64), 16.0, float(DUM))
-    aff(A("Z1", 0, 144), A("Z", 0, 144), LAST)
-    move(A("XO", 0, 64), IND(A("OP4", 0, 1088), A("IDS1", 0, 4)))
-    move(A("XH", 0, 64), A("XO", 0, 64))
-    tt(A("XL", 0, 64), A("XO", 0, 64), A("XH", 0, 64), ALU.subtract)
-    in_parts(A("P1", 0, 4), [(E(p, "Z1"), A(x, p, 64, 16)) for x in ("XH", "XL") for p in range(16)], 8)
+    mark["sums"] = len(ops)
+    low_sums(lambda: copy(A("IU", 0, 64), l2))
+    copy(A("IU", 64, 96), A("SCN", 3, 128, 4))
+    ts(A("IV", 0, 96), A("IU", 0, 96), 255, None, ALU.bitwise_and)
+    in_parts(A("P1", 0, 4), [(E(p), A(x, p, 64, 16)) for x in ("YH", "YL") for p in range(16)], 8)
     copy(A("OFF", 90, 94), A("P1", 0, 4))
-    apart(1, tt(IND(DWIN, A("OFF", 84, 94)), A("UF", 256, 416), A("CADD", 0, 160), ALU.add))
-    apart(1, copy(IND(DWIN, A("OFF", 68, 84)), A("UF", 0, 256)))
-    dma([(T["y"][:, 0:P], T["D"][:, 0:P])], [], [A("D", 0, P)], 256 * P)
+    low = copy(IND(DWIN, A("OFF", 84, 94)), A("IV", 0, 160))
+    copy(IND(DWIN, A("OFF", 68, 84)), A("UF", 0, 256))
+    dma([(T["y"][:, 0:P], T["D"][:, 0:P])], [], [DG], 256 * P)
+
+    def stream(name, size, call, **kw):
+        cut = puts.get(name, (0, size))
+        for lo, hi in zip(cut, cut[1:]):
+            ops[call(lo, hi)].update(stream=name, size=size, **kw)
+
+    def new(win, lst, m):
+        return lambda lo, hi: tt(IND(win, A(lst, lo // 16, hi // 16)), A("A%d" % m, lo, hi), A("MD%d" % m, lo, hi), ALU.add)
+
+    stream("lv", 256, new(LWIN, "CL0", 0), needs=mark["md0"], until=found, rest=((mark["patch"], 1),))
+    stream("d0", 256, new(DWIN, "CP0", 0), needs=mark["cp0"], until=mark["gt1"], rest=((mark["gt1"], 1),))
+    stream("l4", 1024, lambda lo, hi: copy(IND(DWIN, A("OFF", lo // 16, hi // 16)), A("L4", lo, hi)),
+           needs=mark["own0"], until=low, rest=((mark["patch"], REST), (mark["gt1"], 1)))
+    stream("d1", 256, new(DWIN, "CP1", 1), needs=mark["md1"], until=low, rest=((mark["sums"], 1),))
     return ops
 
 
@@ -530,12 +566,11 @@ def _meet(a, b):
 
 
 def _banks(x):
-    return set(a[0] for a in x["w"] + x["r"] if a[0][0] == "P" and a[0][1:].isdigit())
+    return set(a[0] for a in x["w"] + x["r"] if SCRATCH[a[0]][0] == "psum")
 
 
 def _clash(x, y, free=True):
-    apart = free and x.get("apart") is not None and x.get("apart") == y.get("apart")
-    return (any(_meet(a, b) for a in x["r"] + ([] if apart else x["w"]) for b in y["w"])
+    return (any(_meet(a, b) for a in x["r"] + x["w"] for b in y["w"])
             or any(_meet(a, b) for a in x["w"] for b in y["r"]))
 
 
@@ -565,25 +600,63 @@ def _arrange(ops):
     n = len(ops)
     busy, start, end, queue, lanes = {}, [0.0] * n, [0.0] * n, [None] * n, {}
     for i, x in enumerate(ops):
+        if "stream" in x:
+            queue[i] = "vector"
+            continue
         pre = [j for j in range(i) if _clash(x, ops[j]) or _banks(x) & _banks(ops[j]) or x.get("of") == j
                or _line(x, ops[j])]
         best = None
         for q, (_, t) in x["ways"].items():
-            at = max([0.0] + [start[j] + _after(x, ops[j], q, queue[j], end[j] - start[j]) for j in pre])
+            at = max([0.0 if x["since"] is None else start[x["since"]]]
+                     + [start[j] + _after(x, ops[j], q, queue[j], end[j] - start[j]) for j in pre])
             for a, b in busy.get(q, []):
                 if at + t + MARGIN <= a:
                     break
                 at = max(at, b)
-            if best is None or at + t - SPARE < best[0] + best[1]:
-                best = (at, t, q)
-        start[i], t, queue[i] = best
+            price = at + t + ((x.get("spare") or SPARE) if q == "vector" else 0.0)
+            if best is None or price < best[3]:
+                best = (at, t, q, price)
+        start[i], t, queue[i] = best[:3]
         end[i] = start[i] + t
         if queue[i] is not None:
             busy[queue[i]] = sorted(busy.get(queue[i], []) + [(start[i], end[i])])
         if "lane" in x:
             end[i] = max(start[i] + x["lag"], lanes.get(x["lane"], 0.0)) + x["size"]
             lanes[x["lane"]] = end[i]
-    return sorted(range(n), key=lambda i: (start[i], i)), queue
+    return start, end, queue
+
+
+def plan(core, T, topo):
+    ops = build(core, T, topo, {})
+    start, end, queue = _arrange(ops)
+    streams = [x for x in ops if "stream" in x]
+    line = sorted((i for i, x in enumerate(ops) if queue[i] == "vector" and "stream" not in x), key=lambda i: start[i])
+    left = {x["stream"]: x["size"] for x in streams}
+    share = {}
+    free = {}
+    for a, b in zip(line, line[1:]):
+        at = end[a]
+        for x in streams:
+            t = max(at, end[x["needs"]] + TURN, free.get(x["w"][0][0], 0.0))
+            n = min(left[x["stream"]], int((start[b] + OVER - t - 0.07) / (SCATTER * CYC * 32)) * 32)
+            if n >= LEAST and start[b] <= start[x["until"]]:
+                share[x["stream"], b] = n
+                left[x["stream"]] -= n
+                at = t + 0.07 + n * SCATTER * CYC
+                free[x["w"][0][0]] = at + TURN
+    for x in streams:
+        for b, part in x["rest"]:
+            n = min(left[x["stream"]], 32 * int(part * left[x["stream"]] / 32))
+            share[x["stream"], b] = share.get((x["stream"], b), 0) + n
+            left[x["stream"]] -= n
+    cuts, when = {}, []
+    for k, x in enumerate(streams):
+        cuts[x["stream"]] = [0]
+        for b in sorted((b for s, b in share if s == x["stream"] and share[s, b]), key=lambda b: start[b]):
+            cuts[x["stream"]].append(cuts[x["stream"]][-1] + share[x["stream"], b])
+            when.append(start[b] - 1e-3 + 1e-4 * k)
+    start = start[:len(ops) - len(streams)] + when
+    return cuts, sorted(range(len(start)), key=lambda i: (start[i], i)), queue[:len(ops) - len(streams)] + ["vector"] * len(when)
 
 
 _PLAN = {}
@@ -593,12 +666,7 @@ def rank_program(g, core, T, topo):
     if T.rank_of(core) is None:
         return
     if not _PLAN:
-        ops = build(core, T, topo, range(0, 1025, PUT))
-        order, queue = _arrange(ops)
-        line = [ops[i].get("piece") for i in order if queue[i] == "vector"]
-        _PLAN["puts"] = [b for a, b in zip([None] + line, line) if b is not None and a != b - PUT] + [1024]
-        _PLAN["puts"].sort()
-        _PLAN["order"], _PLAN["queue"] = _arrange(build(core, T, topo, _PLAN["puts"]))
+        _PLAN["puts"], _PLAN["order"], _PLAN["queue"] = plan(core, T, topo)
     ops = build(core, T, topo, _PLAN["puts"])
     for x, q in zip(ops, _PLAN["queue"]):
         x["q"], x["fn"] = q, x["ways"][q][0]

from concourse.mybir import AluOpType as ALU, ActivationFunctionType as ACT

P = 5460
DUM = 5504
DW = 6656
MEETS = (1, 6)
BIG = 3221225472.0
MID = 49152.0
WK = (1, 3, 5, 7)
SC = (1, 3, 5, 7, 9, 15, 21, 25, 35, 49, -1, 16)
WR = 2048
WV = (3456, 4416)
WG = (P,)
STEPS = (("mo", 0, 512, "s"), ("mi", 0, 512), ("g4", 0), ("o4",), ("mo", 512, 1024, "s"), ("mi", 512, 1024),
         ("g4", 1), ("g4", 2), ("lp", 0), ("g4", 3), ("lp", 1),
         ("lv", 0, 512, "s"), ("out", 0, 512), ("lv", 1024, 1280, "v"), ("lp", 2), ("lv", 512, 1024, "s"),
         ("lv", 1280, 1536, "v"), ("out", 512, 1536), ("lp", 3), ("lv", 1536, 1792, "v"), ("lv", 1792, 2560, "s"),
         ("out", 1536, 2560), ("up",), ("ne", 0, 512), ("ne", 512, 1024), ("f5",), ("lv", 2560, 3328, "s"),
         ("out", 2560, 3328), ("lv", 3328, 3840, "s"), ("lv", 3840, 4096, "v"), ("out", 3328, 4096), ("ls",),
         ("l4", 0, "s"), ("l4", 1, "s"), ("far", 0, 512), ("l4", 2, "s"), ("l4", 3, "s"), ("far", 512, 1024),
         ("ab",), ("id",))
ALL1 = True
if not ALL1:
    STEPS = STEPS[:11] + (
        ("lv", 0, 1024, "s"), ("lv", 1024, 1280, "v"), ("lp", 2), ("up",), ("lp", 3), ("lv", 1536, 2560, "s"),
        ("lv", 1280, 1536, "v"), ("ne", 0, 512), ("ne", 512, 1024), ("f5",), ("lv", 2560, 3712, "s"),
        ("lv", 3840, 4096, "v"), ("ls",), ("lv", 3712, 3840, "v"), ("ab",), ("l4", 0, "s"), ("l4", 1, "s"),
        ("far", 0, 512), ("l4", 2, "s"), ("l4", 3, "s"), ("far", 512, 1024), ("id",))
DFV = 512
OVER, LEAST, REST = 0.05, 64, 0.4
PUT = 128


def _sb(n, t):
    return ("sbuf", [128, n], t)


_BF = dict(D=DW, Z=144, Z4=576, BM=128, ZQ=144, ZI=144, B=128, U=256, V=128, NV=128, N4=144, N16=128, CB=16,
           IDM=128 * len(SC), MO=1472, MI=1472, ONE=320, IOT=80, CF=64, NE=1536, FB=80, OWN=64,
           LV=4352, LVP=4352, L4=1088, L4P=1024, DF=1088, T4=1024, T3=256, F5=352, RS5=320, RS69=276, STEP=276,
           NB=128, C15=256, LE4=276, S16=276, LE=64, A0=256, A1=256, B0=256, B1=256, GT=256, MD0=256, MD1=256, PA0=64,
           PAP=64, UF=416, YH=64, YL=64, PL=160, M3=256, N32=32, M4=64)
_F32 = dict(COL=24, NF=144, ZR=144, G=352, G4=1088, RSZ=128, FLOOR=276, WP=192, THR=8, XF=64, CW=72,
            X0=64, X1=64, MM=192, ZS=128, SCN=128, XG=32, SF=16)
_I32 = dict(W=P, K0=8, IU=160, IV=160)
_U16 = dict(OFF=104, LP=256, OC=4, CI0=4, CI1=4, IDS0=4, IDS1=4, IDP=4, CP0=16, CP1=16, CL0=16, CL1=16)
SCRATCH = {}
for _d, _t in ((_BF, "bfloat16"), (_F32, "float32"), (_I32, "int32"), (_U16, "uint16")):
    for _k in _d:
        SCRATCH[_k] = _sb(_d[_k], _t)
for _i in range(8):
    SCRATCH["P%d" % _i] = ("psum", [128, 512], "float32")
NPOOL = 90
NMSG = 24
SEMAPHORES = (["s%d" % i for i in range(NPOOL)] + ["d%d" % i for i in range(12)]
              + ["l%d" % i for i in range(NMSG)] + ["r%d" % i for i in range(NMSG)])
CYC, TCYC = 0.87e-3, 0.42e-3
WAKE, TURN = 0.16, 0.14
GATHER, SCATTER = 1.45, 3.0
SMALL, SSMALL = 0.035, 0.16
LOCAL, NEAR, FAR = 540e3, 240e3, 190e3
LAG, RLAG = 1.3, 1.45
MARGIN = 0.0
SPARE = 0.2
LATE = 2.0


def build(core, T, topo, puts=()):
    rank = T.rank_of(core)
    peer = [T.cores[rank ^ m] for m in MEETS]
    ops = []
    gate = [None]
    mark = {}

    def A(name, lo, hi, step=1):
        ap = T[name][:, lo:hi] if step == 1 else T[name][:, lo:hi:step]
        return (ap, [(name, lo, hi)], [], len(range(lo, hi, step)), "")

    def IND(win, off):
        return (win[0].indirect(off[0]), win[1], off[1], 16 * off[3], "ind")

    def col(j):
        return A("COL", j, j + 1)

    def add(ways, outs, ins, kind="c", on="", **kw):
        ways = {q: w for q, w in ways.items() if not on or q[0] in on}
        w = [r for o in outs for r in o[1]]
        rd = [r for o in ins for r in o[1]] + [r for o in list(outs) + list(ins) for r in o[2]]
        ops.append(dict(ways=ways, q=list(ways)[0], w=w, r=rd, kind=kind, since=gate[0], **kw))
        return len(ops) - 1

    def val(s):
        return s[0] if isinstance(s, tuple) else s

    def aps(*s):
        return [x for x in s if isinstance(x, tuple)]

    def psum(x):
        return SCRATCH[x[1][0][0]][0] == "psum"

    def vtime(o, ins, both=1.0):
        if o[4]:
            return 0.07 + o[3] * SCATTER * CYC
        if any(i[4] for i in ins):
            return 0.07 + o[3] * GATHER * CYC
        narrow = all(SCRATCH[x[1][0][0]][2] in ("bfloat16", "uint16") for x in [o] + ins)
        return SMALL + max(64, o[3] * both * (0.5 if narrow else 1)) * CYC

    def stime(o, i):
        return 0.09 + o[3] * GATHER * CYC if i[4] else SSMALL + max(64, o[3]) * CYC

    def copy(o, i):
        return add({"vector": (lambda e: e.tensor_copy(o[0], i[0]), vtime(o, [i]))}, [o], [i])

    def tt(o, a, b, op):
        both = 1.0 if psum(a) or psum(b) else 2.0
        return add({"vector": (lambda e: e.tensor_tensor(o[0], a[0], b[0], op), vtime(o, [a, b], both))}, [o], [a, b])

    def ts(o, a, s1, s2, op0, op1=None):
        if op1 is None:
            fn = lambda e: e.tensor_scalar(o[0], a[0], val(s1), None, op0)
        else:
            fn = lambda e: e.tensor_scalar(o[0], a[0], val(s1), val(s2), op0, op1)
        return add({"vector": (fn, vtime(o, [a]))}, [o], [a] + aps(s1, s2))

    def scan(o, d0, d1, op0, op1, first=0.0):
        return add({"vector": (lambda e: e.tensor_tensor_scan(o[0], d0[0], d1[0], first, op0, op1),
                               vtime(o, [d0, d1]))}, [o], [d0, d1])

    def act(o, i, scale=1.0, bias=0.0, func=ACT.Identity):
        return add({"scalar": (lambda e: e.activation(o[0], i[0], func, bias=val(bias), scale=val(scale)),
                               stime(o, i))}, [o], [i] + aps(scale, bias))

    def aff(o, i, scale=1.0, bias=0.0, on="", spare=None):
        return add({"vector": (lambda e: e.tensor_scalar(o[0], i[0], val(scale), val(bias), ALU.mult, ALU.add),
                               vtime(o, [i])),
                    "scalar": (lambda e: e.activation(o[0], i[0], ACT.Identity, bias=val(bias), scale=val(scale)),
                               stime(o, i))}, [o], [i] + aps(scale, bias), on=on, spare=spare)

    def const(o, i, scale=1.0, bias=0.0, on=""):
        return aff(o, i, scale, bias, on, LATE)

    def move(o, i, on=""):
        return add({"vector": (lambda e: e.tensor_copy(o[0], i[0]), vtime(o, [i])),
                    "scalar": (lambda e: e.activation(o[0], i[0], ACT.Identity), stime(o, i))}, [o], [i], on=on)

    def nonzero(o, i, on=""):
        return add({"vector": (lambda e: e.tensor_scalar(o[0], i[0], 0.0, None, ALU.not_equal), vtime(o, [i])),
                    "scalar": (lambda e: e.activation(o[0], i[0], ACT.Abs), stime(o, i))}, [o], [i], on=on)

    def memset(o, c):
        return add({"vector": (lambda e: e.memset(o[0], c), vtime(o, []))}, [o], [])

    def fill(name, lo, hi, c, on=""):
        o, i = A(name, lo, hi), A("ONE", 0, hi - lo)
        ways = {"vector": (lambda e: e.memset(o[0], c), vtime(o, [])),
                "scalar": (lambda e: e.activation(o[0], i[0], ACT.Identity, bias=c, scale=0.0), stime(o, i))}
        if c == int(c):
            ways["g"] = (lambda e: e.iota(o[0], [[0, o[3]]], int(c), 0, allow_small_or_imprecise_dtypes=True),
                         0.13 + 2 * o[3] * CYC)
        add(ways, [o], [i], on=on, spare=LATE)

    def iota(o, pat, base, cm, fl=True):
        if fl:
            fn = lambda e: e.iota(o[0], pat, base, cm, allow_small_or_imprecise_dtypes=True)
        else:
            fn = lambda e: e.iota(o[0], pat, base, cm)
        return add({"g": (fn, 0.13 + 2 * o[3] * CYC)}, [o], [])

    def pick(o, i, pat, op, other, cm=0):
        return add({"g": (lambda e: e.affine_select(o[0], i[0], pat, op, other, 0, cm), 0.17 + 2 * o[3] * CYC)}, [o], [i])

    def mm(o, terms, start=True, stop=True, after=None):
        def fn(e):
            last = None
            for n, (l, r) in enumerate(terms):
                last = e.matmul(o[0], l[0], r[0], start and n == 0, stop and n == len(terms) - 1)
            return last
        wide = 4 if SCRATCH[terms[0][0][1][0][0]][2] == "float32" else 1
        return add({"tensor": (fn, 0.02 + len(terms) * max(64, o[3]) * wide * TCYC)}, [o],
                   [x for t in terms for x in t], after=after)

    ndma = [0]

    def dma(pairs, outs, ins, size, q="sync"):
        ndma[0] += 1
        return add({q: (lambda e: [e.dma_start(o, i) for o, i in pairs], 0.05 * len(pairs))}, outs, ins, kind="dma",
                   sem="d%d" % (ndma[0] - 1), n=16 * len(pairs), lane="local" if size > 5000 else "small",
                   size=size / LOCAL, lag=LAG)

    nmsg = [0]

    def send(m, dst, src):
        k = nmsg[0]
        nmsg[0] += 1
        rid, pid = topo.addr(peer[m])[:2]
        mask = topo.mask(core, peer[m])
        n = len(topo.engines(core, peer[m]))
        far = topo.chip(core) != topo.chip(peer[m])
        s = add({"g": (lambda e: e.remote_dma(dst[0], src[0], T.sem["r%d" % k], T.sem["l%d" % k], pid, rid, mask), 0.4)},
                [], [src], kind="send", sem="l%d" % k, n=n, lane="far" if far else "near", lag=RLAG,
                size=(0.1 if far else 0.05) + 256 * src[3] / (FAR if far else NEAR))
        add({None: (None, 0.0)}, [dst], [], kind="arr", sem="r%d" % k, n=len(topo.engines(peer[m], core)), of=s)

    def ident(w):
        j = SC.index(w)
        return A("IDM", 128 * j, 128 * j + 128)

    def idents(w0, w1):
        return A("IDM", 128 * SC.index(w0), 128 * SC.index(w1) + 128)

    def slid(name, lo):
        return A(name, lo, lo + 128)

    def R(q):
        return slid("ZR", 12 - 4 * q)

    def E(p, name="Z"):
        return slid(name, 15 - p)

    def rnd(o, i):
        ts(o, i, BIG, BIG, ALU.add, ALU.subtract)

    def apart(m, i):
        ops[i]["apart"] = m

    def in_parts(o, terms, n):
        last = None
        for a in range(0, len(terms), n):
            last = mm(o, terms[a:a + n], a == 0, a + n >= len(terms), last)

    DG = A("D", 0, P)
    DWIN = A("D", 0, DW)
    WWIN = A("W", 0, P)
    LWIN = A("LV", 0, 4352)
    L4W = A("L4", 0, 1088)
    PA = (A("PA0", 0, 64), A("IV", 96, 160))
    BM = A("B", 0, 128)
    G16, G4 = A("CB", 0, 1), A("CB", 8, 9)
    S, K4, LAST = col(5), col(6), col(9)
    l2, l3 = A("P0", 0, 64), A("P7", 0, 256)
    mid = (ident(1), A("C15", 0, 256))

    def NF(n):
        return A("NF", 0, n)

    def ONE(n):
        return A("ONE", 0, n)

    def children(o, src, lo, n):
        return mm(o, [(R(q), A(src, lo + q, lo + n, 4)) for q in range(4)])

    def level(go, n, src, dst):
        copy(A("G", go, go + n), IND(WWIN, A("OFF", src, src + n // 16)))
        children(A("P0", 0, n // 4), "G", go, n)
        copy(A("OFF", dst, dst + n // 4), A("P0", 0, n // 4))

    def quarter(h):
        bank = A(("P0", "P5", "P6", "P7")[h], 0, 64)
        copy(A("G4", 256 * h, 256 * h + 256), IND(WWIN, A("OFF", 16 * h, 16 * h + 16)))
        children(bank, "G4", 256 * h, 256)

    def stored4(lo, hi, on):
        move(A("MO", lo, hi), IND(DG, A("OFF", lo // 16, hi // 16)), on)

    def leaves(lo, hi, on=""):
        move(A("LV", lo, hi), IND(DG, A("LP", lo // 16, hi // 16)), on)

    def across(m, dst, src, lo, hi):
        send(m, A(dst, lo, hi), A(src, lo, hi))

    def level4(h, on=""):
        s4, t4 = A(("P0", "P7", "P2", "P1")[h], 0, 256), A("T4", 256 * h, 256 * h + 256)
        grp = mm(s4, [mid], stop=False)
        mm(s4, [(ident(WK[k]), A("LV", 1024 * h + k, 1024 * h + 1024, 4)) for k in range(4)], False, True, grp)
        aff(t4, s4, 1.0, -127.5, on)
        tt(A("L4", 256 * h, 256 * h + 256), s4, t4, ALU.subtract)

    def count3(l3):
        mm(A("P3", 1, 320, 5), [(slid("Z4", 12 - 4 * k), A("NE", l3 + k, l3 + 256, 4)) for k in range(4)])

    def count_up(t, lo):
        mm(A("P3", t, 320, 5), [(BM, A("NE", lo, lo + 64))])

    def candidates(m, f):
        ci = A("CI%d" % m, 0, 4)
        grp = mm(A("P5", 0, 276), [(ident(1), A("STEP", 0, 276))], stop=False)
        for q in range(4):
            grp = mm(A("P5", 69 * q + 1, 69 * q + 69), [(A("NB", 0, 128), f(0, 68))], False, q == 3, grp)
        grp = mm(A("P4", 0, 68), [(A("U", 0, 128), f(0, 68))], stop=False)
        mm(A("P4", 1, 68), [(A("U", 128, 256), f(0, 67))], False, True, grp)
        scan(A("LE4", 0, 276), A("P5", 0, 276), A("FLOOR", 0, 276), ALU.add, ALU.max)
        scan(A("CW", 0, 68), ONE(68), A("P4", 0, 68), ALU.mult, ALU.add)
        scan(A("S16", 0, 276), A("RS69", 0, 276), A("LE4", 0, 276), ALU.max, ALU.min)
        copy(ci, A("S16", 68, 276, 69))
        tt(A("LE", 0, 64), IND(A("CW", 0, 68), ci), A("XF", 0, 64), ALU.is_equal)
        move(A("CF", 0, 64), IND(A("IOT", 0, 80), ci), "s")
        mm(A("P4", 256, 272), [(slid(z, 12 - 4 * k), A(x, k, 64, 4)) for z, x in (("Z4", "CF"), ("ZQ", "LE")) for k in range(4)])
        ts(A("CL%d" % m, 0, 16), A("P4", 256, 272), K4, None, ALU.add)

    def ids(m):
        in_parts(A("P4", 320, 324),
                 [(ident(16), A("S16", 68, 276, 69))] + [(E(p, "ZI"), A("LE", p, 64, 16)) for p in range(16)], 9)
        copy(A("IDS%d" % m, 0, 4), A("P4", 320, 324))

    def places(m):
        move(A("X%d" % m, 0, 64), IND(A("G4", 0, 1088), A("IDS%d" % m, 0, 4)), "s")
        children(A("P2", 0, 16), "X%d" % m, 0, 64)
        mark["cp%d" % m] = copy(A("CP%d" % m, 0, 16), A("P2", 0, 16))

    def settle(m):
        a, b, pa, md = "A%d" % m, A("B%d" % m, 0, 256), PA[m], "MD%d" % m
        own = (mm(A("P5", 0, 256), [(A("NV", 0, 128), A(a, 0, 256))], stop=False),
               mm(A("P3", 0, 256), [(ident(-1), A(a, 0, 256))], stop=False))
        sums = [(ident(1), A("C15", 0, 64))] + [(ident(WK[k]), A(a, k, 256, 4)) for k in range(4)]
        if m or not ALL1:
            g6 = mm(A("P6", 0, 64), sums, stop=False)
        mm(A("P5", 0, 256), [(A("V", 0, 128), b)], start=False, after=own[0])
        mm(A("P3", 0, 256), [(ident(1), b)], start=False, after=own[1])
        if not m and ALL1:
            g6 = mm(A("P6", 0, 64), sums, stop=False)
        mark["gt%d" % m] = len(ops)
        for lo in (0, 128):
            ts(A("GT", lo, lo + 128), A("P5", lo, lo + 128), 0.0, None, ALU.is_gt)
        for lo in (0, 128):
            mark["md%d" % m] = tt(A(md, lo, lo + 128), A("P3", lo, lo + 128), A("GT", lo, lo + 128), ALU.mult)
        mm(A("P6", 0, 64), [(ident(WK[k]), A(md, k, 256, 4)) for k in range(4)], start=False, after=g6)
        if m:
            copy(A("IU", 96, 160), A("P6", 0, 64))
            ts(pa, A("IU", 96, 160), 255, None, ALU.bitwise_and)
        else:
            ts(A("M4", 0, 64), A("P6", 0, 64), -127.5, None, ALU.add)
            tt(pa, A("P6", 0, 64), A("M4", 0, 64), ALU.subtract)

    def sum2(src, start=True, after=None):
        return mm(l2, [(ident(WK[j // 4] * WK[j % 4]), A(src, j, 1024, 16)) for j in range(16)], start, True, after)

    def terms3(src):
        return [(ident(WK[k]), A(src, k, 1024, 4)) for k in range(4)]

    def low_sums(between):
        tt(A("ZS", 0, 64), l2, A("WP", 0, 64), ALU.mult)
        tt(A("ZS", 64, 128), l2, A("WP", 64, 128), ALU.mult)
        between()
        scan(A("SCN", 0, 128), A("RSZ", 0, 128), A("ZS", 0, 128), ALU.mult, ALU.add)

    def own4(m):
        return copy(IND(L4W, A("IDS%d" % m, 0, 4)), PA[m])

    dma([(T["K0"][q:128:4, 0:4], T["kids"][:, 0:4]) for q in range(4)], [A("K0", 0, 4)], [], 2048, "scalar")
    dma([(T["D"][:, 0:16], T["dg"][:, 0:16])], [A("D", 0, 16)], [], 4096, "scalar")
    dma([(T["W"][q:128:4, 0:WR], T["kids"][:, 0:WR]) for q in range(4)], [A("W", 0, WR)], [], 512 * WR)
    iota(A("COL", 0, 5), [[768, 5]], 0, 1)
    for lo, hi in zip((WR,) + WV, WV):
        memset(A("W", lo, hi), 0)
    for lo, hi in zip(WV[-1:] + WG, WG):
        iota(A("W", lo, hi), [[0, hi - lo]], 0, 0, False)
    iota(NF(144), [[1, 144]], 0, 0)
    ends = (WR,) + WV + WG
    for lo, hi in zip(ends, ends[1:]):
        dma([(T["W"][0:128:4, lo:hi], T["kids"][:, lo:hi])], [A("W", lo, hi)], [], 128 * (hi - lo))
    dma([(T["D"][:, 16:P], T["dg"][:, 16:P])], [A("D", 16, P)], [], 256 * (P - 16))
    const(G16, col(4), 1.0, -7.5, "s")
    const(col(8), col(0), 0.25, 12.0 - 2304.0, "s")
    const(col(7), G16, 0.75, col(8), "s")
    ts(A("ZR", 0, 144), NF(144), col(7), None, ALU.is_equal)
    copy(A("G", 0, 4), A("K0", 0, 4))
    children(A("P0", 0, 1), "G", 0, 4)
    copy(A("OFF", 88, 89), A("P0", 0, 1))
    copy(A("OFF", 64, 68), A("K0", 0, 4))
    copy(A("OC", 0, 4), NF(4))
    first = len(ops)
    level(16, 16, 88, 84)
    level(32, 64, 84, 68)
    for h in range(2):
        copy(A("G", 96 + 128 * h, 224 + 128 * h), IND(WWIN, A("OFF", 68 + 8 * h, 76 + 8 * h)))
    for h, bank in enumerate(("P0", "P1")):
        children(A(bank, 0, 32), "G", 96 + 128 * h, 128)
    copy(A("OFF", 0, 32), A("P0", 0, 32))
    move(A("MO", 1408, 1472), IND(A("D", 0, 16), A("OC", 0, 4)), "s")
    move(A("MO", 1024, 1408), IND(DG, A("OFF", 64, 88)), "s")
    memset(ONE(256), 1.0)
    const(A("N16", 0, 128), NF(128), 1.0, 3064.5, "s")
    ts(BM, A("N16", 0, 128), G16, None, ALU.is_equal)
    iota(A("WP", 0, 64), [[0, 16], [2, 4]], 1, 0)
    iota(A("WP", 128, 192), [[0, 4], [2, 4], [0, 4]], 1, 0)
    iota(A("FLOOR", 0, 276), [[0, 4], [1, 69]], -1, 0)
    pick(A("U", 128, 256), BM, [[-1, 128]], ALU.is_gt, 0.0, 1)
    gate[0] = pick(A("U", 128, 256), A("U", 128, 256), [[-1, 128]], ALU.not_equal, -128.0, 1)
    across(0, "MI", "MO", 1408, 1472)
    gate[0] = None
    across(0, "MI", "MO", 1024, 1408)
    const(G4, col(1), 1.0, -1.5, "s")
    const(S, G16, -1.0, col(4), "s")
    const(K4, G4, -1.0, col(1), "s")
    const(A("N4", 0, 144), NF(144), 1.0, 766.5, "s")
    ts(ident(1), NF(128), col(0), None, ALU.is_equal)
    ts(A("Z", 0, 144), NF(144), 3057.0, G16, ALU.add, ALU.is_equal)
    ts(A("Z4", 0, 144), A("N4", 0, 144), 2292.0, G16, ALU.add, ALU.is_equal)
    const(A("XF", 0, 64), NF(64), 1.0, 129.0, "s")
    const(A("IOT", 0, 80), NF(80), 4.0, 0.0, "s")
    const(A("THR", 0, 4), NF(4), 16.0, S, "s")
    const(col(10), S, 4.0, 0.0, "s")
    act(LAST, S, 1.0, -14.0, ACT.Relu)
    fill("FB", 64, 68, 1.0, "s")
    fill("C15", 0, 256, MID, "s")
    fill("LV", 4096, 4352, 0.0, "s")
    if ALL1:
        fill("LVP", 4096, 4352, 0.0, "s")
    fill("L4", 1024, 1088, 0.0, "s")
    gate[0] = first
    for w in WK[1:] + (-1,):
        const(ident(w), ident(1), float(w), 0.0, "v")
    for name, n, step, c, at in (("RS5", 320, 5, 0.0, 1.0), ("RS69", 276, 69, 0.0, 16384.0), ("STEP", 276, 69, 1.0, -16384.0)):
        memset(A(name, 0, n), c)
        memset(A(name, 0, n, step), at)
    const(A("FLOOR", 0, 276, 69), A("THR", 0, 4), 128.0, 127.0, "s")
    tt(A("U", 0, 128), BM, A("U", 128, 256), ALU.subtract)
    const(A("NB", 0, 128), BM, -128.0, 0.0, "s")
    const(ident(16), ident(1), 16.0, 0.0, "s")
    const(A("ZQ", 0, 144), A("Z4", 0, 144), col(10), 0.0, "v")
    const(A("ZI", 0, 144), A("Z", 0, 144), S, 0.0, "v")
    const(A("V", 0, 128), BM, LAST, 0.0, "v")
    const(A("NV", 0, 128), A("V", 0, 128), -1.0, 0.0, "v")

    def upper():
        tt(A("NE", 1088, 1536), A("MO", 1024, 1472), A("MI", 1024, 1472), ALU.not_equal)
        count3(1152)
        count_up(2, 1408)
        count_up(3, 1088)
        count_up(4, 1472)
        count_up(0, 1472)

    def differ(lo, hi):
        tt(A("NE", lo, hi), A("MO", lo, hi), A("MI", lo, hi), ALU.not_equal)
        if hi == 1024:
            mm(A("P4", 384, 448), [(E(p), A("NE", p, 1024, 16)) for p in range(16)])

    def listed():
        tt(A("FB", 0, 64), A("P4", 384, 448), A("F5", 4, 320, 5), ALU.min)
        candidates(0, lambda lo, hi: A("FB", lo, hi))

    def pair():
        if ALL1:
            move(A("A0", 0, 256), IND(LWIN, A("CL0", 0, 16)), "v")
            move(A("B0", 0, 256), IND(A("LVP", 0, 4352), A("CL0", 0, 16)), "s")
        else:
            for lo, on in ((0, "s"), (128, "v")):
                move(A("A0", lo, lo + 128), IND(LWIN, A("CL0", lo // 16, lo // 16 + 8)), on)
            across(0, "B0", "A0", 0, 256)

    step = dict(mo=stored4, mi=lambda lo, hi: across(0, "MI", "MO", lo, hi), g4=quarter,
                lp=lambda h: copy(A("LP", 64 * h, 64 * h + 64), A(("P0", "P5", "P6", "P7")[h], 0, 64)),
                lv=leaves, out=lambda lo, hi: across(0, "LVP", "LV", lo, hi), up=upper, ne=differ,
                f5=lambda: scan(A("F5", 0, 320), A("RS5", 0, 320), A("P3", 0, 320), ALU.max, ALU.min),
                o4=lambda: copy(A("OFF", 32, 64), A("P1", 0, 32)),
                id=lambda: (ids(0), across(1, "IDP", "IDS0", 0, 4)), ls=listed, ab=pair, l4=level4, far=lambda lo, hi: across(1, "L4P", "L4", lo, hi))
    for x in STEPS:
        step[x[0]](*x[1:])
        if x[0] == "ls":
            found = len(ops) - 1
    gate[0] = found
    settle(0)
    across(1, "PAP", "PA0", 0, 64)
    mark["own0"] = own4(0)
    for lo, hi, bank in ((0, 512, "P2"), (512, DFV, "P1")):
        if lo < hi:
            mm(A(bank, 0, hi - lo), [(ident(1), A("L4P", lo, hi)), (ident(-1), A("L4", lo, hi))])
            act(A("DF", lo, hi), A(bank, 0, hi - lo))
    if DFV < 1024:
        tt(A("DF", DFV, 1024), A("L4P", DFV, 1024), A("L4", DFV, 1024), ALU.subtract)
    act(A("OWN", 0, 64), IND(L4W, A("IDP", 0, 4)), -1.0)
    const(idents(9, 21), idents(3, 7), 3.0)
    const(idents(25, 35), idents(5, 7), 5.0)
    const(ident(49), ident(7), 7.0)
    g3 = mm(l3, [mid], stop=False)
    mark["patch"] = tt(IND(A("DF", 0, 1088), A("IDP", 0, 4)), A("PAP", 0, 64), A("OWN", 0, 64), ALU.add)
    sum2("DF")
    mm(l3, terms3("DF"), False, True, g3)
    nonzero(A("NE", 0, 1024), A("DF", 0, 1024), "s")
    tt(A("WP", 64, 128), A("WP", 0, 64), A("WP", 128, 192), ALU.mult)
    fill("RSZ", 0, 128, 1.0, "vs")
    memset(A("RSZ", 0, 64, 4), 0.0)
    memset(A("RSZ", 64, 128, 16), 0.0)
    ts(col(11), S, K4, 0.25, ALU.subtract, ALU.mult)
    const(col(15), S, 1.0, float(DUM))
    const(A("G4", 1024, 1088), NF(64), 16.0, col(15))
    fill("F5", 320, 340, 1.0, "vs")
    act(col(12), K4, 1.0, -2.0, ACT.Relu)
    const(col(13), S, 1.0, float(DUM + 64))
    ts(col(14), col(11), col(13), None, ALU.subtract)
    const(A("SF", 1, 9), NF(8), 16.0, 15.0)
    const(col(16), col(11), 4.0, 3.0)
    const(A("SF", 9, 13), NF(4), 16.0, col(16))
    const(A("SF", 0, 1), col(12), col(14), col(13))
    copy(A("OFF", 89, 102), A("SF", 0, 13))
    low_sums(lambda: rnd(A("MM", 0, 64), l2))
    wide = IND(A("SCN", 0, 128), A("OFF", 94, 102))
    rnd(A("MM", 64, 192), wide)
    tt(A("NE", 1088, 1216), wide, A("MM", 64, 192), ALU.not_equal)
    act(A("M3", 0, 256), l3, -1.0, 127.5)
    tt(A("NE", 1472, 1536), l2, A("MM", 0, 64), ALU.not_equal)
    for k in range(1, 4):
        const(A("Z4", 144 * k, 144 * k + 144), A("Z4", 0, 144), float(WK[k]))
    const(A("BM", 0, 128), BM, MID)
    g3 = mm(A("P3", 0, 320), [(A("BM", 0, 128), A("RS5", 0, 320))], stop=False)
    for t, terms in ((0, [(slid("Z4", 144 * (j % 4) + 12 - j // 4 * 4), A("DF", j, 1024, 16)) for j in range(16)]),
                     (1, [(E(p), A("NE", p, 1024, 16)) for p in range(16)]),
                     (0, [(slid("Z4", 12 - 4 * k), A("M3", k, 256, 4)) for k in range(4)]),
                     (2, [(BM, A("NE", 1472, 1536))]), (3, [(BM, A("NE", 1152, 1216))]), (4, [(BM, A("NE", 1088, 1152))])):
        g3 = mm(A("P3", t, 320, 5), terms, False, t == 4, g3)
    scan(A("F5", 0, 320), A("RS5", 0, 320), A("P3", 0, 320), ALU.max, ALU.min)
    candidates(1, lambda lo, hi: A("F5", 5 * lo + 4, 5 * hi, 5))
    found = len(ops) - 1
    for lo, on in ((0, "s"), (128, "v")):
        move(A("A1", lo, lo + 128), IND(LWIN, A("CL1", lo // 16, lo // 16 + 8)), on)
    across(1, "B1", "A1", 0, 256)
    ids(1)
    places(0)
    places(1)
    settle(1)
    children(A("P1", 0, 64), "G", 96, 256)
    act(A("PL", 0, 64), A("P1", 0, 64))
    tt(A("PL", 80, 144), A("P1", 0, 64), A("PL", 0, 64), ALU.subtract)
    fill("PL", 64, 68, float(DUM), "vs")
    const(A("PL", 144, 148), A("THR", 0, 4))
    for y, lo in (("YH", 0), ("YL", 80)):
        tt(A(y, 0, 64), IND(A("PL", lo, lo + 68), A("CI1", 0, 4)), A("LE", 0, 64), ALU.mult)
    g3 = mm(l3, [mid], stop=False)
    g4 = mm(A("P2", 0, 256), [mid], stop=False)
    own4(1)
    sum2("L4")
    mm(l3, terms3("L4"), False, True, g3)
    act(A("T3", 0, 256), l3, bias=-127.5)
    g4 = mm(A("P2", 0, 256), terms3("L4"), False, False, g4)
    mm(A("P2", 0, 256), [(ident(-1), A("T3", 0, 256))], start=False, after=g4)
    act(A("UF", 0, 256), A("P2", 0, 256))
    mark["sums"] = len(ops)
    low_sums(lambda: copy(A("IU", 0, 64), l2))
    copy(A("IU", 64, 96), A("SCN", 3, 128, 4))
    ts(A("IV", 0, 96), A("IU", 0, 96), 255, None, ALU.bitwise_and)
    in_parts(A("P1", 0, 4), [(E(p), A(x, p, 64, 16)) for x in ("YH", "YL") for p in range(16)], 8)
    copy(A("OFF", 90, 94), A("P1", 0, 4))
    low = copy(IND(DWIN, A("OFF", 84, 94)), A("IV", 0, 160))
    copy(IND(DWIN, A("OFF", 68, 84)), A("UF", 0, 256))
    dma([(T["y"][:, 0:P], T["D"][:, 0:P])], [], [DG], 256 * P)

    def stream(name, size, call, **kw):
        cut = puts.get(name, (0, size))
        for lo, hi in zip(cut, cut[1:]):
            ops[call(lo, hi)].update(stream=name, size=size, **kw)

    def new(win, lst, m):
        return lambda lo, hi: tt(IND(win, A(lst, lo // 16, hi // 16)), A("A%d" % m, lo, hi), A("MD%d" % m, lo, hi), ALU.add)

    stream("lv", 256, new(LWIN, "CL0", 0), needs=mark["md0"], until=found, rest=((mark["patch"], 1),))
    stream("d0", 256, new(DWIN, "CP0", 0), needs=mark["cp0"], until=mark["gt1"], rest=((mark["gt1"], 1),))
    stream("l4", 1024, lambda lo, hi: copy(IND(DWIN, A("OFF", lo // 16, hi // 16)), A("L4", lo, hi)),
           needs=mark["own0"], until=low, rest=((mark["patch"], REST), (mark["gt1"], 1)))
    stream("d1", 256, new(DWIN, "CP1", 1), needs=mark["md1"], until=low, rest=((mark["sums"], 1),))
    return ops


def _meet(a, b):
    return a[0] == b[0] and a[1] < b[2] and b[1] < a[2]


def _banks(x):
    return set(a[0] for a in x["w"] + x["r"] if SCRATCH[a[0]][0] == "psum")


def _clash(x, y, free=True):
    return (any(_meet(a, b) for a in x["r"] + x["w"] for b in y["w"])
            or any(_meet(a, b) for a in x["w"] for b in y["r"]))


def _line(x, y):
    return x["kind"] == y["kind"] == "dma" and list(x["ways"]) == list(y["ways"])


def _depends(x, y):
    if x["q"] != y["q"] and _banks(x) & _banks(y):
        return True
    if x["q"] == "tensor" and y["q"] == "tensor":
        return False
    return _clash(x, y, False)


def _after(x, y, qx, qy, took):
    if _line(x, y):
        return 0.05
    if x["kind"] == "arr":
        return took
    if qx != qy or y["kind"] != "c":
        return took + WAKE
    return took + (TURN if qx != "tensor" and _clash(x, y) else 0.0)


def _arrange(ops):
    n = len(ops)
    busy, start, end, queue, lanes = {}, [0.0] * n, [0.0] * n, [None] * n, {}
    for i, x in enumerate(ops):
        if "stream" in x:
            queue[i] = "vector"
            continue
        pre = [j for j in range(i) if _clash(x, ops[j]) or _banks(x) & _banks(ops[j]) or x.get("of") == j
               or _line(x, ops[j])]
        best = None
        for q, (_, t) in x["ways"].items():
            at = max([0.0 if x["since"] is None else start[x["since"]]]
                     + [start[j] + _after(x, ops[j], q, queue[j], end[j] - start[j]) for j in pre])
            for a, b in busy.get(q, []):
                if at + t + MARGIN <= a:
                    break
                at = max(at, b)
            price = at + t + ((x.get("spare") or SPARE) if q == "vector" else 0.0)
            if best is None or price < best[3]:
                best = (at, t, q, price)
        start[i], t, queue[i] = best[:3]
        end[i] = start[i] + t
        if queue[i] is not None:
            busy[queue[i]] = sorted(busy.get(queue[i], []) + [(start[i], end[i])])
        if "lane" in x:
            end[i] = max(start[i] + x["lag"], lanes.get(x["lane"], 0.0)) + x["size"]
            lanes[x["lane"]] = end[i]
    return start, end, queue


def plan(core, T, topo):
    ops = build(core, T, topo, {})
    start, end, queue = _arrange(ops)
    streams = [x for x in ops if "stream" in x]
    line = sorted((i for i, x in enumerate(ops) if queue[i] == "vector" and "stream" not in x), key=lambda i: start[i])
    left = {x["stream"]: x["size"] for x in streams}
    share = {}
    free = {}
    for a, b in zip(line, line[1:]):
        at = end[a]
        for x in streams:
            t = max(at, end[x["needs"]] + TURN, free.get(x["w"][0][0], 0.0))
            n = min(left[x["stream"]], int((start[b] + OVER - t - 0.07) / (SCATTER * CYC * 32)) * 32)
            if n >= LEAST and start[b] <= start[x["until"]]:
                share[x["stream"], b] = n
                left[x["stream"]] -= n
                at = t + 0.07 + n * SCATTER * CYC
                free[x["w"][0][0]] = at + TURN
    for x in streams:
        for b, part in x["rest"]:
            n = min(left[x["stream"]], 32 * int(part * left[x["stream"]] / 32))
            share[x["stream"], b] = share.get((x["stream"], b), 0) + n
            left[x["stream"]] -= n
    cuts, when = {}, []
    for k, x in enumerate(streams):
        cuts[x["stream"]] = [0]
        for b in sorted((b for s, b in share if s == x["stream"] and share[s, b]), key=lambda b: start[b]):
            cuts[x["stream"]].append(cuts[x["stream"]][-1] + share[x["stream"], b])
            when.append(start[b] - 1e-3 + 1e-4 * k)
    start = start[:len(ops) - len(streams)] + when
    return cuts, sorted(range(len(start)), key=lambda i: (start[i], i)), queue[:len(ops) - len(streams)] + ["vector"] * len(when)


_PLAN = {}


def rank_program(g, core, T, topo):
    if T.rank_of(core) is None:
        return
    if not _PLAN:
        _PLAN["puts"], _PLAN["order"], _PLAN["queue"] = plan(core, T, topo)
    ops = build(core, T, topo, _PLAN["puts"])
    for x, q in zip(ops, _PLAN["queue"]):
        x["q"], x["fn"] = q, x["ways"][q][0]
    where = {j: i for i, j in enumerate(_PLAN["order"])}
    ops = [ops[j] for j in _PLAN["order"]]
    eng = {"g": g, "vector": g.vector, "scalar": g.scalar, "tensor": g.tensor, "sync": g.sync}
    if "waits" not in _PLAN:
        known = {q: set() for q in eng}
        before = []
        waits = []
        for i, x in enumerate(ops):
            if x["kind"] == "arr":
                before.append(set())
                waits.append([])
                continue
            k = known[x["q"]]
            need = [j for j in range(i) if j not in k and _depends(x, ops[j])]
            implied = set()
            for j in need:
                implied |= before[j]
                if ops[j].get("after") is not None:
                    implied.add(where[ops[j]["after"]])
            need = [j for j in need if j not in implied]
            k |= implied | set(need)
            waits.append(need)
            before.append(set(k))
        _PLAN["waits"], _PLAN["before"] = waits, before
    waits, before = _PLAN["waits"], _PLAN["before"]
    waited = set(j for w in waits for j in w)
    tail = [i for i, x in enumerate(ops) if x["kind"] != "c" and i not in waited]
    waiters = {}
    for i, w in enumerate(waits):
        for j in w:
            waiters.setdefault(j, []).append(i)
    groups = []
    for j in sorted(waiters):
        if ops[j]["kind"] != "c":
            continue
        for grp in groups:
            if (waiters[grp[0]][0] == waiters[j][0] and all(j in before[y] for i in grp for y in waiters[i])
                    and all(i in before[y] for i in grp for y in waiters[j])):
                grp.append(j)
                break
        else:
            groups.append([j])
    pool = [[[], 0] for _ in range(NPOOL)]
    for grp in groups:
        s = [n for n in range(NPOOL) if all(j in before[i] for j in pool[n][0] for i in grp)][0]
        pool[s] = [grp, pool[s][1] + len(grp)]
        for i in grp:
            ops[i]["sem"], ops[i]["n"] = "s%d" % s, pool[s][1]
    done = {q: set() for q in eng}
    for i, x in enumerate(ops):
        if x["kind"] == "arr":
            continue
        e = eng[x["q"]]
        for s, n in sorted(set((ops[j]["sem"], ops[j]["n"]) for j in waits[i]) - done[x["q"]]):
            e.wait_ge(T.sem[s], n)
            done[x["q"]].add((s, n))
        r = x["fn"](e)
        if x["kind"] == "dma":
            for one in r:
                one.then_inc(T.sem[x["sem"]], 16)
        elif x["kind"] == "c" and i in waited:
            r.then_inc(T.sem[x["sem"]], 1)
    for i in tail:
        eng[ops[i]["q"] or "g"].wait_ge(T.sem[ops[i]["sem"]], ops[i]["n"])
